import numpy as np, ml_dtypes
CORES = [113,118,241,246]
N = 4
BF = ml_dtypes.bfloat16
def gentries(a):
    return np.ascontiguousarray(a.reshape(8, 16, -1).transpose(0, 2, 1)).reshape(8, -1)
def gtable(e):
    e = np.asarray(e); return np.ascontiguousarray(e.reshape(8, -1, 16).transpose(0, 2, 1)).reshape(128, -1).astype(np.int32)
V, E, RO, TH = 2304, 1024, 2, 6
S, M, F = 16 * N, RO * E, RO * E // N
U = np.arange(V)
ROOM = min(V // 2 - E, V // 20)
def graph(rng, full=()):
    A = np.full((8, 16, V), V, np.int64); place = np.argsort(rng.random((8, V)), axis=1)
    near = rng.random((8, 16)) < 0.7; near[np.arange(RO), np.arange(RO)] = True
    for g in full: near[g] = True
    for g in range(8):
        mk = np.argsort(rng.random((V // 32, 31)), axis=1)[:, :16] + 1
        for i in range(16):
            if near[g, i]:
                A[g, i, place[g]] = place[g][U ^ mk[U // 32, i]]
            else:
                o = rng.permutation(V); A[g, i, o[0::2]] = o[1::2]; A[g, i, o[1::2]] = o[0::2]
    return A, place
def thin(rng, A, most):
    for g in range(8):
        for i in range(16):
            p = A[g, i]; lo = np.nonzero((p < V) & (U < p) & (U > 0) & (p != V - 1))[0]
            d = rng.permutation(lo)[:int(rng.integers(0, most[i] + 1))]; e = p[d]
            A[g, i, d] = V; A[g, i, e] = V
    return A
def tests(rng, A, first, again):
    tv = np.zeros((8, RO, E), np.int64)
    for g in range(8):
        seen = np.zeros(V)
        for t in range(RO):
            p = A[g, t]; lo = np.nonzero((p < V) & (U < p))[0]
            key = rng.random(len(lo)) - first[g, lo] - first[g, p[lo]] - again * (seen[lo] + seen[p[lo]])
            lo = rng.permutation(lo[np.argsort(key)[:E]])
            tv[g, t] = np.where(rng.random(E) < 0.5, p[lo], lo)
            seen = np.zeros(V); seen[lo] = 1; seen[p[lo]] = 1
    return tv
def cloud(rng, place, lams):
    c = V // 32; n = lambda *s: rng.standard_normal(s, dtype=np.float32)
    lam = rng.choice(np.array(lams, np.float32), (8, 1, c, 1)); ld = (rng.random((8, 1, c, 32)) * 2 - 1).astype(np.float32)
    w = 128 + 25 * n(8, S, c, 1) + 60 * lam * ld * n(8, S, c, 1) + 20 * n(8, S, c, 32)
    w = np.clip(np.rint(w), 0, 255).astype(np.int64).reshape(8, S, V)
    step = rng.choice(np.array([1, 1, 1, 16, 64]), (8, 1, V)); w = w // step * step
    return np.take_along_axis(w, np.argsort(place, axis=1)[:, None, :], 2)
def pack(s, A, tv):
    return {"x": np.ascontiguousarray(s.reshape(8, N, 16, V).transpose(1, 0, 2, 3)).reshape(N, 128, V).astype(np.float32).astype(BF),
            "adj": np.stack([A.reshape(128, V).astype(np.int32)] * N), "tv": np.stack([gtable(tv.reshape(8, M))] * N)}
def setup_inputs(rng):
    A, place = graph(rng); A = thin(rng, A, [ROOM] * 16)
    return pack(cloud(rng, place, [0, 0, 0.3, 1]), A, tests(rng, A, np.zeros((8, V)), 0))
def setup_inputs_edge(rng):
    A, place = graph(rng); A = thin(rng, A, [ROOM] * 16)
    ty = rng.random((8, 1, V)); low = ty < 0.2; high = (ty >= 0.2) & (ty < 0.4)
    lv = np.where(low, rng.integers(40, 110, (8, 1, V)), rng.integers(190, 240, (8, 1, V)))
    goal = rng.choice(np.array([TH, TH - 1, -TH, 1 - TH] + [TH + 1] * 8 + [-TH - 1] * 8 + [TH + 2] * 4 + [-TH - 2] * 4 + [S - 2] * 2), (8, 1, V))
    tie = (S - goal) % 2; nb = (S - tie - goal) // 2
    o = np.argsort(np.argsort(rng.random((8, S - 1, V), dtype=np.float32), axis=1), axis=1)
    run = rng.random((8, 1, V)); k = np.arange(S - 1)[None, :, None]
    o = np.where(run < 0.35, S - 2 - k, np.where(run < 0.6, k, o))
    out = np.where(rng.random((8, S - 1, V), dtype=np.float32) < 0.5, 10, 250)
    rest = np.where(low | high, lv, np.where(o < nb, 150, out))
    head = np.where(low, 100, np.where(high, lv, np.where(tie == 1, 100, 250)))
    s = np.concatenate([head, rest], axis=1)
    return pack(s, A, tests(rng, A, (low | high)[:, 0].astype(np.float64), 0))
def setup_inputs_alike(rng):
    A, place = graph(rng, (0, 6, 7)); o = place[7, :32 * (V // 128)]; A[7][:, o] = A[7, 0, o]
    A = thin(rng, A, [ROOM] * 16); A[1::2, 8:] = A[1::2, :8]
    A[::6, 1] = A[::6, 0]; A[6, 9:] = A[6, 8]
    s = cloud(rng, place, [0, 0.3, 1]); s[2:6] = 255 * (rng.random((4, S, V)) < 0.5)
    for g in (0, 7):
        p = A[g, 15]; lo = np.nonzero((p < V) & (U < p))[0]; lo = rng.permutation(lo)[:V // 20]; s[g][:, p[lo]] = s[g][:, lo]
    return pack(s, A, tests(rng, A, np.zeros((8, V)), 0))
def setup_inputs_bare(rng):
    A, place = graph(rng); A = thin(rng, A, [ROOM] * RO + [V // 2] * (16 - RO))
    A[1, RO:15] = V; A[2, RO:] = V; A[6, RO + 1:] = V
    s = cloud(rng, place, [0, 0, 0.3, 1]); first = np.zeros((8, V)); first[:, 0] = 1; first[:, V - 1] = 1
    for g in range(8):
        for c in (0, V - 1):
            y = int(A[g, RO, c])
            if y < V:
                s[g][:, c] = s[g][:, y]; first[g, y] = 1
    return pack(s, A, tests(rng, A, first, 0))
def setup_inputs_chain(rng):
    A, place = graph(rng, (5, 6)); A = thin(rng, A, [ROOM] * 16)
    s = cloud(rng, place, [0.3, 0.6, 1])
    s[5] = rng.integers(0, 256, (S, 1))
    s[6] = rng.integers(0, 256, (S, V)); p = A[6, 1]; lo = np.nonzero((p < V) & (U < p))[0]; s[6][:, p[lo]] = s[6][:, lo]
    return pack(s, A, tests(rng, A, np.zeros((8, V)), 1))
def setup_inputs_spread(rng):
    A, place = graph(rng); A = thin(rng, A, [ROOM] * 16)
    s = np.floor(np.exp2(8 * rng.random((8, 1, V))) * rng.random((8, S, V))) * (rng.random((8, 1, V)) > 0.0625)
    return pack(s.astype(np.int64), A, tests(rng, A, np.zeros((8, V)), 0))
def check_inputs(d):
    bad = []; xf = d["x"].astype(np.float32)
    if not np.all((xf >= 0) & (xf <= 255) & (np.floor(xf) == xf)): bad.append("range of x")
    for k, hi in (("adj", V), ("tv", V - 1)):
        if np.min(d[k]) < 0 or np.max(d[k]) > hi: bad.append("range of " + k)
        if np.any(d[k] != d[k][:1]): bad.append(k + " alike on all ranks")
    if "range of adj" in bad or "range of tv" in bad: return bad
    A = d["adj"][0].astype(np.int64).reshape(8, 16, V); B = np.concatenate([A, np.full((8, 16, 1), V, np.int64)], axis=2)
    if not np.all((A == V) | ((np.take_along_axis(B, A, 2) == U) & (A != U))): bad.append("partners are mutual")
    vs = gentries(d["tv"][0]).astype(np.int64).reshape(8, RO, E); g8 = np.arange(8)[:, None]
    for t in range(RO):
        v = vs[:, t]; y = A[g8, t, v]; both = np.sort(np.concatenate([v, y], axis=1), axis=1)
        if np.any(y >= V) or np.any(both[:, 1:] == both[:, :-1]): bad.append("ends of round " + str(t))
    return bad
def reference(x, adj, tv):
    A = adj[0].astype(np.int64).reshape(8, 16, V)
    s = np.ascontiguousarray(x.astype(np.float32).astype(np.int32).reshape(N, 8, 16, V).transpose(1, 0, 2, 3)).reshape(8, S, V)
    vs = gentries(tv[0]).astype(np.int64).reshape(8, RO, E); ys = np.zeros((8, RO, E), np.int64); sp = np.full((8, RO, E), V, np.int64)
    g8 = np.arange(8)[:, None]; g3 = np.arange(8)[:, None, None]; i3 = np.arange(16)[None, :, None]
    for t in range(RO):
        v = vs[:, t]; y = A[g8, t, v]; ys[:, t] = y
        z = A[g3, i3, y[:, None, :]]
        zz = np.where(z < V, z, 0); a = np.zeros((8, 16, E), np.int64)
        xv = np.take_along_axis(s, v[:, None, :], 2); xy = np.take_along_axis(s, y[:, None, :], 2)
        for i in range(16):
            xz = np.take_along_axis(s, zz[:, i][:, None, :], 2)
            a[:, i] = np.sum(np.sign((xv - xz) * (xy - xz)), axis=1)
        ok = (z < V) & (z != v[:, None, :]) & (np.abs(a) <= TH)
        hit = np.any(ok, axis=1); i1 = np.argmax(ok, axis=1)
        sp[:, t] = np.where(hit, np.take_along_axis(z, i1[:, None, :], 1)[:, 0], V)
        A[g8, t, v] = np.where(hit, V, y); A[g8, t, y] = np.where(hit, V, v)
    v = vs.reshape(8, 1, M); y = ys.reshape(8, 1, M); se = sp.reshape(8, 1, M)
    w = A[g3, i3, y]; ww = np.where(w < V, w, 0); inside = np.zeros((8, 16, M), bool)
    for i in range(16): inside = inside | (A[g3, i, ww] == v)
    fl = (se < V) & (w < V) & inside & (w != se)
    return {"ysep": np.stack([sp.reshape(8, M)] * N).astype(np.float32),
            "yflag": np.stack([fl[:, :, r * F:(r + 1) * F].reshape(128, F) for r in range(N)]).astype(np.float32).astype(BF)}

@@ -1,0 +1,477 @@
+from concourse.bass import DstId, RemoteDMATransfer
+from concourse.mybir import AluOpType as A, ActivationFunctionType as F
+
+V, H, NB = 2304, 1152.0, 4
+VSIGN = (26, 27, 28)
+SPLIT = (29,)
+VRELU = (0, 4, 8, 12, 16, 20, 24)
+MID = (6, 8)
+PRE = 11
+
+
+def _sb(n, d):
+    return ("sbuf", [128, n], d)
+
+
+SCRATCH = {
+    "XS": ("dram", [4, 128, 576], "bfloat16"), "XL": ("dram", [4, 128, 576], "bfloat16"),
+    "SD0": ("dram", [4, 128, 16], "float32"), "SD1": ("dram", [4, 128, 16], "float32"),
+    "FD": ("dram", [4, 128, 256], "bfloat16"),
+    "X": _sb(V, "bfloat16"), "A32": _sb(576, "int32"), "A16": _sb(576, "float16"), "AW": _sb(V, "float32"),
+    "T32": _sb(128, "int32"), "VL": _sb(128, "uint16"), "YL": _sb(128, "uint16"), "OL": _sb(64, "uint16"),
+    "ZL": _sb(2048, "uint16"), "YO": _sb(32, "float16"), "CV": _sb(512, "float16"), "CY": _sb(512, "float16"),
+    "T1": _sb(512, "float16"),
+    "KI": _sb(1, "int32"), "KB": _sb(8, "int32"), "KF": _sb(8, "float32"), "KS": _sb(16, "float32"),
+    "JX": _sb(256, "bfloat16"), "J": _sb(1024, "bfloat16"), "J16": _sb(128, "bfloat16"),
+    "SA": _sb(512, "float16"), "SY": _sb(288, "float16"), "RK": _sb(512, "float16"), "SQ": _sb(2048, "float16"),
+    "BC": _sb(2048, "float16"), "I16": _sb(128, "float16"), "NI16": _sb(128, "float16"), "OG16": _sb(128, "float16"),
+    "WD": _sb(144, "float16"), "WDM": _sb(144, "bfloat16"),
+    "I1": _sb(128, "bfloat16"), "IN": _sb(128, "bfloat16"), "I2": _sb(128, "bfloat16"), "IM2": _sb(128, "bfloat16"),
+    "IP": _sb(128, "bfloat16"), "IM32": _sb(128, "bfloat16"), "OG": _sb(128, "bfloat16"), "TR": _sb(128, "bfloat16"),
+    "WS": _sb(240, "bfloat16"), "WR": _sb(224, "bfloat16"), "WY0": _sb(224, "bfloat16"), "WY1": _sb(224, "bfloat16"),
+    "WYP": _sb(224, "bfloat16"),
+    "HV": _sb(2048, "bfloat16"), "HY": _sb(2048, "bfloat16"), "M": _sb(2048, "float32"), "R": _sb(2048, "bfloat16"),
+    "EQ": _sb(1024, "bfloat16"), "EV": _sb(512, "bfloat16"), "EN": _sb(512, "bfloat16"), "W": _sb(512, "bfloat16"),
+    "U": _sb(1024 * NB, "bfloat16"), "U2": _sb(1024 * NB, "bfloat16"), "SG": _sb(2048, "bfloat16"),
+    "RM0": _sb(V, "bfloat16"), "RM1": _sb(V, "bfloat16"),
+    "AB": _sb(256, "bfloat16"), "OK": _sb(256, "bfloat16"), "HT": _sb(1024, "bfloat16"), "FI": _sb(256, "bfloat16"),
+    "PR": _sb(256, "float16"), "ES": _sb(512, "bfloat16"), "RV": _sb(2048, "bfloat16"), "RY": _sb(2048, "bfloat16"),
+    "SP0": _sb(16, "float32"), "SP1": _sb(16, "float32"), "FL0": _sb(256, "bfloat16"), "FL1": _sb(256, "bfloat16"),
+    "PB0": ("psum", [128, 1024], "float32"), "PB1": ("psum", [128, 1024], "float32"),
+    "A0": ("psum", [128, 512], "float32"), "A1": ("psum", [128, 512], "float32"),
+    "M0": ("psum", [128, 512], "float32"), "M1": ("psum", [128, 512], "float32"),
+}
+NDMA = 24
+SEMAPHORES = ["ev", "es", "ep", "eg", "sent", "xa0", "xa1", "xa2", "xa3", "sa0", "sa1", "fa"] + ["d%d" % j for j in range(NDMA)]
+BANKS = ("PB0a", "PB0b", "PB1a", "PB1b", "A0", "A1", "M0", "M1")
+
+
+def masks(topo, cores, r):
+    src = cores[r]
+    far = [d for d in range(len(cores)) if cores[d] not in topo.cores_of(src)]
+    near = [d for d in range(len(cores)) if d != r and d not in far]
+    off = topo.engines(src, cores[far[0]])
+    out = {}
+    n = len(off) // len(far)
+    for j, d in enumerate(far):
+        out[d] = off[j * n:(j + 1) * n]
+    for d in near:
+        out[d] = [e for e in topo.engines(src, cores[d]) if e not in off]
+    return out
+
+
+def rank_program(g, core, T, topo):
+    r = T.rank_of(core)
+    if r is None:
+        return
+    cores = T.cores
+    others = [d for d in range(4) if d != r]
+    eng = masks(topo, cores, r)
+    inc = {s: len(masks(topo, cores, s)[r]) for s in others}
+    ops = []
+
+    def op(q, fn, rd, wr, kind="c"):
+        ops.append({"q": q, "fn": fn, "rd": list(rd), "wr": list(wr), "kind": kind})
+
+    def vv(fn, rd, wr):
+        op("v", fn, rd, wr)
+
+    def ts(out, in0, s1, s2, o0, o1, rd, wr):
+        if o1 is None:
+            vv(lambda: g.vector.tensor_scalar(out, in0, s1, None, o0), rd, wr)
+        else:
+            vv(lambda: g.vector.tensor_scalar(out, in0, s1, s2, o0, o1), rd, wr)
+
+    def tt(out, a, b, o, rd, wr):
+        vv(lambda: g.vector.tensor_tensor(out, a, b, o), rd, wr)
+
+    def cp(out, a, rd, wr):
+        vv(lambda: g.vector.tensor_copy(out, a), rd, wr)
+
+    def act(out, a, f, rd, wr, bias=0.0, scale=1.0):
+        op("s", lambda: g.scalar.activation(out, a, f, bias=bias, scale=scale), rd, wr)
+
+    def mm(out, l, rh, st, sp, rd, bank):
+        op("p", lambda: g.tensor.matmul(out, l, rh, st, sp), rd, [bank])
+
+    def dma(q, out, a, rd, wr):
+        e = g.sync if q == "y" else g.scalar
+        op(q, lambda: e.dma_start(out, a), rd, wr, "d")
+
+    def iota(out, pat, base, cm, wr, small=True):
+        if small:
+            op("g", lambda: g.iota(out, pat, base, cm, allow_small_or_imprecise_dtypes=True), [], wr)
+        else:
+            op("g", lambda: g.iota(out, pat, base, cm), [], wr)
+
+    def send(srcs, dst, sem, rd):
+        def fn():
+            trs = []
+            for d in others:
+                rid, pid = topo.addr(cores[d], core)
+                trs.append(RemoteDMATransfer(dst_ids=[DstId(rid=rid, pnc=pid)], dma_engine_mask=sum(1 << e for e in eng[d]),
+                                             remote_sem=sem, src=srcs[d], dst=dst))
+            return g.remote_dma_fused(trs, local_sem=T.sem.sent)
+        op("g", fn, rd, [], "r")
+
+    def arrive(key, sem, n):
+        ops.append({"q": None, "kind": "x", "rd": [], "wr": [key], "sem": sem, "n": n})
+
+    def bank(j):
+        name = BANKS[j]
+        return (T[name[:3]], 512 * (j % 2)) if j < 4 else (T[name], 0)
+
+    lo = 32 * r
+    dma("s", T.A32[:], T.adj[lo:lo + 32, :], [], ["A32"])
+    for d in others:
+        dma("y", T.XS[d], T.x[32 * d:32 * d + 32, :], [], ["XS%d" % d])
+    for k in range(4):
+        dma("s", T.T32[32 * k:32 * k + 32, :], T.tv[lo:lo + 32, :], [], ["T32%d" % k])
+    dma("y", T.X[lo:lo + 32, :], T.x[lo:lo + 32, :], [], ["X%d" % r])
+    iota(T.KI[:], [[0, 1]], 0, 1, ["KI"], False)
+    iota(T.J[:, 0:512], [[32, 4], [0, 4], [1, 32]], 0, 0, ["Ja"])
+    iota(T.JX[:], [[1, 256]], 0, 0, ["JX"])
+    send({d: T.XS[d] for d in others}, T.XL[r], T.sem["xa%d" % r], ["XS%d" % d for d in others])
+    iota(T.J[:, 512:1024], [[32, 4], [0, 4], [1, 32]], 128, 0, ["Jb"])
+    iota(T.J16[:], [[16, 8], [0, 16]], 0, 0, ["J16"])
+    near_first = sorted(others, key=lambda s: -inc[s])
+    for s in near_first:
+        arrive("XL%d" % s, T.sem["xa%d" % s], inc[s])
+        dma("y", T.X[32 * s:32 * s + 32, :], T.XL[s], ["XL%d" % s], ["X%d" % s])
+    XK = ["X%d" % s for s in range(4)]
+
+    sh, an = A.arith_shift_right, A.bitwise_and
+    for c, (s1, s2, o0, o1) in enumerate([(3, None, an, None), (2, None, sh, None), (4, None, sh, None), (4, 1, sh, an),
+                                          (31, None, an, None), (15, None, an, None), (5, None, sh, None), (127, None, an, None)]):
+        ts(T.KB[:, c:c + 1], T.KI[:], s1, s2, o0, o1, ["KI"], ["KB%d" % c])
+    cp(T.KF[:], T.KB[:], ["KB%d" % c for c in range(8)], ["KF"])
+    kf = [T.KF[:, c:c + 1] for c in range(8)]
+    kk = kf[7]
+    ks = [T.KS[:, c:c + 1] for c in range(16)]
+    mu, ad, eq = A.mult, A.add, A.is_equal
+    for c, (a, s1, s2, o0, o1) in enumerate([
+            (0, 32.0, kf[1], mu, ad), (2, 16.0, kk, mu, ad), (3, 16.0, 111.0, mu, ad), (4, 96.0, None, ad, None),
+            (3, 64.0, 15.0, mu, ad), (2, 16.0, 15.0, mu, ad), (2, 16.0, None, mu, None), (5, 0.0, None, eq, None),
+            (5, 1.0, None, eq, None), (5, 0.0, -2.0, eq, mu), (5, 1.0, -2.0, eq, mu), (5, 0.0, 128.0, eq, mu)]):
+        ts(ks[c], kf[a], s1, s2, o0, o1, ["KF"], ["K%d" % c])
+    ts(T.SA[:], T.J[:, 0:512], ks[0], None, eq, None, ["Ja", "K0"], ["SA"])
+    ts(ks[12], kf[6], 16.0, ks[4], mu, ad, ["KF", "K4"], ["K12"])
+    for t in range(2):
+        ts(T.SY[:, 144 * t:144 * t + 144], T.JX[:, 0:144], ks[5], ks[7 + t], eq, mu, ["JX", "K5", "K7", "K8"], ["SY%d" % t])
+    ts(T.I1[:], T.JX[:, 0:128], kk, None, eq, None, ["JX", "KF"], ["I1"])
+    ts(T.I16[:], T.JX[:, 0:128], kk, None, eq, None, ["JX", "KF"], ["I16"])
+    ts(T.RK[:], T.J[:, 0:512], kk, None, eq, None, ["Ja", "KF"], ["RK"])
+
+    ts(T.A16[:], T.A32[:], -H, None, ad, None, ["A32"], ["A16"])
+    for j in range(8):
+        b, o = bank(j)
+        mm(b[:, o:o + 288], T.SA[:, 128 * (j // 2):128 * (j // 2) + 128], T.A16[:, 288 * (j % 2):288 * (j % 2) + 288], True, True,
+           ["SA", "A16"], BANKS[j])
+    for k in range(4):
+        for t in range(2):
+            cp(T.OL[32 * k:32 * k + 32, 32 * t:32 * t + 16], T.T32[32 * k:32 * k + 32, 64 * t + 16 * k:64 * t + 16 * k + 16],
+               ["T32%d" % k], ["OV%d%d" % (t, k)])
+    for j in range(8):
+        b, o = bank(j)
+        if j % 2 == 0 or j == 1:
+            act(T.AW[:, 288 * j:288 * j + 288], b[:, o:o + 288], F.Copy, [BANKS[j]], ["AW%d" % j])
+        else:
+            cp(T.AW[:, 288 * j:288 * j + 288], b[:, o:o + 288], [BANKS[j]], ["AW%d" % j])
+    AWK = ["AW%d" % j for j in range(8)]
+    for name, sc in (("IN", -1.0), ("I2", 2.0), ("IM2", -2.0), ("IP", 128.0), ("IM32", -32.0)):
+        act(T[name][:], T.I1[:], F.Copy, ["I1"], [name], scale=sc)
+    for t in range(2):
+        act(T["RM%d" % t][:], T.AW[:], F.Copy, AWK, ["RM%d" % t], scale=0.0)
+    for t in range(2):
+        cp(T.CV[:, 256 * t:256 * t + 256], T.AW[:].indirect(T.OL[:, 32 * t:32 * t + 16]), AWK + ["OV%d%d" % (t, k) for k in range(4)], ["CV%d" % t])
+        bk = "M%d" % t
+        for p in range(16):
+            mm(T[bk][:, 0:16], T.SY[:, 144 * t + 15 - p:144 * t + 143 - p], T.CV[:, 256 * t + p:256 * t + 256:16], p == 0, p == 15,
+               ["SY%d" % t, "CV%d" % t], bk)
+    cp(T.VL[:], T.T32[:], ["T32%d" % k for k in range(4)], ["VL"])
+    for t in range(2):
+        ts(T.OL[:, 32 * t + 16:32 * t + 32], T["M%d" % t][:, 0:16], H, None, ad, None, ["M%d" % t], ["OY%d" % t])
+        cp(T.YO[:, 16 * t:16 * t + 16], T["M%d" % t][:, 0:16], ["M%d" % t], ["YO%d" % t])
+    for t in range(2):
+        for k in range(4):
+            mm(T.A0[:, 64 * t + 16 * k:64 * t + 16 * k + 16], T.RK[:, 128 * k:128 * k + 128], T.YO[:, 16 * t:16 * t + 16], True, True,
+               ["RK", "YO%d" % t], "A0")
+    cp(T.CY[:, 0:256], T.AW[:].indirect(T.OL[:, 16:32]), AWK + ["OY0"], ["CY0"])
+    ts(T.YL[:], T.A0[:, 0:128], H, None, ad, None, ["A0"], ["YL"])
+    cp(T.CY[:, 256:512], T.AW[:].indirect(T.OL[:, 48:64]), AWK + ["OY1"], ["CY1"])
+    for t in range(2):
+        for h in range(2):
+            for k in range(4):
+                mm(T.M1[:, 8 * t + 2 * k + h:512:16], T.CY[:, 256 * t + 128 * h:256 * t + 128 * h + 128], T.I16[:, 32 * k:32 * k + 32], True, True,
+                   ["CY%d" % t, "I16"], "M1")
+    ts(T.SQ[:, 0:1024], T.J[:], ks[1], None, eq, None, ["Ja", "Jb", "K1"], ["SQ0"])
+    cp(T.T1[:], T.M1[:], ["M1"], ["T1"])
+    ts(T.SQ[:, 1024:2048], T.J[:], -16.0, ks[1], ad, eq, ["Ja", "Jb", "K1"], ["SQ1"])
+    for q in range(8):
+        bk = BANKS[4 + q // 2]
+        for gr in range(2):
+            mm(T[bk][:, 256 * (q % 2):256 * (q % 2) + 256], T.SQ[:, 1024 * gr + 128 * q:1024 * gr + 128 * q + 128], T.T1[:, 256 * gr:256 * gr + 256],
+               gr == 0, gr == 1, ["SQ0", "SQ1", "T1"], bk)
+
+    def bc(j):
+        ts(T.BC[:, 128 * j:128 * j + 128], T.J16[:], float(j), kk, ad, eq, ["J16", "KF"], ["BC%d" % j])
+    for j in range(4):
+        bc(j)
+    for q in range(8):
+        bk = BANKS[4 + q // 2]
+        ts(T.ZL[:, q:2048:8], T[bk][:, 256 * (q % 2):256 * (q % 2) + 256], H, float(V - 1), ad, A.min, [bk], ["ZL%d" % q])
+    ZK = ["ZL%d" % q for q in range(8)]
+
+    def ends(t):
+        for c, (out, lst) in enumerate(((T.HV, "VL"), (T.HY, "YL"))):
+            act(out[:, 1024 * t:1024 * t + 1024], T.X[:].indirect(T[lst][:, 64 * t:64 * t + 64]), F.Copy, XK + [lst], ["H%d%d" % (t, c)], scale=0.5)
+
+    def middle(t, j):
+        wn, out, f = (("I1", "M", F.Copy), ("IN", "R", F.Abs))[j]
+        for h in range(2):
+            b, o = bank(2 * j + h)
+            c = 1024 * t + 512 * h
+            mm(b[:, o:o + 512], T.I1[:], T.HV[:, c:c + 512], True, False, ["I1", "H%d0" % t], BANKS[2 * j + h])
+            mm(b[:, o:o + 512], T[wn][:], T.HY[:, c:c + 512], False, True, [wn, "H%d1" % t], BANKS[2 * j + h])
+        act(T[out][:, 1024 * t:1024 * t + 1024], T["PB%d" % j][:], f, ["PB%da" % j, "PB%db" % j], ["%s%d" % (out + out, t)])
+
+    CK = ["CY0", "CY1"]
+
+    def spread(n):
+        bk = "M%d" % (n % 2)
+        if n >= 2:
+            mm(T[bk][:], T.BC[:, 128 * n:128 * n + 128], T.CV[:], True, True, ["BC%d" % n, "CV0", "CV1"], bk)
+            return
+        for t in range(2):
+            j, src = (t, T.CY) if n == 0 else (1 - t, T.CV)
+            mm(T[bk][:, 256 * t:256 * t + 256], T.BC[:, 128 * j:128 * j + 128], src[:, 256 * t:256 * t + 256], True, True,
+               ["BC0", "BC1", "CV0", "CV1"] + CK, bk)
+
+    def match(n):
+        bk = "M%d" % (n % 2)
+        out, key = (T.EV[:], "EV") if n == 0 else (T.EQ[:, 512 * (n % 2):512 * (n % 2) + 512], "EQ%d" % (n % 2))
+        tt(out, T[bk][:], T.CY[:], eq, [bk] + CK, [key])
+        if n + 4 < 16:
+            bc(n + 4)
+        if n + 2 < 16:
+            spread(n + 2)
+        wn = "IM32" if n == 0 else "I1" if n == 1 else "I2"
+        mm(T.A1[:], T[wn][:], out, False, n == 15, [wn, key], "A1")
+
+    ts(T.EN[:], T.CY[:], H, None, eq, None, CK, ["EN"])
+    spread(0)
+    spread(1)
+    mm(T.A1[:], T.IM32[:], T.EN[:], True, False, ["IM32", "EN"], "A1")
+    ends(0)
+    for n in range(PRE):
+        match(n)
+        for j in range(2):
+            if n == MID[j]:
+                middle(0, j)
+    ends(1)
+    ts(T.WS[:], T.JX[:, 0:240], ks[2], None, eq, None, ["JX", "K2"], ["WS"])
+
+    def late():
+        ts(T.OG[:], T.J16[:], ks[6], None, eq, None, ["J16", "K6"], ["OG"])
+        ts(T.OG16[:], T.J16[:], ks[6], None, eq, None, ["J16", "K6"], ["OG16"])
+        ts(T.TR[:], T.JX[:, 0:128], kk, -1.0, A.is_ge, mu, ["JX", "KF"], ["TR"])
+        ts(T.NI16[:], T.JX[:, 0:128], kk, -1.0, eq, mu, ["JX", "KF"], ["NI16"])
+        ts(T.WD[:], T.JX[:, 0:144], ks[12], None, eq, None, ["JX", "K12"], ["WD"])
+        ts(T.WDM[:], T.JX[:, 0:144], ks[12], -H, eq, mu, ["JX", "K12"], ["WDM"])
+        ts(T.WR[:], T.JX[:, 0:224], ks[3], -1.0, eq, mu, ["JX", "K3"], ["WR"])
+        for name, c in (("WY0", 9), ("WY1", 10), ("WYP", 11)):
+            ts(T[name][:], T.JX[:, 0:224], ks[3], ks[c], eq, mu, ["JX", "K3", "K%d" % c], [name])
+        tt(T.TR[:], T.TR[:], T.OG[:], mu, ["TR", "OG"], ["TR"])
+
+    def removed(bk, c0, wn, src, t, last):
+        for k in range(4):
+            mm(T[bk][:, c0:c0 + 256], T[wn][:, 96 - 32 * k:224 - 32 * k], T[src][:, 1024 * t + 256 * k:1024 * t + 256 * k + 256], False,
+               last and k == 3, [wn, src + str(t)], bk)
+
+    def end_steps(t):
+        o, c = 1 - t, 256 * t
+        at, rm, ht = "A%d" % t, T["RM%d" % t], T.HT[:, 512 * t:512 * t + 512]
+
+        def s0():
+            act(T.AB[:], T[at][:, 0:256], F.Abs, [at], ["AB"])
+            ts(T.OK[:], T.AB[:], 6.0, None, A.is_le, None, ["AB"], ["OK"])
+            for h in range(2):
+                mm(T.M0[:, 256 * h:256 * h + 256], T.OG[:], T.OK[:], True, True, ["OG", "OK"], "M0")
+            mm(T.M1[:, 0:256], T.I2[:], T.OK[:], True, False, ["I2", "OK"], "M1")
+            mm(T.M1[:, 0:256], T.TR[:], T.OK[:], False, True, ["TR", "OK"], "M1")
+
+        def s1():
+            act(ht, T.M0[:], F.Sign, ["M0"], ["HT%d" % t])
+            act(T.FI[:], T.M1[:, 0:256], F.Relu, ["M1"], ["FI"])
+
+        def s2():
+            cp(rm[:].indirect(T.OL[:, 32 * t:32 * t + 32]), ht, ["HT%d" % t, "OY%d" % t, "RM%d" % t], ["RM%d" % t])
+            tt(T.PR[:], T.FI[:], T.CY[:, c:c + 256], mu, ["FI"] + CK, ["PR"])
+            mm(T.M0[:, 0:256], T.OG16[:], T.PR[:], True, False, ["OG16", "PR"], "M0")
+            mm(T.M0[:, 0:256], T.NI16[:], T.CY[:, c:c + 256], False, True, ["NI16"] + CK, "M0")
+            for i in range(16):
+                mm(T.M1[:, 0:16], T.WD[:, 15 - i:143 - i], T.PR[:, 16 * i:16 * i + 16], i == 0, False, ["WD", "PR"], "M1")
+                mm(T.M1[:, 0:16], T.WDM[:, 15 - i:143 - i], T.FI[:, 16 * i:16 * i + 16], False, i == 15, ["WDM", "FI"], "M1")
+
+        def s3():
+            act(T.RY[:, 1024 * t:1024 * t + 1024], rm[:].indirect(T.YL[:, 64 * o:64 * o + 64]), F.Copy, ["RM%d" % t, "YL"], ["RY%d" % t])
+            cp(T.RV[:, 1024 * t:1024 * t + 1024], rm[:].indirect(T.VL[:, 64 * o:64 * o + 64]), ["RM%d" % t, "VL"], ["RV%d" % t])
+            act(T["SP%d" % t][:], T.M1[:, 0:16], F.Identity, ["M1"], ["SP%d" % t], bias=float(V))
+            ts(T.ES[:, c:c + 256], T.M0[:, 0:256], 0.0, None, eq, None, ["M0"], ["ES%d" % t])
+            sd = T["SD%d" % t]
+            send({d: T["SP%d" % t][:] for d in others}, sd[r], T.sem["sa%d" % t], ["SP%d" % t])
+            dma("y", sd[r], T["SP%d" % t][:], ["SP%d" % t], ["SO%d" % t])
+            arrive("SR%d" % t, T.sem["sa%d" % t], sum(inc.values()))
+
+        return [s0, s1, s2, s3]
+
+    def score(t, bk):
+        c = 256 * t
+        mm(T[bk][:, 256:512], T.I1[:], T.W[:, c:c + 256], True, False, ["I1", "W"], bk)
+        mm(T[bk][:, 256:512], T.I2[:], T.HT[:, 512 * t:512 * t + 256], False, False, ["I2", "HT%d" % t], bk)
+
+    def sep_out(t):
+        dma("y", T.ysep[:, 1024 * t:1024 * t + 1024], T["SD%d" % t][:], ["SO%d" % t, "SR%d" % t], ["ys%d" % t])
+
+    chunks = [(t, i) for t in range(2) for i in range(16) if i != t]
+
+    def gather(n):
+        t, i = chunks[n]
+        c = 1024 * (n % NB)
+        tt(T.U[:, c:c + 1024], T.X[:].indirect(T.ZL[:, 128 * i + 64 * t:128 * i + 64 * t + 64]), T.M[:, 1024 * t:1024 * t + 1024], A.subtract,
+           XK + ZK + ["MM%d" % t], ["U%d" % (n % NB)])
+        if n in VRELU:
+            ts(T.U2[:, c:c + 1024], T.U[:, c:c + 1024], 0.0, 2.0, A.max, mu, ["U%d" % (n % NB)], ["UR%d" % (n % NB)])
+
+    def fold(n):
+        t, i = chunks[n]
+        key, c = "U%d" % (n % NB), 1024 * (n % NB)
+        terms = [("I1", T.U, c, key), ("IN", T.R, 1024 * t, "RR%d" % t)]
+        if n in VRELU:
+            terms = [("I1", T.U2, c, "UR%d" % (n % NB)), ("IN", T.U, c, key)] + terms[1:]
+        else:
+            act(T.U[:, c:c + 1024], T.U[:, c:c + 1024], F.Abs, [key], [key])
+        for j, (wn, src, c0, k) in enumerate(terms):
+            for h in range(2):
+                b, o = bank(2 * (n % 2) + h)
+                mm(b[:, o:o + 512], T[wn][:], src[:, c0 + 512 * h:c0 + 512 * h + 512], j == 0, j == len(terms) - 1, [wn, k], BANKS[2 * (n % 2) + h])
+
+    def total(n):
+        t, i = chunks[n]
+        at, key, pb, c = "A%d" % t, "SG%d" % (n % 2), "PB%d" % (n % 2), 1024 * (n % 2)
+        if n in SPLIT:
+            act(T.SG[:, c:c + 512], T[pb][:, 0:512], F.Sign, [pb + "a"], [key + "a"])
+            ts(T.SG[:, c + 512:c + 1024], T[pb][:, 512:1024], -1.0, 1.0, A.max, A.min, [pb + "b"], [key + "b"])
+        elif n in VSIGN:
+            ts(T.SG[:, c:c + 1024], T[pb][:], -1.0, 1.0, A.max, A.min, [pb + "a", pb + "b"], [key + "a", key + "b"])
+        else:
+            act(T.SG[:, c:c + 1024], T[pb][:], F.Sign, [pb + "a", pb + "b"], [key + "a", key + "b"])
+        if n % 15 == 0:
+            mm(T[at][:, 0:256], T.IP[:], T.EV[:, 256 * t:256 * t + 256], True, False, ["IP", "EV"], at)
+            mm(T[at][:, 0:256], T.IP[:], T.EN[:, 256 * t:256 * t + 256], False, False, ["IP", "EN"], at)
+        for k in range(4):
+            x0 = 111 - 32 * k - i
+            mm(T[at][:, 0:256], T.WS[:, x0:x0 + 128], T.SG[:, c + 256 * k:c + 256 * k + 256], False, n % 15 == 14 and k == 3,
+               ["WS", key + "ab"[k // 2]], at)
+
+    e0 = end_steps(0)
+    for n in range(NB - 1):
+        gather(n)
+    middle(1, 0)
+    middle(1, 1)
+    fold(0)
+    for n in range(30):
+        if n + NB - 1 < 30:
+            gather(n + NB - 1)
+        if n + 1 < 30:
+            fold(n + 1)
+        total(n)
+        if PRE + n < 16:
+            match(PRE + n)
+        if PRE + n == 16:
+            ts(T.W[:], T.A1[:], 2.0, None, A.min, None, ["A1"], ["W"])
+        if n == 8:
+            late()
+        if 15 <= n < 19:
+            e0[n - 15]()
+        if n == 21:
+            removed("A1", 0, "WYP", "RY", 0, False)
+            score(0, "A0")
+            mm(T.A0[:, 256:512], T.IM2[:], T.ES[:, 0:256], False, False, ["IM2", "ES0"], "A0")
+            sep_out(0)
+    e1 = end_steps(1)
+    e1[0]()
+    e1[1]()
+    score(1, "A1")
+    removed("A1", 256, "WR", "RV", 0, False)
+    removed("A1", 256, "WY0", "RY", 0, False)
+    e1[2]()
+    e1[3]()
+    removed("A0", 256, "WY1", "RY", 1, False)
+    removed("A0", 256, "WR", "RV", 1, True)
+    mm(T.A1[:, 256:512], T.IM2[:], T.ES[:, 256:512], False, True, ["IM2", "ES1"], "A1")
+    for t in range(2):
+        ts(T["FL%d" % t][:], T["A%d" % t][:, 256:512], 3.0, None, A.is_ge, None, ["A%d" % t], ["FL%d" % t])
+    send({d: T["FL%d" % (d // 2)][:] for d in others}, T.FD[r], T.sem.fa, ["FL0", "FL1"])
+    dma("s", T.FD[r], T["FL%d" % (r // 2)][:], ["FL%d" % (r // 2)], ["FO"])
+    sep_out(1)
+    arrive("FR", T.sem.fa, sum(inc.values()))
+    for h in range(2):
+        p0 = 64 * (r % 2) + 32 * h
+        dma("y" if h == 0 else "s", T.yflag[:, 256 * h:256 * h + 256], T.FD[:, p0:p0 + 32, :], ["FO", "FR"], ["yf%d" % h])
+
+    wrote, read, deps = {}, {}, []
+    for n, o in enumerate(ops):
+        need = set()
+        for key in o["rd"]:
+            if key in wrote:
+                need.add(wrote[key])
+            if key in BANKS:
+                need.update(m for m in read.get(key, []) if ops[m]["q"] != o["q"])
+        for key in o["wr"]:
+            for m in read.get(key, []) + ([wrote[key]] if key in wrote else []):
+                if ops[m]["q"] != o["q"] or ops[m]["kind"] != "c" or o["kind"] != "c":
+                    need.add(m)
+        need.discard(n)
+        last = {}
+        for m in need:
+            c = ops[m]["q"] if ops[m]["kind"] == "c" else ("own", m)
+            last[c] = max(last.get(c, -1), m)
+        deps.append(sorted(last.values()))
+        for key in o["wr"]:
+            wrote[key] = n
+            read[key] = []
+        for key in o["rd"]:
+            if key not in o["wr"]:
+                read.setdefault(key, []).append(n)
+    marked = set(m for d in deps for m in d)
+    queue = {"v": g.vector, "s": g.scalar, "p": g.tensor, "g": g, "y": g.sync}
+    esem = {"v": "ev", "s": "es", "p": "ep", "g": "eg"}
+    count, sig, seen, nd, total_sent, dsems = {}, {}, {}, [0], [0], []
+    for n, o in enumerate(ops):
+        if o["kind"] == "x":
+            sig[n] = (o["sem"], o["n"], "x%d" % n)
+            continue
+        for m in deps[n]:
+            sem, val, name = sig[m]
+            if seen.get((o["q"], name), 0) < val:
+                queue[o["q"]].wait_ge(sem, val)
+                seen[(o["q"], name)] = val
+        ins = o["fn"]()
+        if o["kind"] == "d":
+            name = "d%d" % nd[0]
+            nd[0] += 1
+            ins.then_inc(T.sem[name], 16)
+            sig[n] = (T.sem[name], 16, name)
+            dsems.append(name)
+        elif o["kind"] == "r":
+            total_sent[0] += sum(len(e) for e in eng.values())
+        elif n in marked:
+            name = esem[o["q"]]
+            count[name] = count.get(name, 0) + 1
+            ins.then_inc(T.sem[name], 1)
+            sig[n] = (T.sem[name], count[name], name)
+    g.wait_ge(T.sem.sent, total_sent[0])
+    for name in dsems:
+        if not any(k[1] == name for k in seen):
+            g.sync.wait_ge(T.sem[name], 16)

@@ -1,49 +1,46 @@
 from concourse.bass import DstId, RemoteDMATransfer
 from concourse.mybir import AluOpType as A, ActivationFunctionType as F
 
-V, H, NB = 2304, 1152.0, 4
-VSIGN = (26, 27, 28)
-SPLIT = (29,)
-VRELU = (0, 4, 8, 12, 16, 20, 24)
-MID = (6, 8)
-PRE = 11
+V, H = 2304, 1152.0
+NU, NC, NS, NK = 6, 4, 4, 14
+SCAL = (4, 6, 9, 12, 16, 19, 22, 25, 28)
+SPLIT = ()
+AHEAD, LEAD = 7, 3
+PRE, IDX, MID = 14, 8, (10, 11)
 
 
-def _sb(n, d):
+def _sb(n, d="bfloat16"):
     return ("sbuf", [128, n], d)
 
 
 SCRATCH = {
     "XS": ("dram", [4, 128, 576], "bfloat16"), "XL": ("dram", [4, 128, 576], "bfloat16"),
     "SD0": ("dram", [4, 128, 16], "float32"), "SD1": ("dram", [4, 128, 16], "float32"),
-    "FD": ("dram", [4, 128, 256], "bfloat16"),
-    "X": _sb(V, "bfloat16"), "A32": _sb(576, "int32"), "A16": _sb(576, "float16"), "AW": _sb(V, "float32"),
-    "T32": _sb(128, "int32"), "VL": _sb(128, "uint16"), "YL": _sb(128, "uint16"), "OL": _sb(64, "uint16"),
-    "ZL": _sb(2048, "uint16"), "YO": _sb(32, "float16"), "CV": _sb(512, "float16"), "CY": _sb(512, "float16"),
-    "T1": _sb(512, "float16"),
-    "KI": _sb(1, "int32"), "KB": _sb(8, "int32"), "KF": _sb(8, "float32"), "KS": _sb(16, "float32"),
-    "JX": _sb(256, "bfloat16"), "J": _sb(1024, "bfloat16"), "J16": _sb(128, "bfloat16"),
-    "SA": _sb(512, "float16"), "SY": _sb(288, "float16"), "RK": _sb(512, "float16"), "SQ": _sb(2048, "float16"),
-    "BC": _sb(2048, "float16"), "I16": _sb(128, "float16"), "NI16": _sb(128, "float16"), "OG16": _sb(128, "float16"),
-    "WD": _sb(144, "float16"), "WDM": _sb(144, "bfloat16"),
-    "I1": _sb(128, "bfloat16"), "IN": _sb(128, "bfloat16"), "I2": _sb(128, "bfloat16"), "IM2": _sb(128, "bfloat16"),
-    "IP": _sb(128, "bfloat16"), "IM32": _sb(128, "bfloat16"), "OG": _sb(128, "bfloat16"), "TR": _sb(128, "bfloat16"),
-    "WS": _sb(240, "bfloat16"), "WR": _sb(224, "bfloat16"), "WY0": _sb(224, "bfloat16"), "WY1": _sb(224, "bfloat16"),
-    "WYP": _sb(224, "bfloat16"),
-    "HV": _sb(2048, "bfloat16"), "HY": _sb(2048, "bfloat16"), "M": _sb(2048, "float32"), "R": _sb(2048, "bfloat16"),
-    "EQ": _sb(1024, "bfloat16"), "EV": _sb(512, "bfloat16"), "EN": _sb(512, "bfloat16"), "W": _sb(512, "bfloat16"),
-    "U": _sb(1024 * NB, "bfloat16"), "U2": _sb(1024 * NB, "bfloat16"), "SG": _sb(2048, "bfloat16"),
-    "RM0": _sb(V, "bfloat16"), "RM1": _sb(V, "bfloat16"),
-    "AB": _sb(256, "bfloat16"), "OK": _sb(256, "bfloat16"), "HT": _sb(1024, "bfloat16"), "FI": _sb(256, "bfloat16"),
-    "PR": _sb(256, "float16"), "ES": _sb(512, "bfloat16"), "RV": _sb(2048, "bfloat16"), "RY": _sb(2048, "bfloat16"),
-    "SP0": _sb(16, "float32"), "SP1": _sb(16, "float32"), "FL0": _sb(256, "bfloat16"), "FL1": _sb(256, "bfloat16"),
+    "FD": ("dram", [4, 128, 128], "bfloat16"),
+    "X": _sb(V), "A32": _sb(576, "int32"), "A16": _sb(576, "float16"), "AW": _sb(V, "float32"),
+    "TQ": _sb(104, "int32"), "T32": _sb(128, "int32"), "VL": _sb(128, "uint16"), "YL": _sb(128, "uint16"),
+    "OL": _sb(64, "uint16"), "ML": _sb(32, "uint16"), "ZL": _sb(2048, "uint16"), "YO": _sb(32, "float16"),
+    "CV": _sb(512, "float16"), "CY": _sb(512, "float16"), "T1": _sb(512, "float16"), "IG": _sb(512, "float16"),
+    "KI": _sb(1, "int32"), "KB": _sb(2, "int32"), "KF": _sb(4, "float32"),
+    "ZR": _sb(512), "J16": _sb(128), "JG": _sb(32), "JX": _sb(168),
+    "SA": _sb(512), "SY": _sb(288), "SY4": _sb(144), "RK": _sb(512), "SQ": _sb(1152), "BC": _sb(2048),
+    "I1": _sb(128), "IN": _sb(128), "I2": _sb(128), "GG": _sb(32), "NG": _sb(32), "GK": _sb(512), "WD": _sb(168),
+    "OG": _sb(128), "TR": _sb(128), "PM": _sb(128), "MY": _sb(128),
+    "RV0": _sb(128), "RY0": _sb(128), "RV1": _sb(128), "RY1": _sb(128),
+    "HV": _sb(2048), "HY": _sb(2048), "R": _sb(2048), "LO": _sb(2048), "DL": _sb(2048),
+    "EQ": _sb(1024), "EV": _sb(512), "EN": _sb(512), "W": _sb(512),
+    "U": _sb(1024 * NU), "UK": _sb(1024 * NK), "C": _sb(1024 * NC), "SG": _sb(1024 * NS),
+    "RM": _sb(V), "IM": _sb(V, "float32"), "IV": _sb(256, "float32"), "HW": _sb(1040),
+    "AB": _sb(256), "OK": _sb(256), "HT0": _sb(512), "HT1": _sb(256), "PR": _sb(256, "float16"), "ES": _sb(512),
+    "RG0": _sb(512), "RG1": _sb(512), "SP0": _sb(16, "float32"), "SP1": _sb(16, "float32"), "FL": _sb(512),
     "PB0": ("psum", [128, 1024], "float32"), "PB1": ("psum", [128, 1024], "float32"),
-    "A0": ("psum", [128, 512], "float32"), "A1": ("psum", [128, 512], "float32"),
+    "AT": ("psum", [128, 512], "float32"), "WB": ("psum", [128, 512], "float32"),
     "M0": ("psum", [128, 512], "float32"), "M1": ("psum", [128, 512], "float32"),
 }
-NDMA = 24
-SEMAPHORES = ["ev", "es", "ep", "eg", "sent", "xa0", "xa1", "xa2", "xa3", "sa0", "sa1", "fa"] + ["d%d" % j for j in range(NDMA)]
-BANKS = ("PB0a", "PB0b", "PB1a", "PB1b", "A0", "A1", "M0", "M1")
+NDMA = 40
+SEMAPHORES = (["ev", "es", "ep", "eg", "sent", "sa0", "sa1"] + ["xa%d" % j for j in range(4)] + ["fa%d" % j for j in range(4)]
+              + ["d%d" % j for j in range(NDMA)])
+BANKS = ("PB0a", "PB0b", "PB1a", "PB1b", "AT", "WB", "M0", "M1")
 
 
 def masks(topo, cores, r):
@@ -57,7 +54,7 @@ def masks(topo, cores, r):
         out[d] = off[j * n:(j + 1) * n]
     for d in near:
         out[d] = [e for e in topo.engines(src, cores[d]) if e not in off]
-    return out
+    return out, far, near
 
 
 def rank_program(g, core, T, topo):
@@ -66,27 +63,27 @@ def rank_program(g, core, T, topo):
         return
     cores = T.cores
     others = [d for d in range(4) if d != r]
-    eng = masks(topo, cores, r)
-    inc = {s: len(masks(topo, cores, s)[r]) for s in others}
-    ops = []
+    eng, far, near = masks(topo, cores, r)
+    inc = {s: len(masks(topo, cores, s)[0][r]) for s in others}
+    ops, sent = [], [0]
+    mu, ad, eq, ne, ge = A.mult, A.add, A.is_equal, A.not_equal, A.is_ge
 
     def op(q, fn, rd, wr, kind="c"):
+        if q == "g" and kind == "c" and any(o["kind"] == "r" for o in ops):
+            rd, wr = list(rd) + ["pool"], list(wr) + ["pool"]
         ops.append({"q": q, "fn": fn, "rd": list(rd), "wr": list(wr), "kind": kind})
-
-    def vv(fn, rd, wr):
-        op("v", fn, rd, wr)
 
     def ts(out, in0, s1, s2, o0, o1, rd, wr):
         if o1 is None:
-            vv(lambda: g.vector.tensor_scalar(out, in0, s1, None, o0), rd, wr)
+            op("v", lambda: g.vector.tensor_scalar(out, in0, s1, None, o0), rd, wr)
         else:
-            vv(lambda: g.vector.tensor_scalar(out, in0, s1, s2, o0, o1), rd, wr)
+            op("v", lambda: g.vector.tensor_scalar(out, in0, s1, s2, o0, o1), rd, wr)
 
     def tt(out, a, b, o, rd, wr):
-        vv(lambda: g.vector.tensor_tensor(out, a, b, o), rd, wr)
+        op("v", lambda: g.vector.tensor_tensor(out, a, b, o), rd, wr)
 
     def cp(out, a, rd, wr):
-        vv(lambda: g.vector.tensor_copy(out, a), rd, wr)
+        op("v", lambda: g.vector.tensor_copy(out, a), rd, wr)
 
     def act(out, a, f, rd, wr, bias=0.0, scale=1.0):
         op("s", lambda: g.scalar.activation(out, a, f, bias=bias, scale=scale), rd, wr)
@@ -94,24 +91,30 @@ def rank_program(g, core, T, topo):
     def mm(out, l, rh, st, sp, rd, bank):
         op("p", lambda: g.tensor.matmul(out, l, rh, st, sp), rd, [bank])
 
-    def dma(q, out, a, rd, wr):
+    def dma(q, pairs, rd, wr):
         e = g.sync if q == "y" else g.scalar
-        op(q, lambda: e.dma_start(out, a), rd, wr, "d")
+        op(q, lambda: [e.dma_start(o, a) for o, a in pairs], rd, wr, "d")
 
-    def iota(out, pat, base, cm, wr, small=True):
-        if small:
-            op("g", lambda: g.iota(out, pat, base, cm, allow_small_or_imprecise_dtypes=True), [], wr)
-        else:
-            op("g", lambda: g.iota(out, pat, base, cm), [], wr)
+    def iota(out, pat, base, cm, wr):
+        op("g", lambda: g.iota(out, pat, base, cm, allow_small_or_imprecise_dtypes=True), [], wr)
 
-    def send(srcs, dst, sem, rd):
+    def mark(out, n, pat, base, val, key):
+        op("g", lambda: g.affine_select(out, T.ZR[:, 0:n], pat, ne, val, base, 1), ["ZR"], [key])
+
+    def band(out, n, pat, base, width, val, key):
+        neg = [[-s, c] for s, c in pat]
+        op("g", lambda: g.affine_select(out, T.ZR[:, 0:n], neg, ge, val, -base - 1, -1), ["ZR"], [key])
+        op("g", lambda: g.affine_select(out, out, neg, ge, 0.0, width - 1 - base, -1), [key], [key])
+
+    def send(to, srcs, dst, sem, rd):
         def fn():
             trs = []
-            for d in others:
+            for d in to:
                 rid, pid = topo.addr(cores[d], core)
                 trs.append(RemoteDMATransfer(dst_ids=[DstId(rid=rid, pnc=pid)], dma_engine_mask=sum(1 << e for e in eng[d]),
                                              remote_sem=sem, src=srcs[d], dst=dst))
             return g.remote_dma_fused(trs, local_sem=T.sem.sent)
+        sent[0] += sum(len(eng[d]) for d in to)
         op("g", fn, rd, [], "r")
 
     def arrive(key, sem, n):
@@ -122,55 +125,52 @@ def rank_program(g, core, T, topo):
         return (T[name[:3]], 512 * (j % 2)) if j < 4 else (T[name], 0)
 
     lo = 32 * r
-    dma("s", T.A32[:], T.adj[lo:lo + 32, :], [], ["A32"])
-    for d in others:
-        dma("y", T.XS[d], T.x[32 * d:32 * d + 32, :], [], ["XS%d" % d])
+    dma("s", [(T.A32[:], T.adj[lo:lo + 32, :])], [], ["A32"])
+    dma("y", [(T.TQ[32 * k:32 * k + 32, :], T.tv[lo:lo + 32, 8 * k:8 * k + 104]) for k in range(4)], [], ["TQ"])
+    dma("s", [(T.XS[d], T.x[32 * d:32 * d + 32, :]) for d in far], [], ["XSf"])
+    dma("y", [(T.XS[d], T.x[32 * d:32 * d + 32, :]) for d in near], [], ["XSn"])
+    dma("y", [(T.T32[32 * k:32 * k + 32, :], T.tv[lo:lo + 32, :]) for k in range(4)], [], ["T32"])
+    dma("y", [(T.X[lo:lo + 32, :], T.x[lo:lo + 32, :])], [], ["X%d" % r])
+    op("v", lambda: g.vector.memset(T.ZR[:], 0.0), [], ["ZR"])
+    op("g", lambda: g.iota(T.KI[:], [[0, 1]], 0, 1), [], ["KI"])
+    iota(T.J16[:], [[-16, 8], [0, 16]], 0, 1, ["J16"])
+    mark(T.SA[:], 512, [[-1, 4], [0, 4], [-4, 32]], 0, 1.0, "SA")
+    mark(T.SY[:], 288, [[-1, 2], [-16, 9], [128, 16]], -128 * 15, 1.0, "SY")
+    mark(T.I1[:], 128, [[-1, 128]], 0, 1.0, "I1")
+    mark(T.SQ[:, 128:384], 256, [[128, 2], [-1, 16], [-16, 8]], 0, 1.0, "SQ0")
+    send(far, T.XS, T.XL[r], T.sem["xa%d" % r], ["XSf"])
+    send(near, T.XS, T.XL[r], T.sem["xa%d" % r], ["XSn"])
+    mark(T.RK[:], 512, [[-32, 4], [0, 4], [-1, 32]], 0, 1.0, "RK")
+    iota(T.JG[:], [[1, 2], [0, 16]], 0, 0, ["JG"])
+    iota(T.JX[:], [[1, 168]], -39, 0, ["JX"])
     for k in range(4):
-        dma("s", T.T32[32 * k:32 * k + 32, :], T.tv[lo:lo + 32, :], [], ["T32%d" % k])
-    dma("y", T.X[lo:lo + 32, :], T.x[lo:lo + 32, :], [], ["X%d" % r])
-    iota(T.KI[:], [[0, 1]], 0, 1, ["KI"], False)
-    iota(T.J[:, 0:512], [[32, 4], [0, 4], [1, 32]], 0, 0, ["Ja"])
-    iota(T.JX[:], [[1, 256]], 0, 0, ["JX"])
-    send({d: T.XS[d] for d in others}, T.XL[r], T.sem["xa%d" % r], ["XS%d" % d for d in others])
-    iota(T.J[:, 512:1024], [[32, 4], [0, 4], [1, 32]], 128, 0, ["Jb"])
-    iota(T.J16[:], [[16, 8], [0, 16]], 0, 0, ["J16"])
-    near_first = sorted(others, key=lambda s: -inc[s])
-    for s in near_first:
+        iota(T.IV[32 * k:32 * k + 32, :], [[1, 256]], 16 + 256 * k, 0, ["IV%d" % k])
+    for j, s in enumerate(near + far):
         arrive("XL%d" % s, T.sem["xa%d" % s], inc[s])
-        dma("y", T.X[32 * s:32 * s + 32, :], T.XL[s], ["XL%d" % s], ["X%d" % s])
+        dma("y", [(T.X[32 * s:32 * s + 32, :], T.XL[s])], ["XL%d" % s], ["X%d" % s])
     XK = ["X%d" % s for s in range(4)]
 
-    sh, an = A.arith_shift_right, A.bitwise_and
-    for c, (s1, s2, o0, o1) in enumerate([(3, None, an, None), (2, None, sh, None), (4, None, sh, None), (4, 1, sh, an),
-                                          (31, None, an, None), (15, None, an, None), (5, None, sh, None), (127, None, an, None)]):
-        ts(T.KB[:, c:c + 1], T.KI[:], s1, s2, o0, o1, ["KI"], ["KB%d" % c])
-    cp(T.KF[:], T.KB[:], ["KB%d" % c for c in range(8)], ["KF"])
-    kf = [T.KF[:, c:c + 1] for c in range(8)]
-    kk = kf[7]
-    ks = [T.KS[:, c:c + 1] for c in range(16)]
-    mu, ad, eq = A.mult, A.add, A.is_equal
-    for c, (a, s1, s2, o0, o1) in enumerate([
-            (0, 32.0, kf[1], mu, ad), (2, 16.0, kk, mu, ad), (3, 16.0, 111.0, mu, ad), (4, 96.0, None, ad, None),
-            (3, 64.0, 15.0, mu, ad), (2, 16.0, 15.0, mu, ad), (2, 16.0, None, mu, None), (5, 0.0, None, eq, None),
-            (5, 1.0, None, eq, None), (5, 0.0, -2.0, eq, mu), (5, 1.0, -2.0, eq, mu), (5, 0.0, 128.0, eq, mu)]):
-        ts(ks[c], kf[a], s1, s2, o0, o1, ["KF"], ["K%d" % c])
-    ts(T.SA[:], T.J[:, 0:512], ks[0], None, eq, None, ["Ja", "K0"], ["SA"])
-    ts(ks[12], kf[6], 16.0, ks[4], mu, ad, ["KF", "K4"], ["K12"])
-    for t in range(2):
-        ts(T.SY[:, 144 * t:144 * t + 144], T.JX[:, 0:144], ks[5], ks[7 + t], eq, mu, ["JX", "K5", "K7", "K8"], ["SY%d" % t])
-    ts(T.I1[:], T.JX[:, 0:128], kk, None, eq, None, ["JX", "KF"], ["I1"])
-    ts(T.I16[:], T.JX[:, 0:128], kk, None, eq, None, ["JX", "KF"], ["I16"])
-    ts(T.RK[:], T.J[:, 0:512], kk, None, eq, None, ["Ja", "KF"], ["RK"])
+    op("v", lambda: g.vector.memset(T.SQ[:, 0:128], 0.0), [], ["SQp"])
+    op("v", lambda: g.vector.memset(T.HW[:, 0:16], 0.0), [], ["HWp"])
+    ts(T.KB[:, 0:1], T.KI[:], 4, 1, A.arith_shift_right, A.bitwise_and, ["KI"], ["KB0"])
+    ts(T.KB[:, 1:2], T.KI[:], 5, None, A.arith_shift_right, None, ["KI"], ["KB1"])
+    for j in range(16):
+        ts(T.BC[:, 128 * j:128 * j + 128], T.J16[:], float(j), None, eq, None, ["J16"], ["BC%d" % j])
+        if j == 0:
+            cp(T.KF[:, 0:2], T.KB[:], ["KB0", "KB1"], ["KF"])
+        if j == 2:
+            ts(T.KF[:, 2:3], T.KF[:, 1:2], 8.0, None, mu, None, ["KF"], ["KF2"])
+        if j == 4:
+            ts(T.KF[:, 3:4], T.KF[:, 0:1], 64.0, T.KF[:, 2:3], mu, ad, ["KF", "KF2"], ["KF3"])
 
     ts(T.A16[:], T.A32[:], -H, None, ad, None, ["A32"], ["A16"])
     for j in range(8):
         b, o = bank(j)
         mm(b[:, o:o + 288], T.SA[:, 128 * (j // 2):128 * (j // 2) + 128], T.A16[:, 288 * (j % 2):288 * (j % 2) + 288], True, True,
            ["SA", "A16"], BANKS[j])
-    for k in range(4):
-        for t in range(2):
-            cp(T.OL[32 * k:32 * k + 32, 32 * t:32 * t + 16], T.T32[32 * k:32 * k + 32, 64 * t + 16 * k:64 * t + 16 * k + 16],
-               ["T32%d" % k], ["OV%d%d" % (t, k)])
+    for t in range(2):
+        for h in range(2):
+            cp(T.OL[:, 32 * t + 8 * h:32 * t + 8 * h + 8], T.TQ[:, 64 * t + 32 * h:64 * t + 32 * h + 8], ["TQ"], ["OV%d%d" % (t, h)])
     for j in range(8):
         b, o = bank(j)
         if j % 2 == 0 or j == 1:
@@ -178,63 +178,21 @@ def rank_program(g, core, T, topo):
         else:
             cp(T.AW[:, 288 * j:288 * j + 288], b[:, o:o + 288], [BANKS[j]], ["AW%d" % j])
     AWK = ["AW%d" % j for j in range(8)]
-    for name, sc in (("IN", -1.0), ("I2", 2.0), ("IM2", -2.0), ("IP", 128.0), ("IM32", -32.0)):
+    for name, sc in (("IN", -1.0), ("I2", 2.0)):
         act(T[name][:], T.I1[:], F.Copy, ["I1"], [name], scale=sc)
+    act(T.SQ[:, 384:640], T.SQ[:, 128:384], F.Copy, ["SQ0"], ["SQ1"])
+    act(T.SQ[:, 640:1152], T.SQ[:, 128:640], F.Copy, ["SQ0", "SQ1"], ["SQ2"])
+    for name in ("IM", "RM"):
+        act(T[name][:], T.AW[:], F.Copy, AWK, [name], scale=0.0)
     for t in range(2):
-        act(T["RM%d" % t][:], T.AW[:], F.Copy, AWK, ["RM%d" % t], scale=0.0)
-    for t in range(2):
-        cp(T.CV[:, 256 * t:256 * t + 256], T.AW[:].indirect(T.OL[:, 32 * t:32 * t + 16]), AWK + ["OV%d%d" % (t, k) for k in range(4)], ["CV%d" % t])
+        cp(T.CV[:, 256 * t:256 * t + 256], T.AW[:].indirect(T.OL[:, 32 * t:32 * t + 16]), AWK + ["OV%d0" % t, "OV%d1" % t], ["CV%d" % t])
         bk = "M%d" % t
         for p in range(16):
             mm(T[bk][:, 0:16], T.SY[:, 144 * t + 15 - p:144 * t + 143 - p], T.CV[:, 256 * t + p:256 * t + 256:16], p == 0, p == 15,
-               ["SY%d" % t, "CV%d" % t], bk)
-    cp(T.VL[:], T.T32[:], ["T32%d" % k for k in range(4)], ["VL"])
+               ["SY", "CV%d" % t], bk)
     for t in range(2):
         ts(T.OL[:, 32 * t + 16:32 * t + 32], T["M%d" % t][:, 0:16], H, None, ad, None, ["M%d" % t], ["OY%d" % t])
-        cp(T.YO[:, 16 * t:16 * t + 16], T["M%d" % t][:, 0:16], ["M%d" % t], ["YO%d" % t])
-    for t in range(2):
-        for k in range(4):
-            mm(T.A0[:, 64 * t + 16 * k:64 * t + 16 * k + 16], T.RK[:, 128 * k:128 * k + 128], T.YO[:, 16 * t:16 * t + 16], True, True,
-               ["RK", "YO%d" % t], "A0")
-    cp(T.CY[:, 0:256], T.AW[:].indirect(T.OL[:, 16:32]), AWK + ["OY0"], ["CY0"])
-    ts(T.YL[:], T.A0[:, 0:128], H, None, ad, None, ["A0"], ["YL"])
-    cp(T.CY[:, 256:512], T.AW[:].indirect(T.OL[:, 48:64]), AWK + ["OY1"], ["CY1"])
-    for t in range(2):
-        for h in range(2):
-            for k in range(4):
-                mm(T.M1[:, 8 * t + 2 * k + h:512:16], T.CY[:, 256 * t + 128 * h:256 * t + 128 * h + 128], T.I16[:, 32 * k:32 * k + 32], True, True,
-                   ["CY%d" % t, "I16"], "M1")
-    ts(T.SQ[:, 0:1024], T.J[:], ks[1], None, eq, None, ["Ja", "Jb", "K1"], ["SQ0"])
-    cp(T.T1[:], T.M1[:], ["M1"], ["T1"])
-    ts(T.SQ[:, 1024:2048], T.J[:], -16.0, ks[1], ad, eq, ["Ja", "Jb", "K1"], ["SQ1"])
-    for q in range(8):
-        bk = BANKS[4 + q // 2]
-        for gr in range(2):
-            mm(T[bk][:, 256 * (q % 2):256 * (q % 2) + 256], T.SQ[:, 1024 * gr + 128 * q:1024 * gr + 128 * q + 128], T.T1[:, 256 * gr:256 * gr + 256],
-               gr == 0, gr == 1, ["SQ0", "SQ1", "T1"], bk)
-
-    def bc(j):
-        ts(T.BC[:, 128 * j:128 * j + 128], T.J16[:], float(j), kk, ad, eq, ["J16", "KF"], ["BC%d" % j])
-    for j in range(4):
-        bc(j)
-    for q in range(8):
-        bk = BANKS[4 + q // 2]
-        ts(T.ZL[:, q:2048:8], T[bk][:, 256 * (q % 2):256 * (q % 2) + 256], H, float(V - 1), ad, A.min, [bk], ["ZL%d" % q])
-    ZK = ["ZL%d" % q for q in range(8)]
-
-    def ends(t):
-        for c, (out, lst) in enumerate(((T.HV, "VL"), (T.HY, "YL"))):
-            act(out[:, 1024 * t:1024 * t + 1024], T.X[:].indirect(T[lst][:, 64 * t:64 * t + 64]), F.Copy, XK + [lst], ["H%d%d" % (t, c)], scale=0.5)
-
-    def middle(t, j):
-        wn, out, f = (("I1", "M", F.Copy), ("IN", "R", F.Abs))[j]
-        for h in range(2):
-            b, o = bank(2 * j + h)
-            c = 1024 * t + 512 * h
-            mm(b[:, o:o + 512], T.I1[:], T.HV[:, c:c + 512], True, False, ["I1", "H%d0" % t], BANKS[2 * j + h])
-            mm(b[:, o:o + 512], T[wn][:], T.HY[:, c:c + 512], False, True, [wn, "H%d1" % t], BANKS[2 * j + h])
-        act(T[out][:, 1024 * t:1024 * t + 1024], T["PB%d" % j][:], f, ["PB%da" % j, "PB%db" % j], ["%s%d" % (out + out, t)])
-
+        cp(T.CY[:, 256 * t:256 * t + 256], T.AW[:].indirect(T.OL[:, 32 * t + 16:32 * t + 32]), AWK + ["OY%d" % t], ["CY%d" % t])
     CK = ["CY0", "CY1"]
 
     def spread(n):
@@ -251,174 +209,284 @@ def rank_program(g, core, T, topo):
         bk = "M%d" % (n % 2)
         out, key = (T.EV[:], "EV") if n == 0 else (T.EQ[:, 512 * (n % 2):512 * (n % 2) + 512], "EQ%d" % (n % 2))
         tt(out, T[bk][:], T.CY[:], eq, [bk] + CK, [key])
-        if n + 4 < 16:
-            bc(n + 4)
         if n + 2 < 16:
             spread(n + 2)
-        wn = "IM32" if n == 0 else "I1" if n == 1 else "I2"
-        mm(T.A1[:], T[wn][:], out, False, n == 15, [wn, key], "A1")
+        if n > 0:
+            wn = "I1" if n == 1 else "I2"
+            mm(T.WB[:], T[wn][:], out, False, n == 15, [wn, key], "WB")
 
-    ts(T.EN[:], T.CY[:], H, None, eq, None, CK, ["EN"])
+    for t in range(2):
+        for h in range(2):
+            for k in range(4):
+                mm(T.AT[:, 8 * t + 4 * h + k:512:16], T.CY[:, 256 * t + 128 * h:256 * t + 128 * h + 128], T.I1[:, 32 * k:32 * k + 32], True, True,
+                   ["CY%d" % t, "I1"], "AT")
+    for t in range(2):
+        cp(T.YO[:, 16 * t:16 * t + 16], T["M%d" % t][:, 0:16], ["M%d" % t], ["YO%d" % t])
     spread(0)
     spread(1)
-    mm(T.A1[:], T.IM32[:], T.EN[:], True, False, ["IM32", "EN"], "A1")
-    ends(0)
-    for n in range(PRE):
-        match(n)
-        for j in range(2):
-            if n == MID[j]:
-                middle(0, j)
-    ends(1)
-    ts(T.WS[:], T.JX[:, 0:240], ks[2], None, eq, None, ["JX", "K2"], ["WS"])
+    cp(T.T1[:], T.AT[:], ["AT"], ["T1"])
+    ts(T.EN[:], T.CY[:], H, 64.0, eq, mu, CK, ["EN"])
+    cp(T.VL[:], T.T32[:], ["T32"], ["VL"])
+    mm(T.WB[:], T.IN[:], T.EN[:], True, False, ["IN", "EN"], "WB")
+    SQK = ["SQp"] + ["SQ%d" % k for k in range(3)]
+    for j in range(4):
+        b, o = bank(j)
+        for q in range(8):
+            for gr in range(2):
+                c = 128 * (1 - gr) + q
+                mm(b[:, o + q:o + 512:8], T.SQ[:, c:c + 1017:8], T.T1[:, 256 * gr + 64 * j:256 * gr + 64 * j + 64], gr == 0, gr == 1,
+                   SQK + ["T1"], BANKS[j])
+        if j < 2:
+            match(j)
+    for c in range(4):
+        for k in range(4):
+            mm(T.AT[:, 32 * c + 8 * k:32 * c + 8 * k + 8], T.RK[:, 128 * k:128 * k + 128], T.YO[:, 8 * c:8 * c + 8], True, True,
+               ["RK", "YO%d" % (c // 2)], "AT")
+    for j in range(2):
+        ts(T.ZL[:, 1024 * j:1024 * j + 1024], T["PB%d" % j][:], H, float(V - 1), ad, A.min, ["PB%da" % j, "PB%db" % j], ["ZL%d" % j])
+    ts(T.YL[:], T.AT[:, 0:128], H, None, ad, None, ["AT"], ["YL"])
+    mm(T.AT[:], T.ZR[:, 0:128], T.ZR[:], True, True, ["ZR"], "AT")
+
+    def end(t, c):
+        out, lst = ((T.HV, "VL"), (T.HY, "YL"))[c]
+        act(out[:, 1024 * t:1024 * t + 1024], T.X[:].indirect(T[lst][:, 64 * t:64 * t + 64]), F.Copy, XK + [lst], ["H%d%d" % (t, c)], scale=0.5)
+
+    def middle(t, j, h, bk):
+        c = 1024 * t + 512 * h
+        b, o = bank(BANKS.index(bk))
+        terms = [("I1", T.HV, "H%d0" % t), ("IN", T.HY, "H%d1" % t)] if j == 0 else \
+                [("I1", T.HV, "H%d0" % t), ("I1", T.HY, "H%d1" % t), ("IN", T.R, "R%d%d" % (t, h))]
+        for m, (wn, src, key) in enumerate(terms):
+            mm(b[:, o:o + 512], T[wn][:], src[:, c:c + 512], m == 0, m == len(terms) - 1, [wn, key], bk)
+        out, f = (("R", F.Abs), ("LO", F.Copy))[j]
+        act(T[out][:, c:c + 512], b[:, o:o + 512], f, [bk], ["%s%d%d" % (out, t, h)])
+
+    def dist(t):
+        c = 1024 * t
+        ts(T.DL[:, c:c + 1024], T.R[:, c:c + 1024], 4.0, 1.0, mu, A.max, ["R%d0" % t, "R%d1" % t], ["DL%d" % t])
+
+    def merge(name):
+        dma("y", [(T[name][16 * gr + k:128:32, :], T[name][32 * k + 16 * gr + 8:32 * k + 16 * gr + 12, :]) for k in range(4) for gr in range(2)],
+            [name], [name])
+
+    def index_out():
+        for c in range(2):
+            cp(T.IM[:].indirect(T.OL[:, 32 + 16 * c:48 + 16 * c]), T.IV[:], ["IM", "OV10", "OV11", "OY1"] + ["IV%d" % k for k in range(4)], ["IM"])
+        merge("IM")
+
+    def index_in():
+        cp(T.IG[:], T.IM[:].indirect(T.OL[:, 0:32]), ["IM", "OY0"], ["IG"])
+        for p in range(16):
+            mm(T.M0[:, 0:32], T.SY4[:, 15 - p:143 - p], T.IG[:, p:512:16], p == 0, p == 15, ["SY4", "IG"], "M0")
 
     def late():
-        ts(T.OG[:], T.J16[:], ks[6], None, eq, None, ["J16", "K6"], ["OG"])
-        ts(T.OG16[:], T.J16[:], ks[6], None, eq, None, ["J16", "K6"], ["OG16"])
-        ts(T.TR[:], T.JX[:, 0:128], kk, -1.0, A.is_ge, mu, ["JX", "KF"], ["TR"])
-        ts(T.NI16[:], T.JX[:, 0:128], kk, -1.0, eq, mu, ["JX", "KF"], ["NI16"])
-        ts(T.WD[:], T.JX[:, 0:144], ks[12], None, eq, None, ["JX", "K12"], ["WD"])
-        ts(T.WDM[:], T.JX[:, 0:144], ks[12], -H, eq, mu, ["JX", "K12"], ["WDM"])
-        ts(T.WR[:], T.JX[:, 0:224], ks[3], -1.0, eq, mu, ["JX", "K3"], ["WR"])
-        for name, c in (("WY0", 9), ("WY1", 10), ("WYP", 11)):
-            ts(T[name][:], T.JX[:, 0:224], ks[3], ks[c], eq, mu, ["JX", "K3", "K%d" % c], [name])
-        tt(T.TR[:], T.TR[:], T.OG[:], mu, ["TR", "OG"], ["TR"])
+        grp, turn = [[-16, 8], [0, 16]], [[-16, 2], [0, 16], [-32, 4]]
+        row = [[-16, 2], [128, 16], [-32, 4]]
+        return [
+            lambda: band(T.SY4[:], 144, [[-16, 9], [128, 16]], -128 * 15, 4, 1.0, "SY4"),
+            lambda: band(T.OG[:], 128, grp, 0, 16, 1.0, "OG"),
+            lambda: (band(T.TR[:], 128, grp, 0, 16, 4096.0, "TR"),
+                     op("g", lambda: g.affine_select(T.TR[:], T.TR[:], [[1, 128]], ge, 0.0, 0, -1), ["TR"], ["TR"]),
+                     op("g", lambda: g.affine_select(T.TR[:], T.TR[:], [[1, 128]], ne, -4096.0, 0, -1), ["TR"], ["TR"])),
+            lambda: (mark(T.PM[:], 128, [[-16, 2], [-1, 16], [-32, 4]], 0, 1.0, "PM"),
+                     band(T.MY[:], 128, [[-16, 8], [128, 16]], 0, 4, 1.0, "MY")),
+            lambda: (band(T.RV0[:], 128, turn, 0, 4, -0.5, "RV0"), band(T.RY0[:], 128, row, 0, 4, -1.0, "RY0")),
+            lambda: (mark(T.RV1[:], 128, turn, 0, -0.5, "RV1"), mark(T.RY1[:], 128, row, -128, -1.0, "RY1")),
+        ]
 
-    def removed(bk, c0, wn, src, t, last):
-        for k in range(4):
-            mm(T[bk][:, c0:c0 + 256], T[wn][:, 96 - 32 * k:224 - 32 * k], T[src][:, 1024 * t + 256 * k:1024 * t + 256 * k + 256], False,
-               last and k == 3, [wn, src + str(t)], bk)
+    def reg(bk, n):
+        b, o = bank(BANKS.index(bk))
+        return b[:, o:o + n]
 
-    def end_steps(t):
-        o, c = 1 - t, 256 * t
-        at, rm, ht = "A%d" % t, T["RM%d" % t], T.HT[:, 512 * t:512 * t + 512]
+    def half(bk, h):
+        b, o = bank(BANKS.index(bk))
+        return b[:, o + 128 * h:o + 128 * h + 128]
 
-        def s0():
-            act(T.AB[:], T[at][:, 0:256], F.Abs, [at], ["AB"])
-            ts(T.OK[:], T.AB[:], 6.0, None, A.is_le, None, ["AB"], ["OK"])
-            for h in range(2):
-                mm(T.M0[:, 256 * h:256 * h + 256], T.OG[:], T.OK[:], True, True, ["OG", "OK"], "M0")
-            mm(T.M1[:, 0:256], T.I2[:], T.OK[:], True, False, ["I2", "OK"], "M1")
-            mm(T.M1[:, 0:256], T.TR[:], T.OK[:], False, True, ["TR", "OK"], "M1")
-
-        def s1():
-            act(ht, T.M0[:], F.Sign, ["M0"], ["HT%d" % t])
-            act(T.FI[:], T.M1[:, 0:256], F.Relu, ["M1"], ["FI"])
-
-        def s2():
-            cp(rm[:].indirect(T.OL[:, 32 * t:32 * t + 32]), ht, ["HT%d" % t, "OY%d" % t, "RM%d" % t], ["RM%d" % t])
-            tt(T.PR[:], T.FI[:], T.CY[:, c:c + 256], mu, ["FI"] + CK, ["PR"])
-            mm(T.M0[:, 0:256], T.OG16[:], T.PR[:], True, False, ["OG16", "PR"], "M0")
-            mm(T.M0[:, 0:256], T.NI16[:], T.CY[:, c:c + 256], False, True, ["NI16"] + CK, "M0")
-            for i in range(16):
-                mm(T.M1[:, 0:16], T.WD[:, 15 - i:143 - i], T.PR[:, 16 * i:16 * i + 16], i == 0, False, ["WD", "PR"], "M1")
-                mm(T.M1[:, 0:16], T.WDM[:, 15 - i:143 - i], T.FI[:, 16 * i:16 * i + 16], False, i == 15, ["WDM", "FI"], "M1")
-
-        def s3():
-            act(T.RY[:, 1024 * t:1024 * t + 1024], rm[:].indirect(T.YL[:, 64 * o:64 * o + 64]), F.Copy, ["RM%d" % t, "YL"], ["RY%d" % t])
-            cp(T.RV[:, 1024 * t:1024 * t + 1024], rm[:].indirect(T.VL[:, 64 * o:64 * o + 64]), ["RM%d" % t, "VL"], ["RV%d" % t])
-            act(T["SP%d" % t][:], T.M1[:, 0:16], F.Identity, ["M1"], ["SP%d" % t], bias=float(V))
-            ts(T.ES[:, c:c + 256], T.M0[:, 0:256], 0.0, None, eq, None, ["M0"], ["ES%d" % t])
-            sd = T["SD%d" % t]
-            send({d: T["SP%d" % t][:] for d in others}, sd[r], T.sem["sa%d" % t], ["SP%d" % t])
-            dma("y", sd[r], T["SP%d" % t][:], ["SP%d" % t], ["SO%d" % t])
-            arrive("SR%d" % t, T.sem["sa%d" % t], sum(inc.values()))
-
-        return [s0, s1, s2, s3]
-
-    def score(t, bk):
+    def masked(t, bm):
         c = 256 * t
-        mm(T[bk][:, 256:512], T.I1[:], T.W[:, c:c + 256], True, False, ["I1", "W"], bk)
-        mm(T[bk][:, 256:512], T.I2[:], T.HT[:, 512 * t:512 * t + 256], False, False, ["I2", "HT%d" % t], bk)
+        mm(reg(bm, 256), T.I1[:], T.EV[:, c:c + 256], True, False, ["I1", "EV"], bm)
+        mm(reg(bm, 256), T.I1[:], T.EN[:, c:c + 256], False, False, ["I1", "EN"], bm)
+        if t == 1:
+            mm(reg(bm, 256), T.MY[:], T.RG0[:, 256:512], False, False, ["MY", "RG0"], bm)
+
+    def sums_in(t, bm):
+        act(T.AB[:], T.AT[:, 256 * t:256 * t + 256], F.Abs, ["AT"], ["AB"], bias=0.5, scale=1.0 / 128)
+        for h in range(2):
+            mm(half(bm, h), T.AB[:, 128 * h:128 * h + 128], T.I1[:], False, h == 1, ["AB", "I1"], bm)
+        ts(T.OK[:], reg(bm, 256), 6.5 / 128, None, A.is_le, None, [bm], ["OK"])
+
+    def column(t, bk, wn):
+        mm(reg(bk, 256), T[wn][:], T.CY[:, 256 * t:256 * t + 256], True, False, [wn] + CK, bk)
+
+    def first(t, bp):
+        mm(reg(bp, 256), T.TR[:], T.OK[:], False, True, ["TR", "OK"], bp)
+        ts(T.PR[:], reg(bp, 256), 4096.0, H, ad, A.min, [bp], ["PR"])
+
+    def hit(t, bh):
+        b, o = bank(BANKS.index(bh))
+        for h in range(2 - t):
+            mm(b[:, o + 256 * h:o + 256 * h + 256], T.OG[:], T.OK[:], True, True, ["OG", "OK"], bh)
+        act(T["HT%d" % t][:], reg(bh, 512 - 256 * t), F.Sign, [bh], ["HT%d" % t])
+
+    def same(t, bb):
+        mm(reg(bb, 256), T.OG[:], T.PR[:], False, True, ["OG", "PR"], bb)
+        ts(T.ES[:, 256 * t:256 * t + 256], reg(bb, 256), 15 * H, -1.0, eq, mu, [bb], ["ES%d" % t])
+
+    def seps(t, bs):
+        for j in range(16):
+            x0 = 39 - 32 * (j // 8) - j % 8
+            mm(reg(bs, 16), T.WD[:, x0:x0 + 128], T.PR[:, 16 * j:16 * j + 16], j == 0, j == 15, ["WD", "PR"], bs)
+        sp, sd = T["SP%d" % t], T["SD%d" % t]
+        act(sp[:], reg(bs, 16), F.Identity, [bs], ["SP%d" % t], bias=-14 * H)
+        send(others, {d: sp[:] for d in others}, sd[r], T.sem["sa%d" % t], ["SP%d" % t])
+        dma("y", [(sd[r], sp[:])], ["SP%d" % t], ["SO%d" % t])
+        arrive("SR%d" % t, T.sem["sa%d" % t], sum(inc.values()))
 
     def sep_out(t):
-        dma("y", T.ysep[:, 1024 * t:1024 * t + 1024], T["SD%d" % t][:], ["SO%d" % t, "SR%d" % t], ["ys%d" % t])
+        dma("y", [(T.ysep[:, 1024 * t:1024 * t + 1024], T["SD%d" % t][:])], ["SO%d" % t, "SR%d" % t], ["ys%d" % t])
+
+    def score(bk, terms, st, sp):
+        for m, (wn, src, c, key) in enumerate(terms):
+            mm(reg(bk, 256), T[wn][:], T[src][:, c:c + 256], st and m == 0, sp and m == len(terms) - 1, [wn, key], bk)
 
     chunks = [(t, i) for t in range(2) for i in range(16) if i != t]
+    own = [n for n in range(30) if n not in SCAL]
+
+    def diff(n):
+        if n in SCAL:
+            c = 1024 * SCAL.index(n)
+            return T.UK, c, "UK%d" % n
+        return T.U, 1024 * (own.index(n) % NU), "U%d" % (own.index(n) % NU)
 
     def gather(n):
         t, i = chunks[n]
-        c = 1024 * (n % NB)
-        tt(T.U[:, c:c + 1024], T.X[:].indirect(T.ZL[:, 128 * i + 64 * t:128 * i + 64 * t + 64]), T.M[:, 1024 * t:1024 * t + 1024], A.subtract,
-           XK + ZK + ["MM%d" % t], ["U%d" % (n % NB)])
-        if n in VRELU:
-            ts(T.U2[:, c:c + 1024], T.U[:, c:c + 1024], 0.0, 2.0, A.max, mu, ["U%d" % (n % NB)], ["UR%d" % (n % NB)])
+        u, c, key = diff(n)
+        z, low = T.X[:].indirect(T.ZL[:, 128 * i + 64 * t:128 * i + 64 * t + 64]), T.LO[:, 1024 * t:1024 * t + 1024]
+        lk = ["LO%d0" % t, "LO%d1" % t]
+        if n in SCAL:
+            act(u[:, c:c + 1024], z, F.Copy, XK + ["ZL%d" % (i // 8)], [key], scale=-1.0)
+            op("g", lambda: [g.dma_start(u[:, c:c + 1024], low, accum_op=ad)], [key] + lk, [key], "d")
+        else:
+            tt(u[:, c:c + 1024], z, low, A.subtract, XK + ["ZL%d" % (i // 8)] + lk, [key])
+
+    def clamp(n):
+        u, c, key = diff(n)
+        ts(T.C[:, 1024 * (n % NC):1024 * (n % NC) + 1024], u[:, c:c + 1024], -1.0, 1.0, A.max, A.min, [key], ["C%d" % (n % NC)])
 
     def fold(n):
         t, i = chunks[n]
-        key, c = "U%d" % (n % NB), 1024 * (n % NB)
-        terms = [("I1", T.U, c, key), ("IN", T.R, 1024 * t, "RR%d" % t)]
-        if n in VRELU:
-            terms = [("I1", T.U2, c, "UR%d" % (n % NB)), ("IN", T.U, c, key)] + terms[1:]
-        else:
-            act(T.U[:, c:c + 1024], T.U[:, c:c + 1024], F.Abs, [key], [key])
-        for j, (wn, src, c0, k) in enumerate(terms):
-            for h in range(2):
-                b, o = bank(2 * (n % 2) + h)
-                mm(b[:, o:o + 512], T[wn][:], src[:, c0 + 512 * h:c0 + 512 * h + 512], j == 0, j == len(terms) - 1, [wn, k], BANKS[2 * (n % 2) + h])
+        u, c, key = diff(n)
+        wn = "I1" if n in SCAL else "IN"
+        for h in range(2):
+            b, o = bank(2 * (n % 2) + h)
+            mm(b[:, o:o + 512], T.I2[:], u[:, c + 512 * h:c + 512 * h + 512], True, False, ["I2", key], BANKS[2 * (n % 2) + h])
+            mm(b[:, o:o + 512], T[wn][:], T.DL[:, 1024 * t + 512 * h:1024 * t + 512 * h + 512], False, True, [wn, "DL%d" % t], BANKS[2 * (n % 2) + h])
 
-    def total(n):
-        t, i = chunks[n]
-        at, key, pb, c = "A%d" % t, "SG%d" % (n % 2), "PB%d" % (n % 2), 1024 * (n % 2)
+    def sign(n):
+        pb = "PB%d" % (n % 2)
+        c, key = 1024 * (n % NS), "SG%d" % (n % NS)
         if n in SPLIT:
             act(T.SG[:, c:c + 512], T[pb][:, 0:512], F.Sign, [pb + "a"], [key + "a"])
             ts(T.SG[:, c + 512:c + 1024], T[pb][:, 512:1024], -1.0, 1.0, A.max, A.min, [pb + "b"], [key + "b"])
-        elif n in VSIGN:
-            ts(T.SG[:, c:c + 1024], T[pb][:], -1.0, 1.0, A.max, A.min, [pb + "a", pb + "b"], [key + "a", key + "b"])
         else:
             act(T.SG[:, c:c + 1024], T[pb][:], F.Sign, [pb + "a", pb + "b"], [key + "a", key + "b"])
-        if n % 15 == 0:
-            mm(T[at][:, 0:256], T.IP[:], T.EV[:, 256 * t:256 * t + 256], True, False, ["IP", "EV"], at)
-            mm(T[at][:, 0:256], T.IP[:], T.EN[:, 256 * t:256 * t + 256], False, False, ["IP", "EN"], at)
-        for k in range(4):
-            x0 = 111 - 32 * k - i
-            mm(T[at][:, 0:256], T.WS[:, x0:x0 + 128], T.SG[:, c + 256 * k:c + 256 * k + 256], False, n % 15 == 14 and k == 3,
-               ["WS", key + "ab"[k // 2]], at)
 
-    e0 = end_steps(0)
-    for n in range(NB - 1):
-        gather(n)
-    middle(1, 0)
-    middle(1, 1)
+    def total(n):
+        t, i = chunks[n]
+        pos, neg = T.GG[:, 0:17:16], T.NG[:, 0:17:16]
+        ws, wc = (neg, pos) if n in SCAL else (pos, neg)
+        for b in range(8):
+            c = 256 * t + 32 * b + i
+            s0, c0 = 1024 * (n % NS) + 128 * b, 1024 * (n % NC) + 128 * b
+            mm(T.AT[:, c:c + 17:16], T.C[:, c0:c0 + 128], wc, True, False, ["C%d" % (n % NC), "GG", "NG"], "AT")
+            mm(T.AT[:, c:c + 17:16], T.SG[:, s0:s0 + 128], ws, False, True, ["SG%d%s" % (n % NS, "ab"[b // 4]), "GG", "NG"], "AT")
+
+    for step in late():
+        step()
+    end(0, 0)
+    end(0, 1)
+    for n in range(2, PRE):
+        match(n)
+        if n == 4:
+            ts(T.GG[:], T.JG[:], T.KF[:, 0:1], None, eq, None, ["JG", "KF"], ["GG"])
+            ts(T.NG[:], T.JG[:], T.KF[:, 0:1], -1.0, eq, mu, ["JG", "KF"], ["NG"])
+            ts(T.WD[:], T.JX[:], T.KF[:, 3:4], None, eq, None, ["JX", "KF3"], ["WD"])
+        if n == IDX:
+            index_out()
+        for j in range(2):
+            if n == MID[j]:
+                for h in range(2):
+                    middle(0, j, h, BANKS[2 * j + h])
+    for n in range(AHEAD):
+        if n in SCAL:
+            gather(n)
+    gather(0)
+    dist(0)
     fold(0)
+    for n in range(1, LEAD):
+        if n in own:
+            gather(n)
+    clamp(0)
+
+    steps = {
+        1: [lambda: end(1, 0)],
+        2: [lambda: ts(T.W[:], T.WB[:], 0.5, 1.0, mu, A.min, ["WB"], ["W"])],
+        3: [index_in, lambda: end(1, 1)],
+        5: [lambda: middle(1, 0, 0, "M1"), lambda: middle(1, 0, 1, "WB"), lambda: cp(T.ML[:], T.M0[:, 0:32], ["M0"], ["ML"])],
+        7: [lambda: middle(1, 1, 0, "M1"), lambda: middle(1, 1, 1, "WB"), lambda: dist(1)],
+        10: [lambda: [band(T.GK[:, 128 * k:128 * k + 128], 128, [[0, 4], [-16, 2], [0, 16]], -32 * k, 16, 1.0, "GK%d" % k) for k in range(4)]],
+        13: [lambda: masked(0, "M0"), lambda: column(0, "M1", "I1")],
+        15: [lambda: sums_in(0, "M0")],
+        16: [lambda: first(0, "M1"), lambda: hit(0, "WB"), lambda: column(0, "M0", "IN")],
+        17: [lambda: same(0, "M0"), lambda: seps(0, "M1"),
+             lambda: cp(T.RM[:].indirect(T.OL[:, 0:32]), T.HT0[:], ["HT0", "RM", "OY0"], ["RM"]), lambda: merge("RM")],
+        22: [lambda: act(T.RG0[:], T.RM[:].indirect(T.OL[:, 32:64]), F.Copy, ["RM", "OY1"], ["RG0"]), lambda: sep_out(0)],
+        25: [lambda: masked(1, "M0"),
+             lambda: score("WB", [("PM", "W", 0, "W"), ("PM", "HT0", 0, "HT0"), ("PM", "ES", 0, "ES0")], True, False),
+             lambda: score("M1", [("PM", "W", 256, "W"), ("RV0", "RG0", 0, "RG0"), ("RY0", "RG0", 256, "RG0")], True, False)],
+    }
     for n in range(30):
-        if n + NB - 1 < 30:
-            gather(n + NB - 1)
+        if n + AHEAD in SCAL:
+            gather(n + AHEAD)
         if n + 1 < 30:
             fold(n + 1)
-        total(n)
+        if n + LEAD in own:
+            gather(n + LEAD)
+        if n + 1 < 30:
+            clamp(n + 1)
+        sign(n)
         if PRE + n < 16:
             match(PRE + n)
-        if PRE + n == 16:
-            ts(T.W[:], T.A1[:], 2.0, None, A.min, None, ["A1"], ["W"])
-        if n == 8:
-            late()
-        if 15 <= n < 19:
-            e0[n - 15]()
-        if n == 21:
-            removed("A1", 0, "WYP", "RY", 0, False)
-            score(0, "A0")
-            mm(T.A0[:, 256:512], T.IM2[:], T.ES[:, 0:256], False, False, ["IM2", "ES0"], "A0")
-            sep_out(0)
-    e1 = end_steps(1)
-    e1[0]()
-    e1[1]()
-    score(1, "A1")
-    removed("A1", 256, "WR", "RV", 0, False)
-    removed("A1", 256, "WY0", "RY", 0, False)
-    e1[2]()
-    e1[3]()
-    removed("A0", 256, "WY1", "RY", 1, False)
-    removed("A0", 256, "WR", "RV", 1, True)
-    mm(T.A1[:, 256:512], T.IM2[:], T.ES[:, 256:512], False, True, ["IM2", "ES1"], "A1")
-    for t in range(2):
-        ts(T["FL%d" % t][:], T["A%d" % t][:, 256:512], 3.0, None, A.is_ge, None, ["A%d" % t], ["FL%d" % t])
-    send({d: T["FL%d" % (d // 2)][:] for d in others}, T.FD[r], T.sem.fa, ["FL0", "FL1"])
-    dma("s", T.FD[r], T["FL%d" % (r // 2)][:], ["FL%d" % (r // 2)], ["FO"])
+        for step in steps.get(n, []):
+            step()
+        if n == 29:
+            column(1, "PB0a", "I1")
+            column(1, "PB0b", "IN")
+        total(n)
+
+    sums_in(1, "M0")
+    for k in range(4):
+        mm(T.PB1[:, 256 * k:256 * k + 256], T.GK[:, 128 * k:128 * k + 128], T.OK[:], True, True, ["GK%d" % k, "OK"], BANKS[2 + k // 2])
+        if k == 1:
+            first(1, "PB0a")
+    act(T.HW[:, 16:528], T.PB1[:, 0:512], F.Sign, ["PB1a"], ["HWa"])
+    ts(T.HW[:, 528:1040], T.PB1[:, 512:1024], 1.0, None, A.min, None, ["PB1b"], ["HWb"])
+    hit(1, "AT")
+    same(1, "PB0b")
+    HK = ["HWp", "HWa", "HWb", "ML"]
+    act(T.RG1[:, 256:512], T.HW[:].indirect(T.ML[:, 16:32]), F.Copy, HK, ["RG1y"])
+    cp(T.RG1[:, 0:256], T.HW[:].indirect(T.ML[:, 0:16]), HK, ["RG1v"])
+    seps(1, "M0")
+    score("M1", [("PM", "HT1", 0, "HT1"), ("PM", "ES", 256, "ES1")], False, True)
+    score("WB", [("RY1", "RG1", 256, "RG1y"), ("RV1", "RG1", 0, "RG1v")], False, True)
+    ts(T.FL[:, 256:512], T.M1[:, 0:256], 1.25, None, ge, None, ["M1"], ["FL1"])
+    ts(T.FL[:, 0:256], T.WB[:, 0:256], 1.25, None, ge, None, ["WB"], ["FL0"])
+    send(others, {d: T.FL[:, 128 * d:128 * d + 128] for d in others}, T.FD[r], T.sem["fa%d" % r], ["FL0", "FL1"])
+    dma("s", [(T.yflag[lo:lo + 32, :], T.FL[:, 128 * r:128 * r + 128])], ["FL%d" % (r // 2)], ["yf%d" % r])
     sep_out(1)
-    arrive("FR", T.sem.fa, sum(inc.values()))
-    for h in range(2):
-        p0 = 64 * (r % 2) + 32 * h
-        dma("y" if h == 0 else "s", T.yflag[:, 256 * h:256 * h + 256], T.FD[:, p0:p0 + 32, :], ["FO", "FR"], ["yf%d" % h])
+    for j, s in enumerate(near + far):
+        arrive("FR%d" % s, T.sem["fa%d" % s], inc[s])
+        dma("ys"[j % 2], [(T.yflag[32 * s:32 * s + 32, :], T.FD[s])], ["FR%d" % s], ["yf%d" % s])
 
     wrote, read, deps = {}, {}, []
     for n, o in enumerate(ops):
@@ -447,7 +515,7 @@ def rank_program(g, core, T, topo):
     marked = set(m for d in deps for m in d)
     queue = {"v": g.vector, "s": g.scalar, "p": g.tensor, "g": g, "y": g.sync}
     esem = {"v": "ev", "s": "es", "p": "ep", "g": "eg"}
-    count, sig, seen, nd, total_sent, dsems = {}, {}, {}, [0], [0], []
+    count, sig, seen, dsems = {}, {}, {}, []
     for n, o in enumerate(ops):
         if o["kind"] == "x":
             sig[n] = (o["sem"], o["n"], "x%d" % n)
@@ -459,19 +527,17 @@ def rank_program(g, core, T, topo):
                 seen[(o["q"], name)] = val
         ins = o["fn"]()
         if o["kind"] == "d":
-            name = "d%d" % nd[0]
-            nd[0] += 1
-            ins.then_inc(T.sem[name], 16)
-            sig[n] = (T.sem[name], 16, name)
-            dsems.append(name)
-        elif o["kind"] == "r":
-            total_sent[0] += sum(len(e) for e in eng.values())
+            name = "d%d" % len(dsems)
+            for one in ins:
+                one.then_inc(T.sem[name], 16)
+            sig[n] = (T.sem[name], 16 * len(ins), name)
+            dsems.append(sig[n])
         elif n in marked:
             name = esem[o["q"]]
             count[name] = count.get(name, 0) + 1
             ins.then_inc(T.sem[name], 1)
             sig[n] = (T.sem[name], count[name], name)
-    g.wait_ge(T.sem.sent, total_sent[0])
-    for name in dsems:
+    g.wait_ge(T.sem.sent, sent[0])
+    for sem, val, name in dsems:
         if not any(k[1] == name for k in seen):
-            g.sync.wait_ge(T.sem[name], 16)
+            g.sync.wait_ge(sem, val)

@@ -2,11 +2,15 @@ from concourse.bass import DstId, RemoteDMATransfer
 from concourse.mybir import AluOpType as A, ActivationFunctionType as F
 
 V, H = 2304, 1152.0
-NU, NC, NS, NK = 6, 4, 4, 14
-SCAL = (4, 6, 9, 12, 16, 19, 22, 25, 28)
+NU, NC, NS, NK = 8, 8, 6, 16
+SCAL = tuple(range(3, 28, 2))
+ADDED = (4, 10, 18, 24)
 SPLIT = ()
-AHEAD, LEAD = 7, 3
-PRE, IDX, MID = 14, 8, (10, 11)
+VEND = (0,)
+CYC, GATHER, SCATTER = 0.00083, 1.56, 3.8
+XFAR, XNEAR, ADDMA, GUARD = 4.0, 2.5, 3.5, 0.3
+ENDS, HOLD, PEW = 2, 2.0, 2.0
+EARLY = 20.0
 
 
 def _sb(n, d="bfloat16"):
@@ -24,7 +28,7 @@ SCRATCH = {
     "KI": _sb(1, "int32"), "KB": _sb(2, "int32"), "KF": _sb(4, "float32"),
     "ZR": _sb(512), "J16": _sb(128), "JG": _sb(32), "JX": _sb(168),
     "SA": _sb(512), "SY": _sb(288), "SY4": _sb(144), "RK": _sb(512), "SQ": _sb(1152), "BC": _sb(2048),
-    "I1": _sb(128), "IN": _sb(128), "I2": _sb(128), "GG": _sb(32), "NG": _sb(32), "GK": _sb(512), "WD": _sb(168),
+    "I1": _sb(128), "IN": _sb(128), "I2": _sb(128), "GG": _sb(32), "NG": _sb(32), "G2": _sb(32), "GK": _sb(512), "WD": _sb(168),
     "OG": _sb(128), "TR": _sb(128), "PM": _sb(128), "MY": _sb(128),
     "RV0": _sb(128), "RY0": _sb(128), "RV1": _sb(128), "RY1": _sb(128),
     "HV": _sb(2048), "HY": _sb(2048), "R": _sb(2048), "LO": _sb(2048), "DL": _sb(2048),
@@ -37,7 +41,7 @@ SCRATCH = {
     "AT": ("psum", [128, 512], "float32"), "WB": ("psum", [128, 512], "float32"),
     "M0": ("psum", [128, 512], "float32"), "M1": ("psum", [128, 512], "float32"),
 }
-NDMA = 40
+NDMA = 60
 SEMAPHORES = (["ev", "es", "ep", "eg", "sent", "sa0", "sa1"] + ["xa%d" % j for j in range(4)] + ["fa%d" % j for j in range(4)]
               + ["d%d" % j for j in range(NDMA)])
 BANKS = ("PB0a", "PB0b", "PB1a", "PB1b", "AT", "WB", "M0", "M1")
@@ -57,6 +61,65 @@ def masks(topo, cores, r):
     return out, far, near
 
 
+def conflicts(ops):
+    wrote, read, out = {}, {}, []
+    for n, o in enumerate(ops):
+        raw = set(wrote[key] for key in o["rd"] if key in wrote)
+        rest = set(m for key in o["rd"] if key in BANKS for m in read.get(key, []) if ops[m]["q"] != o["q"])
+        for key in o["wr"]:
+            rest.update(read.get(key, []) + ([wrote[key]] if key in wrote else []))
+        out.append((raw, rest - raw))
+        for key in o["wr"]:
+            wrote[key] = n
+            read[key] = []
+        for key in o["rd"]:
+            if key not in o["wr"]:
+                read.setdefault(key, []).append(n)
+    return out
+
+
+def arrange(ops, fixed):
+    before = [a | b for a, b in conflicts(ops)]
+    for n in range(1, fixed):
+        before[n].update(m for m in range(n) if ops[m]["q"] == ops[n]["q"])
+    after = [[] for _ in ops]
+    for n, ms in enumerate(before):
+        for m in ms:
+            after[m].append(n)
+    way = [0.0] * len(ops)
+    for n in range(len(ops) - 1, -1, -1):
+        way[n] = ops[n]["us"] * (PEW if ops[n]["q"] == "p" else 1.0) + max([way[m] for m in after[n]] + [ops[n].get("ahead", 0.0)])
+    left, at = [len(ms) for ms in before], [0.0] * len(ops)
+    ready, free, order = {}, {}, []
+    for n, o in enumerate(ops):
+        if not left[n]:
+            ready.setdefault(o["q"], []).append(n)
+    while len(order) < len(ops):
+        best = None
+        for q, ns in ready.items():
+            if ns:
+                t0 = max(free.get(q, 0.0), min(at[n] for n in ns))
+                n = max((n for n in ns if at[n] <= t0), key=lambda n: (way[n], -n))
+                soon = [m for m in ns if way[m] > way[n] and at[m] < t0 + GUARD * ops[n]["us"]]
+                if soon:
+                    n = min(soon, key=lambda m: at[m])
+                if best is None or max(t0, at[n]) < best[0]:
+                    best = (max(t0, at[n]), n)
+        t, n = best
+        o = ops[n]
+        ready[o["q"]].remove(n)
+        order.append(o)
+        if o["q"]:
+            free[o["q"]] = t + o.get("hold", o["us"])
+        for m in after[n]:
+            if m >= fixed or ops[m]["q"] != o["q"]:
+                at[m] = max(at[m], t + o["us"] + (0.0 if ops[m]["q"] == o["q"] == "p" else 0.06))
+            left[m] -= 1
+            if not left[m]:
+                ready.setdefault(ops[m]["q"], []).append(m)
+    return order
+
+
 def rank_program(g, core, T, topo):
     r = T.rank_of(core)
     if r is None:
@@ -68,45 +131,62 @@ def rank_program(g, core, T, topo):
     ops, sent = [], [0]
     mu, ad, eq, ne, ge = A.mult, A.add, A.is_equal, A.not_equal, A.is_ge
 
-    def op(q, fn, rd, wr, kind="c"):
-        if q == "g" and kind == "c" and any(o["kind"] == "r" for o in ops):
+    def op(q, fn, rd, wr, us, kind="c"):
+        if q == "g" and kind == "c" and sent[0]:
             rd, wr = list(rd) + ["pool"], list(wr) + ["pool"]
-        ops.append({"q": q, "fn": fn, "rd": list(rd), "wr": list(wr), "kind": kind})
+        ops.append({"q": q, "fn": fn, "rd": list(rd), "wr": list(wr), "kind": kind, "us": us})
 
-    def ts(out, in0, s1, s2, o0, o1, rd, wr):
+    def vec(fn, ap, cyc, rd, wr):
+        op("v", fn, rd, wr, 0.05 + CYC * max(64, cyc * ap.shape[-1]))
+
+    def ts(out, in0, s1, s2, o0, o1, rd, wr, cyc=1.0):
         if o1 is None:
-            op("v", lambda: g.vector.tensor_scalar(out, in0, s1, None, o0), rd, wr)
+            vec(lambda: g.vector.tensor_scalar(out, in0, s1, None, o0), out, cyc, rd, wr)
         else:
-            op("v", lambda: g.vector.tensor_scalar(out, in0, s1, s2, o0, o1), rd, wr)
+            vec(lambda: g.vector.tensor_scalar(out, in0, s1, s2, o0, o1), out, cyc, rd, wr)
 
-    def tt(out, a, b, o, rd, wr):
-        op("v", lambda: g.vector.tensor_tensor(out, a, b, o), rd, wr)
+    def tt(out, a, b, o, rd, wr, cyc=1.0):
+        vec(lambda: g.vector.tensor_tensor(out, a, b, o), out, cyc, rd, wr)
 
-    def cp(out, a, rd, wr):
-        op("v", lambda: g.vector.tensor_copy(out, a), rd, wr)
+    def cp(out, a, rd, wr, cyc=1.0):
+        vec(lambda: g.vector.tensor_copy(out, a), out, cyc, rd, wr)
 
-    def act(out, a, f, rd, wr, bias=0.0, scale=1.0):
-        op("s", lambda: g.scalar.activation(out, a, f, bias=bias, scale=scale), rd, wr)
+    def scatter(win, lst, a, rd, wr):
+        vec(lambda: g.vector.tensor_copy(win.indirect(lst), a), a, SCATTER, rd, wr)
+
+    def zero(ap, key):
+        vec(lambda: g.vector.memset(ap, 0.0), ap, 0.5, [], [key])
+
+    def act(out, a, f, rd, wr, bias=0.0, scale=1.0, cyc=1.0):
+        op("s", lambda: g.scalar.activation(out, a, f, bias=bias, scale=scale), rd, wr, 0.065 + CYC * cyc * out.shape[-1])
 
     def mm(out, l, rh, st, sp, rd, bank):
-        op("p", lambda: g.tensor.matmul(out, l, rh, st, sp), rd, [bank])
+        op("p", lambda: g.tensor.matmul(out, l, rh, st, sp), rd, [bank], CYC / 2 * max(64, out.shape[-1]))
 
-    def dma(q, pairs, rd, wr):
+    def dma(q, pairs, rd, wr, us=2.5):
         e = g.sync if q == "y" else g.scalar
-        op(q, lambda: [e.dma_start(o, a) for o, a in pairs], rd, wr, "d")
+        op(q, lambda: [e.dma_start(o, a) for o, a in pairs], rd, wr, us, "d")
+        ops[-1]["hold"] = 0.1 * len(pairs)
+
+    def add(out, a, rd, key):
+        op("g", lambda: [g.dma_start(out, a, accum_op=ad)], rd, [key], ADDMA, "d")
+        ops[-1]["hold"] = HOLD
 
     def iota(out, pat, base, cm, wr):
-        op("g", lambda: g.iota(out, pat, base, cm, allow_small_or_imprecise_dtypes=True), [], wr)
+        op("g", lambda: g.iota(out, pat, base, cm, allow_small_or_imprecise_dtypes=True), [], wr, 0.13 + 2 * CYC * out.shape[-1])
+
+    def select(out, a, pat, cmp, fill, base, cm, rd, key):
+        op("g", lambda: g.affine_select(out, a, pat, cmp, fill, base, cm), rd, [key], 0.17 + 2 * CYC * out.shape[-1])
 
     def mark(out, n, pat, base, val, key):
-        op("g", lambda: g.affine_select(out, T.ZR[:, 0:n], pat, ne, val, base, 1), ["ZR"], [key])
+        select(out, T.ZR[:, 0:n], pat, ne, val, base, 1, ["ZR"], key)
 
     def band(out, n, pat, base, width, val, key):
         neg = [[-s, c] for s, c in pat]
-        op("g", lambda: g.affine_select(out, T.ZR[:, 0:n], neg, ge, val, -base - 1, -1), ["ZR"], [key])
-        op("g", lambda: g.affine_select(out, out, neg, ge, 0.0, width - 1 - base, -1), [key], [key])
+        select(out, T.ZR[:, 0:n], neg, ge, val, -base - 1, -1, ["ZR"], key)
+        select(out, out, neg, ge, 0.0, width - 1 - base, -1, [key], key)
 
-    def send(to, srcs, dst, sem, rd):
+    def send(to, srcs, dst, sem, rd, tag):
         def fn():
             trs = []
             for d in to:
@@ -114,69 +194,74 @@ def rank_program(g, core, T, topo):
                 trs.append(RemoteDMATransfer(dst_ids=[DstId(rid=rid, pnc=pid)], dma_engine_mask=sum(1 << e for e in eng[d]),
                                              remote_sem=sem, src=srcs[d], dst=dst))
             return g.remote_dma_fused(trs, local_sem=T.sem.sent)
+        op("g", fn, rd, [tag], 0.5 if sent[0] else 2.0, "r")
         sent[0] += sum(len(eng[d]) for d in to)
-        op("g", fn, rd, [], "r")
 
-    def arrive(key, sem, n):
-        ops.append({"q": None, "kind": "x", "rd": [], "wr": [key], "sem": sem, "n": n})
+    def arrive(key, sem, n, tag, us):
+        ops.append({"q": None, "kind": "x", "rd": [tag], "wr": [key], "sem": sem, "n": n, "us": us})
 
     def bank(j):
         name = BANKS[j]
         return (T[name[:3]], 512 * (j % 2)) if j < 4 else (T[name], 0)
 
+    def reg(bk, n, c=0):
+        b, o = bank(BANKS.index(bk))
+        return b[:, o + c:o + c + n]
+
     lo = 32 * r
-    dma("s", [(T.A32[:], T.adj[lo:lo + 32, :])], [], ["A32"])
-    dma("y", [(T.TQ[32 * k:32 * k + 32, :], T.tv[lo:lo + 32, 8 * k:8 * k + 104]) for k in range(4)], [], ["TQ"])
-    dma("s", [(T.XS[d], T.x[32 * d:32 * d + 32, :]) for d in far], [], ["XSf"])
-    dma("y", [(T.XS[d], T.x[32 * d:32 * d + 32, :]) for d in near], [], ["XSn"])
-    dma("y", [(T.T32[32 * k:32 * k + 32, :], T.tv[lo:lo + 32, :]) for k in range(4)], [], ["T32"])
-    dma("y", [(T.X[lo:lo + 32, :], T.x[lo:lo + 32, :])], [], ["X%d" % r])
-    op("v", lambda: g.vector.memset(T.ZR[:], 0.0), [], ["ZR"])
-    op("g", lambda: g.iota(T.KI[:], [[0, 1]], 0, 1), [], ["KI"])
+    dma("s", [(T.A32[:], T.adj[lo:lo + 32, :])], [], ["A32", "s0"], 3.0)
+    dma("y", [(T.TQ[32 * k:32 * k + 32, :], T.tv[lo:lo + 32, 8 * k:8 * k + 104]) for k in range(4)], [], ["TQ"], 3.5)
+    dma("s", [(T.XS[d], T.x[32 * d:32 * d + 32, :]) for d in far], [], ["XSf"], 4.0)
+    dma("y", [(T.XS[d], T.x[32 * d:32 * d + 32, :]) for d in near], [], ["XSn"], 4.5)
+    dma("y", [(T.T32[32 * k:32 * k + 32, :], T.tv[lo:lo + 32, :]) for k in range(4)], [], ["T32"], 5.0)
+    dma("y", [(T.X[lo:lo + 32, :], T.x[lo:lo + 32, :])], [], ["X%d" % r], 5.0)
+    zero(T.ZR[:], "ZR")
+    op("g", lambda: g.iota(T.KI[:], [[0, 1]], 0, 1), [], ["KI"], 0.13)
     iota(T.J16[:], [[-16, 8], [0, 16]], 0, 1, ["J16"])
     mark(T.SA[:], 512, [[-1, 4], [0, 4], [-4, 32]], 0, 1.0, "SA")
     mark(T.SY[:], 288, [[-1, 2], [-16, 9], [128, 16]], -128 * 15, 1.0, "SY")
     mark(T.I1[:], 128, [[-1, 128]], 0, 1.0, "I1")
     mark(T.SQ[:, 128:384], 256, [[128, 2], [-1, 16], [-16, 8]], 0, 1.0, "SQ0")
-    send(far, T.XS, T.XL[r], T.sem["xa%d" % r], ["XSf"])
-    send(near, T.XS, T.XL[r], T.sem["xa%d" % r], ["XSn"])
+    fixed = len(ops)
+    send(far, T.XS, T.XL[r], T.sem["xa%d" % r], ["XSf"], "xf")
+    send(near, T.XS, T.XL[r], T.sem["xa%d" % r], ["XSn", "xf"], "xn")
     mark(T.RK[:], 512, [[-32, 4], [0, 4], [-1, 32]], 0, 1.0, "RK")
+    ops[-1]["rd"].append("xn")
     iota(T.JG[:], [[1, 2], [0, 16]], 0, 0, ["JG"])
     iota(T.JX[:], [[1, 168]], -39, 0, ["JX"])
     for k in range(4):
         iota(T.IV[32 * k:32 * k + 32, :], [[1, 256]], 16 + 256 * k, 0, ["IV%d" % k])
-    for j, s in enumerate(near + far):
-        arrive("XL%d" % s, T.sem["xa%d" % s], inc[s])
+    for s in near + far:
+        arrive("XL%d" % s, T.sem["xa%d" % s], inc[s], "xn" if s in near else "xf", XNEAR if s in near else XFAR)
         dma("y", [(T.X[32 * s:32 * s + 32, :], T.XL[s])], ["XL%d" % s], ["X%d" % s])
     XK = ["X%d" % s for s in range(4)]
 
-    op("v", lambda: g.vector.memset(T.SQ[:, 0:128], 0.0), [], ["SQp"])
-    op("v", lambda: g.vector.memset(T.HW[:, 0:16], 0.0), [], ["HWp"])
+    zero(T.SQ[:, 0:128], "SQp")
+    zero(T.HW[:, 0:16], "HWp")
     ts(T.KB[:, 0:1], T.KI[:], 4, 1, A.arith_shift_right, A.bitwise_and, ["KI"], ["KB0"])
     ts(T.KB[:, 1:2], T.KI[:], 5, None, A.arith_shift_right, None, ["KI"], ["KB1"])
+    cp(T.KF[:, 0:2], T.KB[:], ["KB0", "KB1"], ["KF"])
+    ts(T.KF[:, 2:3], T.KF[:, 1:2], 8.0, None, mu, None, ["KF"], ["KF2"])
+    ts(T.KF[:, 3:4], T.KF[:, 0:1], 64.0, T.KF[:, 2:3], mu, ad, ["KF", "KF2"], ["KF3"])
     for j in range(16):
-        ts(T.BC[:, 128 * j:128 * j + 128], T.J16[:], float(j), None, eq, None, ["J16"], ["BC%d" % j])
-        if j == 0:
-            cp(T.KF[:, 0:2], T.KB[:], ["KB0", "KB1"], ["KF"])
-        if j == 2:
-            ts(T.KF[:, 2:3], T.KF[:, 1:2], 8.0, None, mu, None, ["KF"], ["KF2"])
-        if j == 4:
-            ts(T.KF[:, 3:4], T.KF[:, 0:1], 64.0, T.KF[:, 2:3], mu, ad, ["KF", "KF2"], ["KF3"])
+        ts(T.BC[:, 128 * j:128 * j + 128], T.J16[:], float(j), None, eq, None, ["J16"], ["BC%d" % j], 0.5)
+    ts(T.GG[:], T.JG[:], T.KF[:, 0:1], None, eq, None, ["JG", "KF"], ["GG"])
+    ts(T.NG[:], T.JG[:], T.KF[:, 0:1], -1.0, eq, mu, ["JG", "KF"], ["NG"])
+    ts(T.G2[:], T.JG[:], T.KF[:, 0:1], 2.0, eq, mu, ["JG", "KF"], ["G2"])
+    ts(T.WD[:], T.JX[:], T.KF[:, 3:4], None, eq, None, ["JX", "KF3"], ["WD"], 0.5)
 
     ts(T.A16[:], T.A32[:], -H, None, ad, None, ["A32"], ["A16"])
     for j in range(8):
-        b, o = bank(j)
-        mm(b[:, o:o + 288], T.SA[:, 128 * (j // 2):128 * (j // 2) + 128], T.A16[:, 288 * (j % 2):288 * (j % 2) + 288], True, True,
+        mm(reg(BANKS[j], 288), T.SA[:, 128 * (j // 2):128 * (j // 2) + 128], T.A16[:, 288 * (j % 2):288 * (j % 2) + 288], True, True,
            ["SA", "A16"], BANKS[j])
     for t in range(2):
         for h in range(2):
             cp(T.OL[:, 32 * t + 8 * h:32 * t + 8 * h + 8], T.TQ[:, 64 * t + 32 * h:64 * t + 32 * h + 8], ["TQ"], ["OV%d%d" % (t, h)])
     for j in range(8):
-        b, o = bank(j)
         if j % 2 == 0 or j == 1:
-            act(T.AW[:, 288 * j:288 * j + 288], b[:, o:o + 288], F.Copy, [BANKS[j]], ["AW%d" % j])
+            act(T.AW[:, 288 * j:288 * j + 288], reg(BANKS[j], 288), F.Copy, [BANKS[j]], ["AW%d" % j])
         else:
-            cp(T.AW[:, 288 * j:288 * j + 288], b[:, o:o + 288], [BANKS[j]], ["AW%d" % j])
+            cp(T.AW[:, 288 * j:288 * j + 288], reg(BANKS[j], 288), [BANKS[j]], ["AW%d" % j])
     AWK = ["AW%d" % j for j in range(8)]
     for name, sc in (("IN", -1.0), ("I2", 2.0)):
         act(T[name][:], T.I1[:], F.Copy, ["I1"], [name], scale=sc)
@@ -185,49 +270,30 @@ def rank_program(g, core, T, topo):
     for name in ("IM", "RM"):
         act(T[name][:], T.AW[:], F.Copy, AWK, [name], scale=0.0)
     for t in range(2):
-        cp(T.CV[:, 256 * t:256 * t + 256], T.AW[:].indirect(T.OL[:, 32 * t:32 * t + 16]), AWK + ["OV%d0" % t, "OV%d1" % t], ["CV%d" % t])
+        cp(T.CV[:, 256 * t:256 * t + 256], T.AW[:].indirect(T.OL[:, 32 * t:32 * t + 16]), AWK + ["OV%d0" % t, "OV%d1" % t], ["CV%d" % t], GATHER)
         bk = "M%d" % t
         for p in range(16):
             mm(T[bk][:, 0:16], T.SY[:, 144 * t + 15 - p:144 * t + 143 - p], T.CV[:, 256 * t + p:256 * t + 256:16], p == 0, p == 15,
                ["SY", "CV%d" % t], bk)
     for t in range(2):
         ts(T.OL[:, 32 * t + 16:32 * t + 32], T["M%d" % t][:, 0:16], H, None, ad, None, ["M%d" % t], ["OY%d" % t])
-        cp(T.CY[:, 256 * t:256 * t + 256], T.AW[:].indirect(T.OL[:, 32 * t + 16:32 * t + 32]), AWK + ["OY%d" % t], ["CY%d" % t])
+        cp(T.CY[:, 256 * t:256 * t + 256], T.AW[:].indirect(T.OL[:, 32 * t + 16:32 * t + 32]), AWK + ["OY%d" % t], ["CY%d" % t], GATHER)
+        cp(T.YO[:, 16 * t:16 * t + 16], T["M%d" % t][:, 0:16], ["M%d" % t], ["YO%d" % t])
     CK = ["CY0", "CY1"]
-
-    def spread(n):
-        bk = "M%d" % (n % 2)
-        if n >= 2:
-            mm(T[bk][:], T.BC[:, 128 * n:128 * n + 128], T.CV[:], True, True, ["BC%d" % n, "CV0", "CV1"], bk)
-            return
-        for t in range(2):
-            j, src = (t, T.CY) if n == 0 else (1 - t, T.CV)
-            mm(T[bk][:, 256 * t:256 * t + 256], T.BC[:, 128 * j:128 * j + 128], src[:, 256 * t:256 * t + 256], True, True,
-               ["BC0", "BC1", "CV0", "CV1"] + CK, bk)
-
-    def match(n):
-        bk = "M%d" % (n % 2)
-        out, key = (T.EV[:], "EV") if n == 0 else (T.EQ[:, 512 * (n % 2):512 * (n % 2) + 512], "EQ%d" % (n % 2))
-        tt(out, T[bk][:], T.CY[:], eq, [bk] + CK, [key])
-        if n + 2 < 16:
-            spread(n + 2)
-        if n > 0:
-            wn = "I1" if n == 1 else "I2"
-            mm(T.WB[:], T[wn][:], out, False, n == 15, [wn, key], "WB")
-
+    cp(T.VL[:], T.T32[:], ["T32"], ["VL"])
+    for c in range(4):
+        for k in range(4):
+            mm(T.WB[:, 32 * c + 8 * k:32 * c + 8 * k + 8], T.RK[:, 128 * k:128 * k + 128], T.YO[:, 8 * c:8 * c + 8], True, True,
+               ["RK", "YO%d" % (c // 2)], "WB")
+    ts(T.YL[:], T.WB[:, 0:128], H, None, ad, None, ["WB"], ["YL"])
     for t in range(2):
         for h in range(2):
             for k in range(4):
                 mm(T.AT[:, 8 * t + 4 * h + k:512:16], T.CY[:, 256 * t + 128 * h:256 * t + 128 * h + 128], T.I1[:, 32 * k:32 * k + 32], True, True,
                    ["CY%d" % t, "I1"], "AT")
-    for t in range(2):
-        cp(T.YO[:, 16 * t:16 * t + 16], T["M%d" % t][:, 0:16], ["M%d" % t], ["YO%d" % t])
-    spread(0)
-    spread(1)
     cp(T.T1[:], T.AT[:], ["AT"], ["T1"])
-    ts(T.EN[:], T.CY[:], H, 64.0, eq, mu, CK, ["EN"])
-    cp(T.VL[:], T.T32[:], ["T32"], ["VL"])
-    mm(T.WB[:], T.IN[:], T.EN[:], True, False, ["IN", "EN"], "WB")
+    mm(T.AT[:], T.ZR[:, 0:128], T.ZR[:], True, True, ["ZR"], "AT")
+    ops[-1]["wr"].append("A0")
     SQK = ["SQp"] + ["SQ%d" % k for k in range(3)]
     for j in range(4):
         b, o = bank(j)
@@ -236,71 +302,84 @@ def rank_program(g, core, T, topo):
                 c = 128 * (1 - gr) + q
                 mm(b[:, o + q:o + 512:8], T.SQ[:, c:c + 1017:8], T.T1[:, 256 * gr + 64 * j:256 * gr + 64 * j + 64], gr == 0, gr == 1,
                    SQK + ["T1"], BANKS[j])
-        if j < 2:
-            match(j)
-    for c in range(4):
-        for k in range(4):
-            mm(T.AT[:, 32 * c + 8 * k:32 * c + 8 * k + 8], T.RK[:, 128 * k:128 * k + 128], T.YO[:, 8 * c:8 * c + 8], True, True,
-               ["RK", "YO%d" % (c // 2)], "AT")
     for j in range(2):
         ts(T.ZL[:, 1024 * j:1024 * j + 1024], T["PB%d" % j][:], H, float(V - 1), ad, A.min, ["PB%da" % j, "PB%db" % j], ["ZL%d" % j])
-    ts(T.YL[:], T.AT[:, 0:128], H, None, ad, None, ["AT"], ["YL"])
-    mm(T.AT[:], T.ZR[:, 0:128], T.ZR[:], True, True, ["ZR"], "AT")
 
-    def end(t, c):
-        out, lst = ((T.HV, "VL"), (T.HY, "YL"))[c]
-        act(out[:, 1024 * t:1024 * t + 1024], T.X[:].indirect(T[lst][:, 64 * t:64 * t + 64]), F.Copy, XK + [lst], ["H%d%d" % (t, c)], scale=0.5)
+    ts(T.EN[:], T.CY[:], H, 64.0, eq, mu, CK, ["EN"], 0.5)
+    mm(T.WB[:], T.IN[:], T.EN[:], True, False, ["IN", "EN"], "WB")
+    for n in range(16):
+        bk = "M%d" % (n % 2)
+        if n >= 2:
+            mm(T[bk][:], T.BC[:, 128 * n:128 * n + 128], T.CV[:], True, True, ["BC%d" % n, "CV0", "CV1"], bk)
+        else:
+            for t in range(2):
+                j, src = (t, T.CY) if n == 0 else (1 - t, T.CV)
+                mm(T[bk][:, 256 * t:256 * t + 256], T.BC[:, 128 * j:128 * j + 128], src[:, 256 * t:256 * t + 256], True, True,
+                   ["BC0", "BC1", "CV0", "CV1"] + CK, bk)
+        out, key = (T.EV[:], "EV") if n == 0 else (T.EQ[:, 512 * (n % 2):512 * (n % 2) + 512], "EQ%d" % (n % 2))
+        tt(out, T[bk][:], T.CY[:], eq, [bk] + CK, [key])
+        if n > 0:
+            wn = "I1" if n == 1 else "I2"
+            mm(T.WB[:], T[wn][:], out, False, n == 15, [wn, key], "WB")
+    ts(T.W[:], T.WB[:], 0.5, 1.0, mu, A.min, ["WB"], ["W"])
 
-    def middle(t, j, h, bk):
-        c = 1024 * t + 512 * h
-        b, o = bank(BANKS.index(bk))
-        terms = [("I1", T.HV, "H%d0" % t), ("IN", T.HY, "H%d1" % t)] if j == 0 else \
-                [("I1", T.HV, "H%d0" % t), ("I1", T.HY, "H%d1" % t), ("IN", T.R, "R%d%d" % (t, h))]
-        for m, (wn, src, key) in enumerate(terms):
-            mm(b[:, o:o + 512], T[wn][:], src[:, c:c + 512], m == 0, m == len(terms) - 1, [wn, key], bk)
-        out, f = (("R", F.Abs), ("LO", F.Copy))[j]
-        act(T[out][:, c:c + 512], b[:, o:o + 512], f, [bk], ["%s%d%d" % (out, t, h)])
-
-    def dist(t):
+    def ends(t, banks):
+        if t in VEND:
+            c = 1024 * t
+            for j, (out, lst) in enumerate(((T.HV, "VL"), (T.HY, "YL"))):
+                act(out[:, c:c + 1024], T.X[:].indirect(T[lst][:, 64 * t:64 * t + 64]), F.Copy, XK + [lst], ["H%d%d" % (t, j)], cyc=GATHER)
+            tt(T.LO[:, c:c + 1024], T.X[:].indirect(T.YL[:, 64 * t:64 * t + 64]), T.HV[:, c:c + 1024], A.min, XK + ["YL", "H%d0" % t],
+               ["LO%d0" % t, "LO%d1" % t], GATHER)
+            for h, bk in enumerate(banks[0:2]):
+                for m, (wn, src, key) in enumerate([("IN", T.HV, "H%d0" % t), ("IN", T.HY, "H%d1" % t), ("I2", T.LO, "LO%d0" % t)]):
+                    mm(reg(bk, 512), T[wn][:], src[:, c + 512 * h:c + 512 * h + 512], m == 0, m == 2, [wn, key], bk)
+            ts(T.DL[:, c:c + 1024], T[banks[0][:3]][:], -0.5, None, A.min, None, banks[0:2], ["DL%d" % t])
+            return
+        for c, (out, lst) in enumerate(((T.HV, "VL"), (T.HY, "YL"))):
+            o, z = out[:, 1024 * t:1024 * t + 1024], T.X[:].indirect(T[lst][:, 64 * t:64 * t + 64])
+            act(o, z, F.Copy, XK + [lst], ["H%d%d" % (t, c)], scale=0.5, cyc=GATHER)
+        for j in range(2):
+            for h in range(2):
+                c, bk = 1024 * t + 512 * h, banks[2 * j + h]
+                terms = [("I1", T.HV, "H%d0" % t), ("IN", T.HY, "H%d1" % t)] if j == 0 else \
+                        [("I1", T.HV, "H%d0" % t), ("I1", T.HY, "H%d1" % t), ("IN", T.R, "R%d%d" % (t, h))]
+                for m, (wn, src, key) in enumerate(terms):
+                    mm(reg(bk, 512), T[wn][:], src[:, c:c + 512], m == 0, m == len(terms) - 1, [wn, key], bk)
+                out, f = (("R", F.Abs), ("LO", F.Copy))[j]
+                if t == 0:
+                    act(T[out][:, c:c + 512], reg(bk, 512), f, [bk], ["%s%d%d" % (out, t, h)])
+            if t == 1:
+                act(T[out][:, 1024:2048], T[bk[:3]][:], f, banks[2 * j:2 * j + 2], [out + "10", out + "11"])
         c = 1024 * t
-        ts(T.DL[:, c:c + 1024], T.R[:, c:c + 1024], 4.0, 1.0, mu, A.max, ["R%d0" % t, "R%d1" % t], ["DL%d" % t])
+        ts(T.DL[:, c:c + 1024], T.R[:, c:c + 1024], -2.0, -0.5, mu, A.min, ["R%d0" % t, "R%d1" % t], ["DL%d" % t], 0.5)
 
     def merge(name):
         dma("y", [(T[name][16 * gr + k:128:32, :], T[name][32 * k + 16 * gr + 8:32 * k + 16 * gr + 12, :]) for k in range(4) for gr in range(2)],
-            [name], [name])
+            [name], [name], 5.0)
 
-    def index_out():
+    def index():
         for c in range(2):
-            cp(T.IM[:].indirect(T.OL[:, 32 + 16 * c:48 + 16 * c]), T.IV[:], ["IM", "OV10", "OV11", "OY1"] + ["IV%d" % k for k in range(4)], ["IM"])
+            scatter(T.IM[:], T.OL[:, 32 + 16 * c:48 + 16 * c], T.IV[:], ["IM", "OV10", "OV11", "OY1"] + ["IV%d" % k for k in range(4)], ["IM"])
         merge("IM")
-
-    def index_in():
-        cp(T.IG[:], T.IM[:].indirect(T.OL[:, 0:32]), ["IM", "OY0"], ["IG"])
+        cp(T.IG[:], T.IM[:].indirect(T.OL[:, 0:32]), ["IM", "OY0"], ["IG"], GATHER)
         for p in range(16):
             mm(T.M0[:, 0:32], T.SY4[:, 15 - p:143 - p], T.IG[:, p:512:16], p == 0, p == 15, ["SY4", "IG"], "M0")
+        cp(T.ML[:], T.M0[:, 0:32], ["M0"], ["ML"])
 
-    def late():
-        grp, turn = [[-16, 8], [0, 16]], [[-16, 2], [0, 16], [-32, 4]]
-        row = [[-16, 2], [128, 16], [-32, 4]]
-        return [
-            lambda: band(T.SY4[:], 144, [[-16, 9], [128, 16]], -128 * 15, 4, 1.0, "SY4"),
-            lambda: band(T.OG[:], 128, grp, 0, 16, 1.0, "OG"),
-            lambda: (band(T.TR[:], 128, grp, 0, 16, 4096.0, "TR"),
-                     op("g", lambda: g.affine_select(T.TR[:], T.TR[:], [[1, 128]], ge, 0.0, 0, -1), ["TR"], ["TR"]),
-                     op("g", lambda: g.affine_select(T.TR[:], T.TR[:], [[1, 128]], ne, -4096.0, 0, -1), ["TR"], ["TR"])),
-            lambda: (mark(T.PM[:], 128, [[-16, 2], [-1, 16], [-32, 4]], 0, 1.0, "PM"),
-                     band(T.MY[:], 128, [[-16, 8], [128, 16]], 0, 4, 1.0, "MY")),
-            lambda: (band(T.RV0[:], 128, turn, 0, 4, -0.5, "RV0"), band(T.RY0[:], 128, row, 0, 4, -1.0, "RY0")),
-            lambda: (mark(T.RV1[:], 128, turn, 0, -0.5, "RV1"), mark(T.RY1[:], 128, row, -128, -1.0, "RY1")),
-        ]
-
-    def reg(bk, n):
-        b, o = bank(BANKS.index(bk))
-        return b[:, o:o + n]
-
-    def half(bk, h):
-        b, o = bank(BANKS.index(bk))
-        return b[:, o + 128 * h:o + 128 * h + 128]
+    grp, turn, row = [[-16, 8], [0, 16]], [[-16, 2], [0, 16], [-32, 4]], [[-16, 2], [128, 16], [-32, 4]]
+    band(T.OG[:], 128, grp, 0, 16, 1.0, "OG")
+    band(T.TR[:], 128, grp, 0, 16, 4096.0, "TR")
+    select(T.TR[:], T.TR[:], [[1, 128]], ge, 0.0, 0, -1, ["TR"], "TR")
+    select(T.TR[:], T.TR[:], [[1, 128]], ne, -4096.0, 0, -1, ["TR"], "TR")
+    band(T.SY4[:], 144, [[-16, 9], [128, 16]], -128 * 15, 4, 1.0, "SY4")
+    mark(T.PM[:], 128, [[-16, 2], [-1, 16], [-32, 4]], 0, 1.0, "PM")
+    band(T.MY[:], 128, [[-16, 8], [128, 16]], 0, 4, 1.0, "MY")
+    band(T.RV0[:], 128, turn, 0, 4, -0.5, "RV0")
+    band(T.RY0[:], 128, row, 0, 4, -1.0, "RY0")
+    mark(T.RV1[:], 128, turn, 0, -0.5, "RV1")
+    mark(T.RY1[:], 128, row, -128, -1.0, "RY1")
+    for k in range(4):
+        band(T.GK[:, 128 * k:128 * k + 128], 128, [[0, 4], [-16, 2], [0, 16]], -32 * k, 16, 1.0, "GK%d" % k)
 
     def masked(t, bm):
         c = 256 * t
@@ -310,9 +389,10 @@ def rank_program(g, core, T, topo):
             mm(reg(bm, 256), T.MY[:], T.RG0[:, 256:512], False, False, ["MY", "RG0"], bm)
 
     def sums_in(t, bm):
-        act(T.AB[:], T.AT[:, 256 * t:256 * t + 256], F.Abs, ["AT"], ["AB"], bias=0.5, scale=1.0 / 128)
+        act(T.AB[:], T.AT[:, 256 * t:256 * t + 256], F.Abs, ["AT"] + ["A%d%d" % (n, h) for n in range(15 * t, 15 * t + 15) for h in range(2)],
+            ["AB"], bias=0.5, scale=1.0 / 128)
         for h in range(2):
-            mm(half(bm, h), T.AB[:, 128 * h:128 * h + 128], T.I1[:], False, h == 1, ["AB", "I1"], bm)
+            mm(reg(bm, 128, 128 * h), T.AB[:, 128 * h:128 * h + 128], T.I1[:], False, h == 1, ["AB", "I1"], bm)
         ts(T.OK[:], reg(bm, 256), 6.5 / 128, None, A.is_le, None, [bm], ["OK"])
 
     def column(t, bk, wn):
@@ -323,9 +403,8 @@ def rank_program(g, core, T, topo):
         ts(T.PR[:], reg(bp, 256), 4096.0, H, ad, A.min, [bp], ["PR"])
 
     def hit(t, bh):
-        b, o = bank(BANKS.index(bh))
         for h in range(2 - t):
-            mm(b[:, o + 256 * h:o + 256 * h + 256], T.OG[:], T.OK[:], True, True, ["OG", "OK"], bh)
+            mm(reg(bh, 256, 256 * h), T.OG[:], T.OK[:], True, True, ["OG", "OK"], bh)
         act(T["HT%d" % t][:], reg(bh, 512 - 256 * t), F.Sign, [bh], ["HT%d" % t])
 
     def same(t, bb):
@@ -338,12 +417,11 @@ def rank_program(g, core, T, topo):
             mm(reg(bs, 16), T.WD[:, x0:x0 + 128], T.PR[:, 16 * j:16 * j + 16], j == 0, j == 15, ["WD", "PR"], bs)
         sp, sd = T["SP%d" % t], T["SD%d" % t]
         act(sp[:], reg(bs, 16), F.Identity, [bs], ["SP%d" % t], bias=-14 * H)
-        send(others, {d: sp[:] for d in others}, sd[r], T.sem["sa%d" % t], ["SP%d" % t])
+        send(others, {d: sp[:] for d in others}, sd[r], T.sem["sa%d" % t], ["SP%d" % t], "ss%d" % t)
         dma("y", [(sd[r], sp[:])], ["SP%d" % t], ["SO%d" % t])
-        arrive("SR%d" % t, T.sem["sa%d" % t], sum(inc.values()))
-
-    def sep_out(t):
-        dma("y", [(T.ysep[:, 1024 * t:1024 * t + 1024], T["SD%d" % t][:])], ["SO%d" % t, "SR%d" % t], ["ys%d" % t])
+        arrive("SR%d" % t, T.sem["sa%d" % t], sum(inc.values()), "ss%d" % t, 3.0 + 5 * (1 - t))
+        dma("y", [(T.ysep[:, 1024 * t:1024 * t + 1024], sd[:])], ["SO%d" % t, "SR%d" % t], ["ys%d" % t])
+        ops[-1]["ahead"] = EARLY if t == 0 else 2.0
 
     def score(bk, terms, st, sp):
         for m, (wn, src, c, key) in enumerate(terms):
@@ -352,166 +430,107 @@ def rank_program(g, core, T, topo):
     chunks = [(t, i) for t in range(2) for i in range(16) if i != t]
     own = [n for n in range(30) if n not in SCAL]
 
-    def diff(n):
-        if n in SCAL:
-            c = 1024 * SCAL.index(n)
-            return T.UK, c, "UK%d" % n
-        return T.U, 1024 * (own.index(n) % NU), "U%d" % (own.index(n) % NU)
-
-    def gather(n):
+    def chunk(n):
         t, i = chunks[n]
-        u, c, key = diff(n)
         z, low = T.X[:].indirect(T.ZL[:, 128 * i + 64 * t:128 * i + 64 * t + 64]), T.LO[:, 1024 * t:1024 * t + 1024]
-        lk = ["LO%d0" % t, "LO%d1" % t]
+        lk, pos, neg = ["LO%d0" % t, "LO%d1" % t], T.GG[:, 0:17:16], T.NG[:, 0:17:16]
         if n in SCAL:
-            act(u[:, c:c + 1024], z, F.Copy, XK + ["ZL%d" % (i // 8)], [key], scale=-1.0)
-            op("g", lambda: [g.dma_start(u[:, c:c + 1024], low, accum_op=ad)], [key] + lk, [key], "d")
+            u, c, key, wn, ws, wc = T.UK, 1024 * SCAL.index(n), "UK%d" % n, "IN", neg, pos
+            act(u[:, c:c + 1024], z, F.Copy, XK + ["ZL%d" % (i // 8)], [key], scale=-1.0, cyc=GATHER)
+            add(u[:, c:c + 1024], low, [key] + lk, key)
         else:
-            tt(u[:, c:c + 1024], z, low, A.subtract, XK + ["ZL%d" % (i // 8)] + lk, [key])
-
-    def clamp(n):
-        u, c, key = diff(n)
-        ts(T.C[:, 1024 * (n % NC):1024 * (n % NC) + 1024], u[:, c:c + 1024], -1.0, 1.0, A.max, A.min, [key], ["C%d" % (n % NC)])
-
-    def fold(n):
-        t, i = chunks[n]
-        u, c, key = diff(n)
-        wn = "I1" if n in SCAL else "IN"
+            u, c, key, wn, ws, wc = T.U, 1024 * (own.index(n) % NU), "U%d" % (own.index(n) % NU), "I1", pos, neg
+            tt(u[:, c:c + 1024], z, low, A.subtract, XK + ["ZL%d" % (i // 8)] + lk, [key], GATHER)
+        pb = "PB%d" % (len([m for m in range(n) if m not in ADDED]) % 2)
+        c0, ck, s0, sk = 1024 * (n % NC), "C%d" % (n % NC), 1024 * (n % NS), "SG%d" % (n % NS)
+        ts(T.C[:, c0:c0 + 1024], u[:, c:c + 1024], -1.0, 1.0, A.max, A.min, [key], [ck], 0.5)
+        ws = [ws, ws]
+        if n in ADDED:
+            add(u[:, c:c + 1024], T.DL[:, 1024 * t:1024 * t + 1024], [key, "DL%d" % t], key)
+            ts(T.SG[:, s0:s0 + 1024], u[:, c:c + 1024], -0.5, 0.5, A.max, A.min, [key], [sk + "a", sk + "b"], 0.5)
+            ws = [T.G2[:, 0:17:16]] * 2
+        else:
+            for h, bk in enumerate((pb + "a", pb + "b")):
+                mm(reg(bk, 512), T.I1[:], u[:, c + 512 * h:c + 512 * h + 512], True, False, ["I1", key], bk)
+                mm(reg(bk, 512), T[wn][:], T.DL[:, 1024 * t + 512 * h:1024 * t + 512 * h + 512], False, True, [wn, "DL%d" % t], bk)
+            if n in SPLIT:
+                act(T.SG[:, s0:s0 + 512], T[pb][:, 0:512], F.Sign, [pb + "a"], [sk + "a"])
+                ts(T.SG[:, s0 + 512:s0 + 1024], T[pb][:, 512:1024], -0.5, 0.5, A.max, A.min, [pb + "b"], [sk + "b"])
+                ws[1] = T.G2[:, 0:17:16]
+            else:
+                act(T.SG[:, s0:s0 + 1024], T[pb][:], F.Sign, [pb + "a", pb + "b"], [sk + "a", sk + "b"])
         for h in range(2):
-            b, o = bank(2 * (n % 2) + h)
-            mm(b[:, o:o + 512], T.I2[:], u[:, c + 512 * h:c + 512 * h + 512], True, False, ["I2", key], BANKS[2 * (n % 2) + h])
-            mm(b[:, o:o + 512], T[wn][:], T.DL[:, 1024 * t + 512 * h:1024 * t + 512 * h + 512], False, True, [wn, "DL%d" % t], BANKS[2 * (n % 2) + h])
+            def sums(h=h):
+                for b in range(4 * h, 4 * h + 4):
+                    a = 256 * t + 32 * b + i
+                    g.tensor.matmul(T.AT[:, a:a + 17:16], T.C[:, c0 + 128 * b:c0 + 128 * b + 128], wc, True, False)
+                    last = g.tensor.matmul(T.AT[:, a:a + 17:16], T.SG[:, s0 + 128 * b:s0 + 128 * b + 128], ws[h], False, True)
+                return last
+            op("p", sums, [ck, sk + "ab"[h], "GG", "NG", "G2", "A0"], ["A%d%d" % (n, h)], 4 * 64 * CYC)
+            ops[-1]["bank"] = "AT"
 
-    def sign(n):
-        pb = "PB%d" % (n % 2)
-        c, key = 1024 * (n % NS), "SG%d" % (n % NS)
-        if n in SPLIT:
-            act(T.SG[:, c:c + 512], T[pb][:, 0:512], F.Sign, [pb + "a"], [key + "a"])
-            ts(T.SG[:, c + 512:c + 1024], T[pb][:, 512:1024], -1.0, 1.0, A.max, A.min, [pb + "b"], [key + "b"])
-        else:
-            act(T.SG[:, c:c + 1024], T[pb][:], F.Sign, [pb + "a", pb + "b"], [key + "a", key + "b"])
+    ends(0, list(BANKS[0:4]))
+    index()
+    for n in range(15):
+        if n == ENDS:
+            ends(1, list(BANKS[0:4]))
+        chunk(n)
+    masked(0, "M0")
+    column(0, "M1", "I1")
+    sums_in(0, "M0")
+    first(0, "M1")
+    hit(0, "WB")
+    column(0, "M0", "IN")
+    same(0, "M0")
+    seps(0, "M1")
+    scatter(T.RM[:], T.OL[:, 0:32], T.HT0[:], ["HT0", "RM", "OY0"], ["RM"])
+    merge("RM")
+    act(T.RG0[:], T.RM[:].indirect(T.OL[:, 32:64]), F.Copy, ["RM", "OY1"], ["RG0"], cyc=GATHER)
+    masked(1, "M0")
+    ops[-1]["ahead"] = EARLY
+    score("WB", [("PM", "W", 0, "W"), ("PM", "HT0", 0, "HT0"), ("PM", "ES", 0, "ES0")], True, False)
+    ops[-1]["ahead"] = EARLY
+    score("M1", [("PM", "W", 256, "W"), ("RV0", "RG0", 0, "RG0"), ("RY0", "RG0", 256, "RG0")], True, False)
+    ops[-1]["ahead"] = EARLY
+    for n in range(15, 30):
+        chunk(n)
 
-    def total(n):
-        t, i = chunks[n]
-        pos, neg = T.GG[:, 0:17:16], T.NG[:, 0:17:16]
-        ws, wc = (neg, pos) if n in SCAL else (pos, neg)
-        for b in range(8):
-            c = 256 * t + 32 * b + i
-            s0, c0 = 1024 * (n % NS) + 128 * b, 1024 * (n % NC) + 128 * b
-            mm(T.AT[:, c:c + 17:16], T.C[:, c0:c0 + 128], wc, True, False, ["C%d" % (n % NC), "GG", "NG"], "AT")
-            mm(T.AT[:, c:c + 17:16], T.SG[:, s0:s0 + 128], ws, False, True, ["SG%d%s" % (n % NS, "ab"[b // 4]), "GG", "NG"], "AT")
-
-    for step in late():
-        step()
-    end(0, 0)
-    end(0, 1)
-    for n in range(2, PRE):
-        match(n)
-        if n == 4:
-            ts(T.GG[:], T.JG[:], T.KF[:, 0:1], None, eq, None, ["JG", "KF"], ["GG"])
-            ts(T.NG[:], T.JG[:], T.KF[:, 0:1], -1.0, eq, mu, ["JG", "KF"], ["NG"])
-            ts(T.WD[:], T.JX[:], T.KF[:, 3:4], None, eq, None, ["JX", "KF3"], ["WD"])
-        if n == IDX:
-            index_out()
-        for j in range(2):
-            if n == MID[j]:
-                for h in range(2):
-                    middle(0, j, h, BANKS[2 * j + h])
-    for n in range(AHEAD):
-        if n in SCAL:
-            gather(n)
-    gather(0)
-    dist(0)
-    fold(0)
-    for n in range(1, LEAD):
-        if n in own:
-            gather(n)
-    clamp(0)
-
-    steps = {
-        1: [lambda: end(1, 0)],
-        2: [lambda: ts(T.W[:], T.WB[:], 0.5, 1.0, mu, A.min, ["WB"], ["W"])],
-        3: [index_in, lambda: end(1, 1)],
-        5: [lambda: middle(1, 0, 0, "M1"), lambda: middle(1, 0, 1, "WB"), lambda: cp(T.ML[:], T.M0[:, 0:32], ["M0"], ["ML"])],
-        7: [lambda: middle(1, 1, 0, "M1"), lambda: middle(1, 1, 1, "WB"), lambda: dist(1)],
-        10: [lambda: [band(T.GK[:, 128 * k:128 * k + 128], 128, [[0, 4], [-16, 2], [0, 16]], -32 * k, 16, 1.0, "GK%d" % k) for k in range(4)]],
-        13: [lambda: masked(0, "M0"), lambda: column(0, "M1", "I1")],
-        15: [lambda: sums_in(0, "M0")],
-        16: [lambda: first(0, "M1"), lambda: hit(0, "WB"), lambda: column(0, "M0", "IN")],
-        17: [lambda: same(0, "M0"), lambda: seps(0, "M1"),
-             lambda: cp(T.RM[:].indirect(T.OL[:, 0:32]), T.HT0[:], ["HT0", "RM", "OY0"], ["RM"]), lambda: merge("RM")],
-        22: [lambda: act(T.RG0[:], T.RM[:].indirect(T.OL[:, 32:64]), F.Copy, ["RM", "OY1"], ["RG0"]), lambda: sep_out(0)],
-        25: [lambda: masked(1, "M0"),
-             lambda: score("WB", [("PM", "W", 0, "W"), ("PM", "HT0", 0, "HT0"), ("PM", "ES", 0, "ES0")], True, False),
-             lambda: score("M1", [("PM", "W", 256, "W"), ("RV0", "RG0", 0, "RG0"), ("RY0", "RG0", 256, "RG0")], True, False)],
-    }
-    for n in range(30):
-        if n + AHEAD in SCAL:
-            gather(n + AHEAD)
-        if n + 1 < 30:
-            fold(n + 1)
-        if n + LEAD in own:
-            gather(n + LEAD)
-        if n + 1 < 30:
-            clamp(n + 1)
-        sign(n)
-        if PRE + n < 16:
-            match(PRE + n)
-        for step in steps.get(n, []):
-            step()
-        if n == 29:
-            column(1, "PB0a", "I1")
-            column(1, "PB0b", "IN")
-        total(n)
-
+    column(1, "PB0a", "I1")
+    column(1, "PB0b", "IN")
     sums_in(1, "M0")
     for k in range(4):
         mm(T.PB1[:, 256 * k:256 * k + 256], T.GK[:, 128 * k:128 * k + 128], T.OK[:], True, True, ["GK%d" % k, "OK"], BANKS[2 + k // 2])
-        if k == 1:
-            first(1, "PB0a")
+    first(1, "PB0a")
     act(T.HW[:, 16:528], T.PB1[:, 0:512], F.Sign, ["PB1a"], ["HWa"])
     ts(T.HW[:, 528:1040], T.PB1[:, 512:1024], 1.0, None, A.min, None, ["PB1b"], ["HWb"])
     hit(1, "AT")
     same(1, "PB0b")
     HK = ["HWp", "HWa", "HWb", "ML"]
-    act(T.RG1[:, 256:512], T.HW[:].indirect(T.ML[:, 16:32]), F.Copy, HK, ["RG1y"])
-    cp(T.RG1[:, 0:256], T.HW[:].indirect(T.ML[:, 0:16]), HK, ["RG1v"])
+    act(T.RG1[:, 256:512], T.HW[:].indirect(T.ML[:, 16:32]), F.Copy, HK, ["RG1y"], cyc=GATHER)
+    cp(T.RG1[:, 0:256], T.HW[:].indirect(T.ML[:, 0:16]), HK, ["RG1v"], GATHER)
     seps(1, "M0")
     score("M1", [("PM", "HT1", 0, "HT1"), ("PM", "ES", 256, "ES1")], False, True)
     score("WB", [("RY1", "RG1", 256, "RG1y"), ("RV1", "RG1", 0, "RG1v")], False, True)
     ts(T.FL[:, 256:512], T.M1[:, 0:256], 1.25, None, ge, None, ["M1"], ["FL1"])
     ts(T.FL[:, 0:256], T.WB[:, 0:256], 1.25, None, ge, None, ["WB"], ["FL0"])
-    send(others, {d: T.FL[:, 128 * d:128 * d + 128] for d in others}, T.FD[r], T.sem["fa%d" % r], ["FL0", "FL1"])
+    send(others, {d: T.FL[:, 128 * d:128 * d + 128] for d in others}, T.FD[r], T.sem["fa%d" % r], ["FL0", "FL1"], "sf")
     dma("s", [(T.yflag[lo:lo + 32, :], T.FL[:, 128 * r:128 * r + 128])], ["FL%d" % (r // 2)], ["yf%d" % r])
-    sep_out(1)
     for j, s in enumerate(near + far):
-        arrive("FR%d" % s, T.sem["fa%d" % s], inc[s])
-        dma("ys"[j % 2], [(T.yflag[32 * s:32 * s + 32, :], T.FD[s])], ["FR%d" % s], ["yf%d" % s])
+        arrive("FR%d" % s, T.sem["fa%d" % s], inc[s], "sf", 3.0 + 0.3 * j)
+        dma("sys"[j], [(T.yflag[32 * s:32 * s + 32, :], T.FD[s])], ["FR%d" % s], ["yf%d" % s])
 
-    wrote, read, deps = {}, {}, []
-    for n, o in enumerate(ops):
-        need = set()
-        for key in o["rd"]:
-            if key in wrote:
-                need.add(wrote[key])
-            if key in BANKS:
-                need.update(m for m in read.get(key, []) if ops[m]["q"] != o["q"])
-        for key in o["wr"]:
-            for m in read.get(key, []) + ([wrote[key]] if key in wrote else []):
-                if ops[m]["q"] != o["q"] or ops[m]["kind"] != "c" or o["kind"] != "c":
-                    need.add(m)
-        need.discard(n)
+    ops = arrange(ops, fixed)
+    for o in ops:
+        if "bank" in o:
+            o["wr"].append(o["bank"])
+    deps = []
+    for o, (raw, rest) in zip(ops, conflicts(ops)):
         last = {}
-        for m in need:
-            c = ops[m]["q"] if ops[m]["kind"] == "c" else ("own", m)
-            last[c] = max(last.get(c, -1), m)
+        for m in raw | rest:
+            if ops[m]["kind"] != "r" and o["kind"] != "x" and not ops[m]["q"] == o["q"] == "p":
+                c = ops[m]["q"] if ops[m]["kind"] == "c" else ("own", m)
+                last[c] = max(last.get(c, -1), m)
         deps.append(sorted(last.values()))
-        for key in o["wr"]:
-            wrote[key] = n
-            read[key] = []
-        for key in o["rd"]:
-            if key not in o["wr"]:
-                read.setdefault(key, []).append(n)
     marked = set(m for d in deps for m in d)
     queue = {"v": g.vector, "s": g.scalar, "p": g.tensor, "g": g, "y": g.sync}
     esem = {"v": "ev", "s": "es", "p": "ep", "g": "eg"}

@@ -1,16 +1,16 @@
+import math
 from concourse.bass import DstId, RemoteDMATransfer
 from concourse.mybir import AluOpType as A, ActivationFunctionType as F
 
 V, H = 2304, 1152.0
-NU, NC, NS, NK = 8, 8, 6, 16
-SCAL = tuple(range(3, 28, 2))
-ADDED = (4, 10, 18, 24)
-SPLIT = ()
-VEND = (0,)
+NS = 6
+PLAN = "v v s vv ss dd ss dd ss  s ss dd ss ss dd s s v h".split()
 CYC, GATHER, SCATTER = 0.00083, 1.56, 3.8
-XFAR, XNEAR, ADDMA, GUARD = 4.0, 2.5, 3.5, 0.3
-ENDS, HOLD, PEW = 2, 2.0, 2.0
-EARLY = 20.0
+XFAR, XNEAR, GUARD, ROUNDS = 4.0, 2.5, 0.3, 12
+ADDMA, HOLD, AHEAD = 2.0, 1.4, 2.0
+LOAD, LEAN, FIRST, SOON = 2.2, True, 3.0, 66.0
+EARLY, LATE, PRE = 16.0, 10.0, 16
+SHAKE, SLOWS, ROOM = 1.5, (0.7, 1.15), {"p": 1.3, "g": 1.2}
 
 
 def _sb(n, d="bfloat16"):
@@ -22,20 +22,20 @@ SCRATCH = {
     "SD0": ("dram", [4, 128, 16], "float32"), "SD1": ("dram", [4, 128, 16], "float32"),
     "FD": ("dram", [4, 128, 128], "bfloat16"),
     "X": _sb(V), "A32": _sb(576, "int32"), "A16": _sb(576, "float16"), "AW": _sb(V, "float32"),
-    "TQ": _sb(104, "int32"), "T32": _sb(128, "int32"), "VL": _sb(128, "uint16"), "YL": _sb(128, "uint16"),
+    "TQ": _sb(104, "int32"), "YL": _sb(128, "uint16"),
     "OL": _sb(64, "uint16"), "ML": _sb(32, "uint16"), "ZL": _sb(2048, "uint16"), "YO": _sb(32, "float16"),
     "CV": _sb(512, "float16"), "CY": _sb(512, "float16"), "T1": _sb(512, "float16"), "IG": _sb(512, "float16"),
-    "KI": _sb(1, "int32"), "KB": _sb(2, "int32"), "KF": _sb(4, "float32"),
+    "KI": _sb(1, "int32"), "KB": _sb(2, "int32"), "KF": _sb(5, "float32"), "JV": _sb(256, "float32"),
     "ZR": _sb(512), "J16": _sb(128), "JG": _sb(32), "JX": _sb(168),
     "SA": _sb(512), "SY": _sb(288), "SY4": _sb(144), "RK": _sb(512), "SQ": _sb(1152), "BC": _sb(2048),
     "I1": _sb(128), "IN": _sb(128), "I2": _sb(128), "GG": _sb(32), "NG": _sb(32), "G2": _sb(32), "GK": _sb(512), "WD": _sb(168),
-    "OG": _sb(128), "TR": _sb(128), "PM": _sb(128), "MY": _sb(128),
+    "OG": _sb(128), "TR": _sb(128), "PM": _sb(128), "PN": _sb(128), "P2": _sb(128), "P64": _sb(128), "MY": _sb(128),
     "RV0": _sb(128), "RY0": _sb(128), "RV1": _sb(128), "RY1": _sb(128),
-    "HV": _sb(2048), "HY": _sb(2048), "R": _sb(2048), "LO": _sb(2048), "DL": _sb(2048),
-    "EQ": _sb(1024), "EV": _sb(512), "EN": _sb(512), "W": _sb(512),
-    "U": _sb(1024 * NU), "UK": _sb(1024 * NK), "C": _sb(1024 * NC), "SG": _sb(1024 * NS),
+    "XV": _sb(1024), "XY": _sb(2048), "NP": _sb(1024), "LO": _sb(4096), "DL": _sb(4096),
+    "EQ": _sb(1024), "EV": _sb(512), "EN": _sb(512),
+    "U": _sb(1024 * 30), "C": _sb(1024 * 30), "SG": _sb(1024 * NS),
     "RM": _sb(V), "IM": _sb(V, "float32"), "IV": _sb(256, "float32"), "HW": _sb(1040),
-    "AB": _sb(256), "OK": _sb(256), "HT0": _sb(512), "HT1": _sb(256), "PR": _sb(256, "float16"), "ES": _sb(512),
+    "AB": _sb(256), "OK": _sb(256), "HT0": _sb(256), "HT1": _sb(256), "PR": _sb(256, "float16"), "ES": _sb(512),
     "RG0": _sb(512), "RG1": _sb(512), "SP0": _sb(16, "float32"), "SP1": _sb(16, "float32"), "FL": _sb(512),
     "PB0": ("psum", [128, 1024], "float32"), "PB1": ("psum", [128, 1024], "float32"),
     "AT": ("psum", [128, 512], "float32"), "WB": ("psum", [128, 512], "float32"),
@@ -78,29 +78,23 @@ def conflicts(ops):
     return out
 
 
-def arrange(ops, fixed):
-    before = [a | b for a, b in conflicts(ops)]
-    for n in range(1, fixed):
-        before[n].update(m for m in range(n) if ops[m]["q"] == ops[n]["q"])
+def place(ops, before, rank, fixed=0, back=False):
     after = [[] for _ in ops]
     for n, ms in enumerate(before):
         for m in ms:
             after[m].append(n)
-    way = [0.0] * len(ops)
-    for n in range(len(ops) - 1, -1, -1):
-        way[n] = ops[n]["us"] * (PEW if ops[n]["q"] == "p" else 1.0) + max([way[m] for m in after[n]] + [ops[n].get("ahead", 0.0)])
-    left, at = [len(ms) for ms in before], [0.0] * len(ops)
-    ready, free, order = {}, {}, []
+    left, at, start = [len(ms) for ms in before], [o.get("ahead", 0.0) * back for o in ops], [0.0] * len(ops)
+    ready, free = {}, {}
     for n, o in enumerate(ops):
         if not left[n]:
             ready.setdefault(o["q"], []).append(n)
-    while len(order) < len(ops):
+    for _ in ops:
         best = None
         for q, ns in ready.items():
             if ns:
                 t0 = max(free.get(q, 0.0), min(at[n] for n in ns))
-                n = max((n for n in ns if at[n] <= t0), key=lambda n: (way[n], -n))
-                soon = [m for m in ns if way[m] > way[n] and at[m] < t0 + GUARD * ops[n]["us"]]
+                n = max((n for n in ns if at[n] <= t0), key=lambda n: (rank[n], -n))
+                soon = [m for m in ns if rank[m] > rank[n] and at[m] < t0 + GUARD * ops[n]["us"]]
                 if soon:
                     n = min(soon, key=lambda m: at[m])
                 if best is None or max(t0, at[n]) < best[0]:
@@ -108,16 +102,48 @@ def arrange(ops, fixed):
         t, n = best
         o = ops[n]
         ready[o["q"]].remove(n)
-        order.append(o)
+        start[n] = t
         if o["q"]:
-            free[o["q"]] = t + o.get("hold", o["us"])
+            free[o["q"]] = t + o.get("hold", o["us"]) * (ROOM.get(o["q"], 1.0) if back else 1.0)
         for m in after[n]:
-            if m >= fixed or ops[m]["q"] != o["q"]:
-                at[m] = max(at[m], t + o["us"] + (0.0 if ops[m]["q"] == o["q"] == "p" else 0.06))
+            same = ops[m]["q"] == o["q"]
+            at[m] = max(at[m], t + (1e-6 if same and m < fixed else o["us"] + (0.0 if same and o["q"] == "p" else 0.06)) + o.get("lead", 0.0) * back)
             left[m] -= 1
             if not left[m]:
                 ready.setdefault(ops[m]["q"], []).append(m)
-    return order
+    return start, after
+
+
+def replay(ops, before, start, slow):
+    end, free = [0.0] * len(ops), {}
+    for n in sorted(range(len(ops)), key=lambda n: (start[n], n)):
+        o = ops[n]
+        t = max([free.get(o["q"], 0.0)] + [end[m] + (0.0 if ops[m]["q"] == o["q"] == "p" else 0.06) for m in before[n] if ops[m]["kind"] != "d" or o["kind"] != "d" or o["q"] == "g" or o["rd"]])
+        more = o["hold"] * (slow - 1) if o["q"] == "g" and o["kind"] == "d" else 0.0
+        end[n] = t + o["us"] + more
+        if o["q"]:
+            free[o["q"]] = t + o.get("hold", o["us"]) + more
+    return max(end)
+
+
+def arrange(ops, fixed):
+    before = [a | b for a, b in conflicts(ops)]
+    for n in range(1, fixed):
+        before[n].update(m for m in range(n) if ops[m]["q"] == ops[n]["q"])
+    start, after = place(ops, before, [-n for n in range(len(ops))], fixed)
+    best = None
+    for k in range(ROUNDS):
+        shake = [SHAKE * math.sin(12.9898 * n + 78.233 * k) for n in range(len(ops))]
+        back = place(ops, after, [t + o["us"] + d for t, o, d in zip(start, ops, shake)], 0, True)[0]
+        start = place(ops, before, [t + o["us"] + o.get("lead", 0.0) for t, o in zip(back, ops)], fixed)[0]
+        length = sum(replay(ops, before, start, slow) for slow in SLOWS)
+        if best is None or length < best[0]:
+            best = (length, start)
+        if k % 3 == 2:
+            start = best[1]
+    for t, o in zip(best[1], ops):
+        o["t"] = t
+    return [ops[n] for n in sorted(range(len(ops)), key=lambda n: (best[1][n], n))]
 
 
 def rank_program(g, core, T, topo):
@@ -133,7 +159,7 @@ def rank_program(g, core, T, topo):
 
     def op(q, fn, rd, wr, us, kind="c"):
         if q == "g" and kind == "c" and sent[0]:
-            rd, wr = list(rd) + ["pool"], list(wr) + ["pool"]
+            rd = list(rd) + ["xn"]
         ops.append({"q": q, "fn": fn, "rd": list(rd), "wr": list(wr), "kind": kind, "us": us})
 
     def vec(fn, ap, cyc, rd, wr):
@@ -163,14 +189,15 @@ def rank_program(g, core, T, topo):
     def mm(out, l, rh, st, sp, rd, bank):
         op("p", lambda: g.tensor.matmul(out, l, rh, st, sp), rd, [bank], CYC / 2 * max(64, out.shape[-1]))
 
-    def dma(q, pairs, rd, wr, us=2.5):
+    def dma(q, pairs, rd, wr, us=LOAD):
         e = g.sync if q == "y" else g.scalar
         op(q, lambda: [e.dma_start(o, a) for o, a in pairs], rd, wr, us, "d")
         ops[-1]["hold"] = 0.1 * len(pairs)
 
     def add(out, a, rd, key):
-        op("g", lambda: [g.dma_start(out, a, accum_op=ad)], rd, [key], ADDMA, "d")
-        ops[-1]["hold"] = HOLD
+        op("g", lambda: [g.dma_start(out, a, accum_op=ad)], rd, key, ADDMA + HOLD * out.shape[-1] / 1024, "d")
+        ops[-1]["hold"] = HOLD * out.shape[-1] / 1024
+        ops[-1]["lead"] = AHEAD
 
     def iota(out, pat, base, cm, wr):
         op("g", lambda: g.iota(out, pat, base, cm, allow_small_or_imprecise_dtypes=True), [], wr, 0.13 + 2 * CYC * out.shape[-1])
@@ -209,12 +236,11 @@ def rank_program(g, core, T, topo):
         return b[:, o + c:o + c + n]
 
     lo = 32 * r
-    dma("s", [(T.A32[:], T.adj[lo:lo + 32, :])], [], ["A32", "s0"], 3.0)
-    dma("y", [(T.TQ[32 * k:32 * k + 32, :], T.tv[lo:lo + 32, 8 * k:8 * k + 104]) for k in range(4)], [], ["TQ"], 3.5)
-    dma("s", [(T.XS[d], T.x[32 * d:32 * d + 32, :]) for d in far], [], ["XSf"], 4.0)
-    dma("y", [(T.XS[d], T.x[32 * d:32 * d + 32, :]) for d in near], [], ["XSn"], 4.5)
-    dma("y", [(T.T32[32 * k:32 * k + 32, :], T.tv[lo:lo + 32, :]) for k in range(4)], [], ["T32"], 5.0)
-    dma("y", [(T.X[lo:lo + 32, :], T.x[lo:lo + 32, :])], [], ["X%d" % r], 5.0)
+    dma("s", [(T.A32[:], T.adj[lo:lo + 32, :])], [], ["A32"], 2.3)
+    dma("y", [(T.TQ[32 * k:32 * k + 32, :], T.tv[lo:lo + 32, 8 * k:8 * k + 104]) for k in range(4)], [], ["TQ"], 3.0)
+    dma("s", [(T.XS[d], T.x[32 * d:32 * d + 32, :]) for d in far], [], ["XSf"], 3.2)
+    dma("y", [(T.XS[d], T.x[32 * d:32 * d + 32, :]) for d in near], [], ["XSn"], 3.5)
+    dma("y", [(T.X[lo:lo + 32, :], T.x[lo:lo + 32, :])], [], ["X%d" % r], 4.0)
     zero(T.ZR[:], "ZR")
     op("g", lambda: g.iota(T.KI[:], [[0, 1]], 0, 1), [], ["KI"], 0.13)
     iota(T.J16[:], [[-16, 8], [0, 16]], 0, 1, ["J16"])
@@ -225,12 +251,14 @@ def rank_program(g, core, T, topo):
     fixed = len(ops)
     send(far, T.XS, T.XL[r], T.sem["xa%d" % r], ["XSf"], "xf")
     send(near, T.XS, T.XL[r], T.sem["xa%d" % r], ["XSn", "xf"], "xn")
+    iota(T.JV[:], [[1, 256]], 16, 0, ["JV"])
+    ops[-1]["rd"].append("xn")
     mark(T.RK[:], 512, [[-32, 4], [0, 4], [-1, 32]], 0, 1.0, "RK")
+    ops[-1]["rd"].append("xn")
+    mark(T.PM[:], 128, [[-16, 2], [-1, 16], [-32, 4]], 0, 1.0, "PM")
     ops[-1]["rd"].append("xn")
     iota(T.JG[:], [[1, 2], [0, 16]], 0, 0, ["JG"])
     iota(T.JX[:], [[1, 168]], -39, 0, ["JX"])
-    for k in range(4):
-        iota(T.IV[32 * k:32 * k + 32, :], [[1, 256]], 16 + 256 * k, 0, ["IV%d" % k])
     for s in near + far:
         arrive("XL%d" % s, T.sem["xa%d" % s], inc[s], "xn" if s in near else "xf", XNEAR if s in near else XFAR)
         dma("y", [(T.X[32 * s:32 * s + 32, :], T.XL[s])], ["XL%d" % s], ["X%d" % s])
@@ -243,6 +271,8 @@ def rank_program(g, core, T, topo):
     cp(T.KF[:, 0:2], T.KB[:], ["KB0", "KB1"], ["KF"])
     ts(T.KF[:, 2:3], T.KF[:, 1:2], 8.0, None, mu, None, ["KF"], ["KF2"])
     ts(T.KF[:, 3:4], T.KF[:, 0:1], 64.0, T.KF[:, 2:3], mu, ad, ["KF", "KF2"], ["KF3"])
+    ts(T.KF[:, 4:5], T.KF[:, 1:2], 256.0, None, mu, None, ["KF"], ["KF4"])
+    act(T.IV[:], T.JV[:], F.Identity, ["JV", "KF4"], ["IV"], bias=T.KF[:, 4:5])
     for j in range(16):
         ts(T.BC[:, 128 * j:128 * j + 128], T.J16[:], float(j), None, eq, None, ["J16"], ["BC%d" % j], 0.5)
     ts(T.GG[:], T.JG[:], T.KF[:, 0:1], None, eq, None, ["JG", "KF"], ["GG"])
@@ -263,12 +293,13 @@ def rank_program(g, core, T, topo):
         else:
             cp(T.AW[:, 288 * j:288 * j + 288], reg(BANKS[j], 288), [BANKS[j]], ["AW%d" % j])
     AWK = ["AW%d" % j for j in range(8)]
-    for name, sc in (("IN", -1.0), ("I2", 2.0)):
-        act(T[name][:], T.I1[:], F.Copy, ["I1"], [name], scale=sc)
+    for name, src, sc in (("IN", "I1", -1.0), ("I2", "I1", 2.0), ("PN", "PM", -1.0), ("P2", "PM", 2.0), ("P64", "PM", 64.0)):
+        act(T[name][:], T[src][:], F.Copy, [src], [name], scale=sc)
     act(T.SQ[:, 384:640], T.SQ[:, 128:384], F.Copy, ["SQ0"], ["SQ1"])
     act(T.SQ[:, 640:1152], T.SQ[:, 128:640], F.Copy, ["SQ0", "SQ1"], ["SQ2"])
-    for name in ("IM", "RM"):
-        act(T[name][:], T.AW[:], F.Copy, AWK, [name], scale=0.0)
+    for j in range(5):
+        n = min(512, V - 512 * j)
+        act(T.IM[:, 512 * j:512 * j + n], T.ZR[:, 0:n], F.Copy, ["ZR"], ["IM%d" % j])
     for t in range(2):
         cp(T.CV[:, 256 * t:256 * t + 256], T.AW[:].indirect(T.OL[:, 32 * t:32 * t + 16]), AWK + ["OV%d0" % t, "OV%d1" % t], ["CV%d" % t], GATHER)
         bk = "M%d" % t
@@ -280,7 +311,6 @@ def rank_program(g, core, T, topo):
         cp(T.CY[:, 256 * t:256 * t + 256], T.AW[:].indirect(T.OL[:, 32 * t + 16:32 * t + 32]), AWK + ["OY%d" % t], ["CY%d" % t], GATHER)
         cp(T.YO[:, 16 * t:16 * t + 16], T["M%d" % t][:, 0:16], ["M%d" % t], ["YO%d" % t])
     CK = ["CY0", "CY1"]
-    cp(T.VL[:], T.T32[:], ["T32"], ["VL"])
     for c in range(4):
         for k in range(4):
             mm(T.WB[:, 32 * c + 8 * k:32 * c + 8 * k + 8], T.RK[:, 128 * k:128 * k + 128], T.YO[:, 8 * c:8 * c + 8], True, True,
@@ -289,9 +319,9 @@ def rank_program(g, core, T, topo):
     for t in range(2):
         for h in range(2):
             for k in range(4):
-                mm(T.AT[:, 8 * t + 4 * h + k:512:16], T.CY[:, 256 * t + 128 * h:256 * t + 128 * h + 128], T.I1[:, 32 * k:32 * k + 32], True, True,
-                   ["CY%d" % t, "I1"], "AT")
-    cp(T.T1[:], T.AT[:], ["AT"], ["T1"])
+                mm(T.AT[:, 256 * t + 4 * h + k:256 * t + 256:8], T.CY[:, 256 * t + 128 * h:256 * t + 128 * h + 128], T.I1[:, 32 * k:32 * k + 32],
+                   True, True, ["CY%d" % t, "I1"], "AT")
+        cp(T.T1[:, 256 * t:256 * t + 256], T.AT[:, 256 * t:256 * t + 256], ["AT"], ["T1%d" % t])
     mm(T.AT[:], T.ZR[:, 0:128], T.ZR[:], True, True, ["ZR"], "AT")
     ops[-1]["wr"].append("A0")
     SQK = ["SQp"] + ["SQ%d" % k for k in range(3)]
@@ -299,15 +329,15 @@ def rank_program(g, core, T, topo):
         b, o = bank(j)
         for q in range(8):
             for gr in range(2):
-                c = 128 * (1 - gr) + q
-                mm(b[:, o + q:o + 512:8], T.SQ[:, c:c + 1017:8], T.T1[:, 256 * gr + 64 * j:256 * gr + 64 * j + 64], gr == 0, gr == 1,
-                   SQK + ["T1"], BANKS[j])
+                c, c1 = 128 * (1 - gr) + q, 256 * (j // 2) + 128 * gr + 64 * (j % 2)
+                mm(b[:, o + q:o + 512:8], T.SQ[:, c:c + 1017:8], T.T1[:, c1:c1 + 64], gr == 0, gr == 1, SQK + ["T1%d" % (j // 2)], BANKS[j])
     for j in range(2):
         ts(T.ZL[:, 1024 * j:1024 * j + 1024], T["PB%d" % j][:], H, float(V - 1), ad, A.min, ["PB%da" % j, "PB%db" % j], ["ZL%d" % j])
 
     ts(T.EN[:], T.CY[:], H, 64.0, eq, mu, CK, ["EN"], 0.5)
-    mm(T.WB[:], T.IN[:], T.EN[:], True, False, ["IN", "EN"], "WB")
-    for n in range(16):
+    mm(T.WB[:], T.PN[:], T.EN[:], True, False, ["PN", "EN"], "WB")
+
+    def match(n):
         bk = "M%d" % (n % 2)
         if n >= 2:
             mm(T[bk][:], T.BC[:, 128 * n:128 * n + 128], T.CV[:], True, True, ["BC%d" % n, "CV0", "CV1"], bk)
@@ -319,39 +349,42 @@ def rank_program(g, core, T, topo):
         out, key = (T.EV[:], "EV") if n == 0 else (T.EQ[:, 512 * (n % 2):512 * (n % 2) + 512], "EQ%d" % (n % 2))
         tt(out, T[bk][:], T.CY[:], eq, [bk] + CK, [key])
         if n > 0:
-            wn = "I1" if n == 1 else "I2"
-            mm(T.WB[:], T[wn][:], out, False, n == 15, [wn, key], "WB")
-    ts(T.W[:], T.WB[:], 0.5, 1.0, mu, A.min, ["WB"], ["W"])
+            wn = "PM" if n == 1 else "P2"
+            mm(T.WB[:], T[wn][:], out, False, False, [wn, key], "WB")
 
-    def ends(t, banks):
-        if t in VEND:
-            c = 1024 * t
-            for j, (out, lst) in enumerate(((T.HV, "VL"), (T.HY, "YL"))):
-                act(out[:, c:c + 1024], T.X[:].indirect(T[lst][:, 64 * t:64 * t + 64]), F.Copy, XK + [lst], ["H%d%d" % (t, j)], cyc=GATHER)
-            tt(T.LO[:, c:c + 1024], T.X[:].indirect(T.YL[:, 64 * t:64 * t + 64]), T.HV[:, c:c + 1024], A.min, XK + ["YL", "H%d0" % t],
-               ["LO%d0" % t, "LO%d1" % t], GATHER)
-            for h, bk in enumerate(banks[0:2]):
-                for m, (wn, src, key) in enumerate([("IN", T.HV, "H%d0" % t), ("IN", T.HY, "H%d1" % t), ("I2", T.LO, "LO%d0" % t)]):
-                    mm(reg(bk, 512), T[wn][:], src[:, c + 512 * h:c + 512 * h + 512], m == 0, m == 2, [wn, key], bk)
-            ts(T.DL[:, c:c + 1024], T[banks[0][:3]][:], -0.5, None, A.min, None, banks[0:2], ["DL%d" % t])
-            return
-        for c, (out, lst) in enumerate(((T.HV, "VL"), (T.HY, "YL"))):
-            o, z = out[:, 1024 * t:1024 * t + 1024], T.X[:].indirect(T[lst][:, 64 * t:64 * t + 64])
-            act(o, z, F.Copy, XK + [lst], ["H%d%d" % (t, c)], scale=0.5, cyc=GATHER)
-        for j in range(2):
-            for h in range(2):
-                c, bk = 1024 * t + 512 * h, banks[2 * j + h]
-                terms = [("I1", T.HV, "H%d0" % t), ("IN", T.HY, "H%d1" % t)] if j == 0 else \
-                        [("I1", T.HV, "H%d0" % t), ("I1", T.HY, "H%d1" % t), ("IN", T.R, "R%d%d" % (t, h))]
-                for m, (wn, src, key) in enumerate(terms):
-                    mm(reg(bk, 512), T[wn][:], src[:, c:c + 512], m == 0, m == len(terms) - 1, [wn, key], bk)
-                out, f = (("R", F.Abs), ("LO", F.Copy))[j]
-                if t == 0:
-                    act(T[out][:, c:c + 512], reg(bk, 512), f, [bk], ["%s%d%d" % (out, t, h)])
-            if t == 1:
-                act(T[out][:, 1024:2048], T[bk[:3]][:], f, banks[2 * j:2 * j + 2], [out + "10", out + "11"])
-        c = 1024 * t
-        ts(T.DL[:, c:c + 1024], T.R[:, c:c + 1024], -2.0, -0.5, mu, A.min, ["R%d0" % t, "R%d1" % t], ["DL%d" % t], 0.5)
+    for n in range(PRE):
+        match(n)
+
+    def ends(t):
+        xv, xy = T.X[:].indirect(T.ZL[:, 1088 * t:1088 * t + 64]), T.X[:].indirect(T.YL[:, 64 * t:64 * t + 64])
+        low, dist, y = T.LO[:, 2048 * t:2048 * t + 1024], T.DL[:, 2048 * t:2048 * t + 1024], T.XY[:, 1024 * t:1024 * t + 1024]
+        if t == 0:
+            act(T.XV[:], xv, F.Copy, XK + ["ZL0"], ["XV"], cyc=GATHER)
+            tt(low, xy, T.XV[:], A.min, XK + ["YL", "XV"], ["LO0"], GATHER)
+            ops[-1]["lead"] = FIRST
+            act(y, xy, F.Copy, XK + ["YL"], ["XY0"], cyc=GATHER)
+            for h, bk in enumerate(BANKS[0:2]):
+                for m, (wn, src, key) in enumerate([("IN", T.XV, "XV"), ("IN", T.XY, "XY0"), ("I2", T.LO, "LO0")]):
+                    mm(reg(bk, 512), T[wn][:], src[:, 512 * h:512 * h + 512], m == 0, m == 2, [wn, key], bk)
+            ts(dist, T.PB0[:], -0.5, None, A.min, None, BANKS[0:2], ["DL0"])
+        else:
+            act(low, xv, F.Copy, XK + ["ZL1"], ["LO1"], cyc=GATHER)
+            if LEAN:
+                tt(y, xy, low, A.subtract, XK + ["YL", "LO1"], ["XY1"], GATHER)
+                ts(T.NP[:], y, 0.0, None, A.min, None, ["XY1"], ["NP"], 0.5)
+                add(low, T.NP[:], ["LO1", "NP"], ["LO1"])
+                act(dist, y, F.Abs, ["XY1"], ["DL1"])
+                ts(dist, dist, -1.0, -0.5, mu, A.min, ["DL1"], ["DL1"], 0.5)
+            else:
+                act(y, xy, F.Copy, XK + ["YL"], ["XY1"], scale=-1.0, cyc=GATHER)
+                add(y, low, ["XY1", "LO1"], ["XY1"])
+                ts(T.NP[:], y, 0.0, -1.0, A.max, mu, ["XY1"], ["NP"], 0.5)
+                add(low, T.NP[:], ["LO1", "NP"], ["LO1"])
+                add(y, T.NP[:], ["XY1", "NP"], ["XY1"])
+                add(y, T.NP[:], ["XY1", "NP"], ["XY1"])
+                ts(dist, y, -0.5, None, A.min, None, ["XY1"], ["DL1"], 0.5)
+        for name, src in (("LO", low), ("DL", dist)):
+            dma("y", [(T[name][:, 2048 * t + 1024:2048 * t + 2048], src)], ["%s%d" % (name, t)], ["%s%d+" % (name, t)])
 
     def merge(name):
         dma("y", [(T[name][16 * gr + k:128:32, :], T[name][32 * k + 16 * gr + 8:32 * k + 16 * gr + 12, :]) for k in range(4) for gr in range(2)],
@@ -359,7 +392,10 @@ def rank_program(g, core, T, topo):
 
     def index():
         for c in range(2):
-            scatter(T.IM[:], T.OL[:, 32 + 16 * c:48 + 16 * c], T.IV[:], ["IM", "OV10", "OV11", "OY1"] + ["IV%d" % k for k in range(4)], ["IM"])
+            op("s", lambda c=c: g.scalar.activation(T.IM[:].indirect(T.OL[:, 32 + 16 * c:48 + 16 * c]), T.IV[:], F.Silu),
+               ["IV", "IM", "OV10", "OV11", "OY1"][:4 + c] + ["IM%d" % j for j in range(5)], ["IM"],
+               0.065 + 256 * CYC * SCATTER + 1.3 * (1 - c))
+            ops[-1]["ahead"] = SOON
         merge("IM")
         cp(T.IG[:], T.IM[:].indirect(T.OL[:, 0:32]), ["IM", "OY0"], ["IG"], GATHER)
         for p in range(16):
@@ -372,12 +408,13 @@ def rank_program(g, core, T, topo):
     select(T.TR[:], T.TR[:], [[1, 128]], ge, 0.0, 0, -1, ["TR"], "TR")
     select(T.TR[:], T.TR[:], [[1, 128]], ne, -4096.0, 0, -1, ["TR"], "TR")
     band(T.SY4[:], 144, [[-16, 9], [128, 16]], -128 * 15, 4, 1.0, "SY4")
-    mark(T.PM[:], 128, [[-16, 2], [-1, 16], [-32, 4]], 0, 1.0, "PM")
+    for j in range(4):
+        iota(T.RM[:, 576 * j:576 * j + 576], [[0, 576]], 0, 0, ["RM%d" % j])
     band(T.MY[:], 128, [[-16, 8], [128, 16]], 0, 4, 1.0, "MY")
-    band(T.RV0[:], 128, turn, 0, 4, -0.5, "RV0")
-    band(T.RY0[:], 128, row, 0, 4, -1.0, "RY0")
-    mark(T.RV1[:], 128, turn, 0, -0.5, "RV1")
-    mark(T.RY1[:], 128, row, -128, -1.0, "RY1")
+    band(T.RV0[:], 128, turn, 0, 4, -1.0, "RV0")
+    band(T.RY0[:], 128, row, 0, 4, -64.0, "RY0")
+    mark(T.RV1[:], 128, turn, 0, -1.0, "RV1")
+    mark(T.RY1[:], 128, row, -128, -64.0, "RY1")
     for k in range(4):
         band(T.GK[:, 128 * k:128 * k + 128], 128, [[0, 4], [-16, 2], [0, 16]], -32 * k, 16, 1.0, "GK%d" % k)
 
@@ -403,9 +440,8 @@ def rank_program(g, core, T, topo):
         ts(T.PR[:], reg(bp, 256), 4096.0, H, ad, A.min, [bp], ["PR"])
 
     def hit(t, bh):
-        for h in range(2 - t):
-            mm(reg(bh, 256, 256 * h), T.OG[:], T.OK[:], True, True, ["OG", "OK"], bh)
-        act(T["HT%d" % t][:], reg(bh, 512 - 256 * t), F.Sign, [bh], ["HT%d" % t])
+        mm(reg(bh, 256), T.OG[:], T.OK[:], True, True, ["OG", "OK"], bh)
+        act(T["HT%d" % t][:], reg(bh, 256), F.Sign, [bh], ["HT%d" % t])
 
     def same(t, bb):
         mm(reg(bb, 256), T.OG[:], T.PR[:], False, True, ["OG", "PR"], bb)
@@ -419,88 +455,101 @@ def rank_program(g, core, T, topo):
         act(sp[:], reg(bs, 16), F.Identity, [bs], ["SP%d" % t], bias=-14 * H)
         send(others, {d: sp[:] for d in others}, sd[r], T.sem["sa%d" % t], ["SP%d" % t], "ss%d" % t)
         dma("y", [(sd[r], sp[:])], ["SP%d" % t], ["SO%d" % t])
-        arrive("SR%d" % t, T.sem["sa%d" % t], sum(inc.values()), "ss%d" % t, 3.0 + 5 * (1 - t))
+        arrive("SR%d" % t, T.sem["sa%d" % t], sum(inc.values()), "ss%d" % t, 2.5 + 5 * (1 - t))
         dma("y", [(T.ysep[:, 1024 * t:1024 * t + 1024], sd[:])], ["SO%d" % t, "SR%d" % t], ["ys%d" % t])
-        ops[-1]["ahead"] = EARLY if t == 0 else 2.0
+        ops[-1]["ahead"] = EARLY if t == 0 else 1.0
 
-    def score(bk, terms, st, sp):
-        for m, (wn, src, c, key) in enumerate(terms):
-            mm(reg(bk, 256), T[wn][:], T[src][:, c:c + 256], st and m == 0, sp and m == len(terms) - 1, [wn, key], bk)
+    def score(terms, sp):
+        for m, (t, wn, src, c, key) in enumerate(terms):
+            mm(reg("WB", 256, 256 * t), T[wn][:], T[src][:, c:c + 256], False, sp and m == len(terms) - 1, [wn, key], "WB")
 
     chunks = [(t, i) for t in range(2) for i in range(16) if i != t]
-    own = [n for n in range(30) if n not in SCAL]
+    pos, neg, two = T.GG[:, 0:17:16], T.NG[:, 0:17:16], T.G2[:, 0:17:16]
+    jobs = [0]
 
-    def chunk(n):
+    def sums(n, h, sg, s0, key, wc, ws):
         t, i = chunks[n]
-        z, low = T.X[:].indirect(T.ZL[:, 128 * i + 64 * t:128 * i + 64 * t + 64]), T.LO[:, 1024 * t:1024 * t + 1024]
-        lk, pos, neg = ["LO%d0" % t, "LO%d1" % t], T.GG[:, 0:17:16], T.NG[:, 0:17:16]
-        if n in SCAL:
-            u, c, key, wn, ws, wc = T.UK, 1024 * SCAL.index(n), "UK%d" % n, "IN", neg, pos
-            act(u[:, c:c + 1024], z, F.Copy, XK + ["ZL%d" % (i // 8)], [key], scale=-1.0, cyc=GATHER)
-            add(u[:, c:c + 1024], low, [key] + lk, key)
+
+        def fn():
+            for b in range(4 * h, 4 * h + 4):
+                a = T.AT[:, 256 * t + 32 * b + i:256 * t + 32 * b + i + 17:16]
+                g.tensor.matmul(a, T.C[:, 1024 * n + 128 * b:1024 * n + 128 * b + 128], wc, True, False)
+                last = g.tensor.matmul(a, sg[:, s0 + 128 * b:s0 + 128 * b + 128], ws, False, True)
+            return last
+        op("p", fn, ["C%d" % n, key, "GG", "NG", "G2", "A0"], ["A%d%d" % (n, h)], 4 * 64 * CYC)
+        ops[-1]["bank"] = "AT"
+
+    def unit(n0, kind):
+        (t, i), w, kind = chunks[n0], len(kind), kind[0]
+        keys, more = ["U%d" % n for n in range(n0, n0 + w)], "+" * (w - 1)
+        u, z = T.U[:, 1024 * n0:1024 * (n0 + w)], T.X[:].indirect(T.ZL[:, 1024 * t + 64 * i:1024 * t + 64 * (i + w)])
+        low, lk = T.LO[:, 2048 * t:2048 * t + 1024 * w], ["LO%d" % t, "LO%d" % t + more]
+        if kind == "s":
+            act(u, z, F.Copy, XK + ["ZL%d" % t], keys, scale=-1.0, cyc=GATHER)
+            add(u, low, keys + lk, keys)
         else:
-            u, c, key, wn, ws, wc = T.U, 1024 * (own.index(n) % NU), "U%d" % (own.index(n) % NU), "I1", pos, neg
-            tt(u[:, c:c + 1024], z, low, A.subtract, XK + ["ZL%d" % (i // 8)] + lk, [key], GATHER)
-        pb = "PB%d" % (len([m for m in range(n) if m not in ADDED]) % 2)
-        c0, ck, s0, sk = 1024 * (n % NC), "C%d" % (n % NC), 1024 * (n % NS), "SG%d" % (n % NS)
-        ts(T.C[:, c0:c0 + 1024], u[:, c:c + 1024], -1.0, 1.0, A.max, A.min, [key], [ck], 0.5)
-        ws = [ws, ws]
-        if n in ADDED:
-            add(u[:, c:c + 1024], T.DL[:, 1024 * t:1024 * t + 1024], [key, "DL%d" % t], key)
-            ts(T.SG[:, s0:s0 + 1024], u[:, c:c + 1024], -0.5, 0.5, A.max, A.min, [key], [sk + "a", sk + "b"], 0.5)
-            ws = [T.G2[:, 0:17:16]] * 2
+            tt(u, z, low, A.subtract, XK + ["ZL%d" % t] + lk, keys, GATHER)
+        if kind == "w":
+            act(T.C[:, 1024 * n0:1024 * (n0 + w)], u, F.Sign, keys, ["C%d" % n for n in range(n0, n0 + w)])
         else:
+            ts(T.C[:, 1024 * n0:1024 * (n0 + w)], u, -1.0, 1.0, A.max, A.min, keys, ["C%d" % n for n in range(n0, n0 + w)], 0.5)
+        if kind == "d":
+            add(u, T.DL[:, 2048 * t:2048 * t + 1024 * w], keys + ["DL%d" % t, "DL%d" % t + more], keys)
+            ts(u, u, -0.5, 0.5, A.max, A.min, keys, keys, 0.5)
+        for n in range(n0, n0 + w):
+            if kind == "d":
+                for h in range(2):
+                    sums(n, h, T.U, 1024 * n, "U%d" % n, neg, two)
+                continue
+            pb, s0, sk = "PB%d" % (jobs[0] % 2), 1024 * (jobs[0] % NS), "SG%d" % (jobs[0] % NS)
+            jobs[0] += 1
+            wn, wc, ws = ("IN", pos, neg) if kind == "s" else ("I1", neg, pos)
             for h, bk in enumerate((pb + "a", pb + "b")):
-                mm(reg(bk, 512), T.I1[:], u[:, c + 512 * h:c + 512 * h + 512], True, False, ["I1", key], bk)
-                mm(reg(bk, 512), T[wn][:], T.DL[:, 1024 * t + 512 * h:1024 * t + 512 * h + 512], False, True, [wn, "DL%d" % t], bk)
-            if n in SPLIT:
+                mm(reg(bk, 512), T.I1[:], T.U[:, 1024 * n + 512 * h:1024 * n + 512 * h + 512], True, False, ["I1", "U%d" % n], bk)
+                mm(reg(bk, 512), T[wn][:], T.DL[:, 2048 * t + 512 * h:2048 * t + 512 * h + 512], False, True, [wn, "DL%d" % t], bk)
+            if kind == "h":
                 act(T.SG[:, s0:s0 + 512], T[pb][:, 0:512], F.Sign, [pb + "a"], [sk + "a"])
                 ts(T.SG[:, s0 + 512:s0 + 1024], T[pb][:, 512:1024], -0.5, 0.5, A.max, A.min, [pb + "b"], [sk + "b"])
-                ws[1] = T.G2[:, 0:17:16]
             else:
                 act(T.SG[:, s0:s0 + 1024], T[pb][:], F.Sign, [pb + "a", pb + "b"], [sk + "a", sk + "b"])
-        for h in range(2):
-            def sums(h=h):
-                for b in range(4 * h, 4 * h + 4):
-                    a = 256 * t + 32 * b + i
-                    g.tensor.matmul(T.AT[:, a:a + 17:16], T.C[:, c0 + 128 * b:c0 + 128 * b + 128], wc, True, False)
-                    last = g.tensor.matmul(T.AT[:, a:a + 17:16], T.SG[:, s0 + 128 * b:s0 + 128 * b + 128], ws[h], False, True)
-                return last
-            op("p", sums, [ck, sk + "ab"[h], "GG", "NG", "G2", "A0"], ["A%d%d" % (n, h)], 4 * 64 * CYC)
-            ops[-1]["bank"] = "AT"
+            for h in range(2):
+                sums(n, h, T.SG, s0, sk + "ab"[h], wc, two if kind == "h" and h else ws)
 
-    ends(0, list(BANKS[0:4]))
+    starts = [sum(len(k) for k in PLAN[:j]) for j in range(len(PLAN))]
+    ends(0)
+    ends(1)
     index()
-    for n in range(15):
-        if n == ENDS:
-            ends(1, list(BANKS[0:4]))
-        chunk(n)
+    for n0, kind in zip(starts, PLAN):
+        if n0 < 15:
+            unit(n0, kind)
     masked(0, "M0")
     column(0, "M1", "I1")
     sums_in(0, "M0")
     first(0, "M1")
-    hit(0, "WB")
+    hit(0, "M0")
     column(0, "M0", "IN")
     same(0, "M0")
     seps(0, "M1")
-    scatter(T.RM[:], T.OL[:, 0:32], T.HT0[:], ["HT0", "RM", "OY0"], ["RM"])
+    for c in range(2):
+        scatter(T.RM[:], T.OL[:, 16 * c:16 * c + 16], T.HT0[:], ["HT0", "RM", "OY0"] + ["RM%d" % j for j in range(4)], ["RM"])
     merge("RM")
     act(T.RG0[:], T.RM[:].indirect(T.OL[:, 32:64]), F.Copy, ["RM", "OY1"], ["RG0"], cyc=GATHER)
+    for n in range(PRE, 16):
+        match(n)
     masked(1, "M0")
-    ops[-1]["ahead"] = EARLY
-    score("WB", [("PM", "W", 0, "W"), ("PM", "HT0", 0, "HT0"), ("PM", "ES", 0, "ES0")], True, False)
-    ops[-1]["ahead"] = EARLY
-    score("M1", [("PM", "W", 256, "W"), ("RV0", "RG0", 0, "RG0"), ("RY0", "RG0", 256, "RG0")], True, False)
-    ops[-1]["ahead"] = EARLY
-    for n in range(15, 30):
-        chunk(n)
+    ops[-1]["ahead"] = LATE
+    score([(0, "P64", "HT0", 0, "HT0"), (0, "P64", "ES", 0, "ES0"), (1, "RV0", "RG0", 0, "RG0"), (1, "RY0", "RG0", 256, "RG0")], False)
+    ops[-1]["ahead"] = LATE
+    column(1, "M1", "I1")
+    for n0, kind in zip(starts, PLAN):
+        if n0 >= 15:
+            unit(n0, kind)
 
-    column(1, "PB0a", "I1")
     column(1, "PB0b", "IN")
     sums_in(1, "M0")
     for k in range(4):
         mm(T.PB1[:, 256 * k:256 * k + 256], T.GK[:, 128 * k:128 * k + 128], T.OK[:], True, True, ["GK%d" % k, "OK"], BANKS[2 + k // 2])
-    first(1, "PB0a")
+    first(1, "M1")
     act(T.HW[:, 16:528], T.PB1[:, 0:512], F.Sign, ["PB1a"], ["HWa"])
     ts(T.HW[:, 528:1040], T.PB1[:, 512:1024], 1.0, None, A.min, None, ["PB1b"], ["HWb"])
     hit(1, "AT")
@@ -509,14 +558,12 @@ def rank_program(g, core, T, topo):
     act(T.RG1[:, 256:512], T.HW[:].indirect(T.ML[:, 16:32]), F.Copy, HK, ["RG1y"], cyc=GATHER)
     cp(T.RG1[:, 0:256], T.HW[:].indirect(T.ML[:, 0:16]), HK, ["RG1v"], GATHER)
     seps(1, "M0")
-    score("M1", [("PM", "HT1", 0, "HT1"), ("PM", "ES", 256, "ES1")], False, True)
-    score("WB", [("RY1", "RG1", 256, "RG1y"), ("RV1", "RG1", 0, "RG1v")], False, True)
-    ts(T.FL[:, 256:512], T.M1[:, 0:256], 1.25, None, ge, None, ["M1"], ["FL1"])
-    ts(T.FL[:, 0:256], T.WB[:, 0:256], 1.25, None, ge, None, ["WB"], ["FL0"])
-    send(others, {d: T.FL[:, 128 * d:128 * d + 128] for d in others}, T.FD[r], T.sem["fa%d" % r], ["FL0", "FL1"], "sf")
-    dma("s", [(T.yflag[lo:lo + 32, :], T.FL[:, 128 * r:128 * r + 128])], ["FL%d" % (r // 2)], ["yf%d" % r])
+    score([(1, "P64", "HT1", 0, "HT1"), (1, "P64", "ES", 256, "ES1"), (0, "RY1", "RG1", 256, "RG1y"), (0, "RV1", "RG1", 0, "RG1v")], True)
+    ts(T.FL[:], T.WB[:], 64.5, None, ge, None, ["WB"], ["FL"])
+    send(others, {d: T.FL[:, 128 * d:128 * d + 128] for d in others}, T.FD[r], T.sem["fa%d" % r], ["FL"], "sf")
+    dma("s", [(T.yflag[lo:lo + 32, :], T.FL[:, 128 * r:128 * r + 128])], ["FL"], ["yf%d" % r])
     for j, s in enumerate(near + far):
-        arrive("FR%d" % s, T.sem["fa%d" % s], inc[s], "sf", 3.0 + 0.3 * j)
+        arrive("FR%d" % s, T.sem["fa%d" % s], inc[s], "sf", 2.5 + 0.2 * j)
         dma("sys"[j], [(T.yflag[32 * s:32 * s + 32, :], T.FD[s])], ["FR%d" % s], ["yf%d" % s])
 
     ops = arrange(ops, fixed)

import math
from concourse.bass import DstId, RemoteDMATransfer
from concourse.mybir import AluOpType as A, ActivationFunctionType as F

V, H = 2304, 1152.0
NS = 6
PLAN = "v v s vv ss dd ss dd ss  s ss dd ss ss dd s s v h".split()
CYC, GATHER, SCATTER = 0.00083, 1.56, 3.8
XFAR, XNEAR, GUARD, ROUNDS = 4.0, 2.5, 0.3, 12
ADDMA, HOLD, AHEAD = 2.0, 1.4, 2.0
LOAD, LEAN, FIRST, SOON = 2.2, True, 3.0, 66.0
EARLY, LATE, PRE = 16.0, 10.0, 16
SHAKE, SLOWS, ROOM = 1.5, (0.7, 1.15), {"p": 1.3, "g": 1.2}


def _sb(n, d="bfloat16"):
    return ("sbuf", [128, n], d)


SCRATCH = {
    "XS": ("dram", [4, 128, 576], "bfloat16"), "XL": ("dram", [4, 128, 576], "bfloat16"),
    "SD0": ("dram", [4, 128, 16], "float32"), "SD1": ("dram", [4, 128, 16], "float32"),
    "FD": ("dram", [4, 128, 128], "bfloat16"),
    "X": _sb(V), "A32": _sb(576, "int32"), "A16": _sb(576, "float16"), "AW": _sb(V, "float32"),
    "TQ": _sb(104, "int32"), "YL": _sb(128, "uint16"),
    "OL": _sb(64, "uint16"), "ML": _sb(32, "uint16"), "ZL": _sb(2048, "uint16"), "YO": _sb(32, "float16"),
    "CV": _sb(512, "float16"), "CY": _sb(512, "float16"), "T1": _sb(512, "float16"), "IG": _sb(512, "float16"),
    "KI": _sb(1, "int32"), "KB": _sb(2, "int32"), "KF": _sb(5, "float32"), "JV": _sb(256, "float32"),
    "ZR": _sb(512), "J16": _sb(128), "JG": _sb(32), "JX": _sb(168),
    "SA": _sb(512), "SY": _sb(288), "SY4": _sb(144), "RK": _sb(512), "SQ": _sb(1152), "BC": _sb(2048),
    "I1": _sb(128), "IN": _sb(128), "I2": _sb(128), "GG": _sb(32), "NG": _sb(32), "G2": _sb(32), "GK": _sb(512), "WD": _sb(168),
    "OG": _sb(128), "TR": _sb(128), "PM": _sb(128), "PN": _sb(128), "P2": _sb(128), "P64": _sb(128), "MY": _sb(128),
    "RV0": _sb(128), "RY0": _sb(128), "RV1": _sb(128), "RY1": _sb(128),
    "XV": _sb(1024), "XY": _sb(2048), "NP": _sb(1024), "LO": _sb(4096), "DL": _sb(4096),
    "EQ": _sb(1024), "EV": _sb(512), "EN": _sb(512),
    "U": _sb(1024 * 30), "C": _sb(1024 * 30), "SG": _sb(1024 * NS),
    "RM": _sb(V), "IM": _sb(V, "float32"), "IV": _sb(256, "float32"), "HW": _sb(1040),
    "AB": _sb(256), "OK": _sb(256), "HT0": _sb(256), "HT1": _sb(256), "PR": _sb(256, "float16"), "ES": _sb(512),
    "RG0": _sb(512), "RG1": _sb(512), "SP0": _sb(16, "float32"), "SP1": _sb(16, "float32"), "FL": _sb(512),
    "PB0": ("psum", [128, 1024], "float32"), "PB1": ("psum", [128, 1024], "float32"),
    "AT": ("psum", [128, 512], "float32"), "WB": ("psum", [128, 512], "float32"),
    "M0": ("psum", [128, 512], "float32"), "M1": ("psum", [128, 512], "float32"),
}
NDMA = 60
SEMAPHORES = (["ev", "es", "ep", "eg", "sent", "sa0", "sa1"] + ["xa%d" % j for j in range(4)] + ["fa%d" % j for j in range(4)]
              + ["d%d" % j for j in range(NDMA)])
BANKS = ("PB0a", "PB0b", "PB1a", "PB1b", "AT", "WB", "M0", "M1")


def masks(topo, cores, r):
    src = cores[r]
    far = [d for d in range(len(cores)) if cores[d] not in topo.cores_of(src)]
    near = [d for d in range(len(cores)) if d != r and d not in far]
    off = topo.engines(src, cores[far[0]])
    out = {}
    n = len(off) // len(far)
    for j, d in enumerate(far):
        out[d] = off[j * n:(j + 1) * n]
    for d in near:
        out[d] = [e for e in topo.engines(src, cores[d]) if e not in off]
    return out, far, near


def conflicts(ops):
    wrote, read, out = {}, {}, []
    for n, o in enumerate(ops):
        raw = set(wrote[key] for key in o["rd"] if key in wrote)
        rest = set(m for key in o["rd"] if key in BANKS for m in read.get(key, []) if ops[m]["q"] != o["q"])
        for key in o["wr"]:
            rest.update(read.get(key, []) + ([wrote[key]] if key in wrote else []))
        out.append((raw, rest - raw))
        for key in o["wr"]:
            wrote[key] = n
            read[key] = []
        for key in o["rd"]:
            if key not in o["wr"]:
                read.setdefault(key, []).append(n)
    return out


def place(ops, before, rank, fixed=0, back=False):
    after = [[] for _ in ops]
    for n, ms in enumerate(before):
        for m in ms:
            after[m].append(n)
    left, at, start = [len(ms) for ms in before], [o.get("ahead", 0.0) * back for o in ops], [0.0] * len(ops)
    ready, free = {}, {}
    for n, o in enumerate(ops):
        if not left[n]:
            ready.setdefault(o["q"], []).append(n)
    for _ in ops:
        best = None
        for q, ns in ready.items():
            if ns:
                t0 = max(free.get(q, 0.0), min(at[n] for n in ns))
                n = max((n for n in ns if at[n] <= t0), key=lambda n: (rank[n], -n))
                soon = [m for m in ns if rank[m] > rank[n] and at[m] < t0 + GUARD * ops[n]["us"]]
                if soon:
                    n = min(soon, key=lambda m: at[m])
                if best is None or max(t0, at[n]) < best[0]:
                    best = (max(t0, at[n]), n)
        t, n = best
        o = ops[n]
        ready[o["q"]].remove(n)
        start[n] = t
        if o["q"]:
            free[o["q"]] = t + o.get("hold", o["us"]) * (ROOM.get(o["q"], 1.0) if back else 1.0)
        for m in after[n]:
            same = ops[m]["q"] == o["q"]
            at[m] = max(at[m], t + (1e-6 if same and m < fixed else o["us"] + (0.0 if same and o["q"] == "p" else 0.06)) + o.get("lead", 0.0) * back)
            left[m] -= 1
            if not left[m]:
                ready.setdefault(ops[m]["q"], []).append(m)
    return start, after


def replay(ops, before, start, slow):
    end, free = [0.0] * len(ops), {}
    for n in sorted(range(len(ops)), key=lambda n: (start[n], n)):
        o = ops[n]
        t = max([free.get(o["q"], 0.0)] + [end[m] + (0.0 if ops[m]["q"] == o["q"] == "p" else 0.06) for m in before[n] if ops[m]["kind"] != "d" or o["kind"] != "d" or o["q"] == "g" or o["rd"]])
        more = o["hold"] * (slow - 1) if o["q"] == "g" and o["kind"] == "d" else 0.0
        end[n] = t + o["us"] + more
        if o["q"]:
            free[o["q"]] = t + o.get("hold", o["us"]) + more
    return max(end)


def arrange(ops, fixed):
    before = [a | b for a, b in conflicts(ops)]
    for n in range(1, fixed):
        before[n].update(m for m in range(n) if ops[m]["q"] == ops[n]["q"])
    start, after = place(ops, before, [-n for n in range(len(ops))], fixed)
    best = None
    for k in range(ROUNDS):
        shake = [SHAKE * math.sin(12.9898 * n + 78.233 * k) for n in range(len(ops))]
        back = place(ops, after, [t + o["us"] + d for t, o, d in zip(start, ops, shake)], 0, True)[0]
        start = place(ops, before, [t + o["us"] + o.get("lead", 0.0) for t, o in zip(back, ops)], fixed)[0]
        length = sum(replay(ops, before, start, slow) for slow in SLOWS)
        if best is None or length < best[0]:
            best = (length, start)
        if k % 3 == 2:
            start = best[1]
    for t, o in zip(best[1], ops):
        o["t"] = t
    return [ops[n] for n in sorted(range(len(ops)), key=lambda n: (best[1][n], n))]


def rank_program(g, core, T, topo):
    r = T.rank_of(core)
    if r is None:
        return
    cores = T.cores
    others = [d for d in range(4) if d != r]
    eng, far, near = masks(topo, cores, r)
    inc = {s: len(masks(topo, cores, s)[0][r]) for s in others}
    ops, sent = [], [0]
    mu, ad, eq, ne, ge = A.mult, A.add, A.is_equal, A.not_equal, A.is_ge

    def op(q, fn, rd, wr, us, kind="c"):
        if q == "g" and kind == "c" and sent[0]:
            rd = list(rd) + ["xn"]
        ops.append({"q": q, "fn": fn, "rd": list(rd), "wr": list(wr), "kind": kind, "us": us})

    def vec(fn, ap, cyc, rd, wr):
        op("v", fn, rd, wr, 0.05 + CYC * max(64, cyc * ap.shape[-1]))

    def ts(out, in0, s1, s2, o0, o1, rd, wr, cyc=1.0):
        if o1 is None:
            vec(lambda: g.vector.tensor_scalar(out, in0, s1, None, o0), out, cyc, rd, wr)
        else:
            vec(lambda: g.vector.tensor_scalar(out, in0, s1, s2, o0, o1), out, cyc, rd, wr)

    def tt(out, a, b, o, rd, wr, cyc=1.0):
        vec(lambda: g.vector.tensor_tensor(out, a, b, o), out, cyc, rd, wr)

    def cp(out, a, rd, wr, cyc=1.0):
        vec(lambda: g.vector.tensor_copy(out, a), out, cyc, rd, wr)

    def scatter(win, lst, a, rd, wr):
        vec(lambda: g.vector.tensor_copy(win.indirect(lst), a), a, SCATTER, rd, wr)

    def zero(ap, key):
        vec(lambda: g.vector.memset(ap, 0.0), ap, 0.5, [], [key])

    def act(out, a, f, rd, wr, bias=0.0, scale=1.0, cyc=1.0):
        op("s", lambda: g.scalar.activation(out, a, f, bias=bias, scale=scale), rd, wr, 0.065 + CYC * cyc * out.shape[-1])

    def mm(out, l, rh, st, sp, rd, bank):
        op("p", lambda: g.tensor.matmul(out, l, rh, st, sp), rd, [bank], CYC / 2 * max(64, out.shape[-1]))

    def dma(q, pairs, rd, wr, us=LOAD):
        e = g.sync if q == "y" else g.scalar
        op(q, lambda: [e.dma_start(o, a) for o, a in pairs], rd, wr, us, "d")
        ops[-1]["hold"] = 0.1 * len(pairs)

    def add(out, a, rd, key):
        op("g", lambda: [g.dma_start(out, a, accum_op=ad)], rd, key, ADDMA + HOLD * out.shape[-1] / 1024, "d")
        ops[-1]["hold"] = HOLD * out.shape[-1] / 1024
        ops[-1]["lead"] = AHEAD

    def iota(out, pat, base, cm, wr):
        op("g", lambda: g.iota(out, pat, base, cm, allow_small_or_imprecise_dtypes=True), [], wr, 0.13 + 2 * CYC * out.shape[-1])

    def select(out, a, pat, cmp, fill, base, cm, rd, key):
        op("g", lambda: g.affine_select(out, a, pat, cmp, fill, base, cm), rd, [key], 0.17 + 2 * CYC * out.shape[-1])

    def mark(out, n, pat, base, val, key):
        select(out, T.ZR[:, 0:n], pat, ne, val, base, 1, ["ZR"], key)

    def band(out, n, pat, base, width, val, key):
        neg = [[-s, c] for s, c in pat]
        select(out, T.ZR[:, 0:n], neg, ge, val, -base - 1, -1, ["ZR"], key)
        select(out, out, neg, ge, 0.0, width - 1 - base, -1, [key], key)

    def send(to, srcs, dst, sem, rd, tag):
        def fn():
            trs = []
            for d in to:
                rid, pid = topo.addr(cores[d], core)
                trs.append(RemoteDMATransfer(dst_ids=[DstId(rid=rid, pnc=pid)], dma_engine_mask=sum(1 << e for e in eng[d]),
                                             remote_sem=sem, src=srcs[d], dst=dst))
            return g.remote_dma_fused(trs, local_sem=T.sem.sent)
        op("g", fn, rd, [tag], 0.5 if sent[0] else 2.0, "r")
        sent[0] += sum(len(eng[d]) for d in to)

    def arrive(key, sem, n, tag, us):
        ops.append({"q": None, "kind": "x", "rd": [tag], "wr": [key], "sem": sem, "n": n, "us": us})

    def bank(j):
        name = BANKS[j]
        return (T[name[:3]], 512 * (j % 2)) if j < 4 else (T[name], 0)

    def reg(bk, n, c=0):
        b, o = bank(BANKS.index(bk))
        return b[:, o + c:o + c + n]

    lo = 32 * r
    dma("s", [(T.A32[:], T.adj[lo:lo + 32, :])], [], ["A32"], 2.3)
    dma("y", [(T.TQ[32 * k:32 * k + 32, :], T.tv[lo:lo + 32, 8 * k:8 * k + 104]) for k in range(4)], [], ["TQ"], 3.0)
    dma("s", [(T.XS[d], T.x[32 * d:32 * d + 32, :]) for d in far], [], ["XSf"], 3.2)
    dma("y", [(T.XS[d], T.x[32 * d:32 * d + 32, :]) for d in near], [], ["XSn"], 3.5)
    dma("y", [(T.X[lo:lo + 32, :], T.x[lo:lo + 32, :])], [], ["X%d" % r], 4.0)
    zero(T.ZR[:], "ZR")
    op("g", lambda: g.iota(T.KI[:], [[0, 1]], 0, 1), [], ["KI"], 0.13)
    iota(T.J16[:], [[-16, 8], [0, 16]], 0, 1, ["J16"])
    mark(T.SA[:], 512, [[-1, 4], [0, 4], [-4, 32]], 0, 1.0, "SA")
    mark(T.SY[:], 288, [[-1, 2], [-16, 9], [128, 16]], -128 * 15, 1.0, "SY")
    mark(T.I1[:], 128, [[-1, 128]], 0, 1.0, "I1")
    mark(T.SQ[:, 128:384], 256, [[128, 2], [-1, 16], [-16, 8]], 0, 1.0, "SQ0")
    fixed = len(ops)
    send(far, T.XS, T.XL[r], T.sem["xa%d" % r], ["XSf"], "xf")
    send(near, T.XS, T.XL[r], T.sem["xa%d" % r], ["XSn", "xf"], "xn")
    iota(T.JV[:], [[1, 256]], 16, 0, ["JV"])
    ops[-1]["rd"].append("xn")
    mark(T.RK[:], 512, [[-32, 4], [0, 4], [-1, 32]], 0, 1.0, "RK")
    ops[-1]["rd"].append("xn")
    mark(T.PM[:], 128, [[-16, 2], [-1, 16], [-32, 4]], 0, 1.0, "PM")
    ops[-1]["rd"].append("xn")
    iota(T.JG[:], [[1, 2], [0, 16]], 0, 0, ["JG"])
    iota(T.JX[:], [[1, 168]], -39, 0, ["JX"])
    for s in near + far:
        arrive("XL%d" % s, T.sem["xa%d" % s], inc[s], "xn" if s in near else "xf", XNEAR if s in near else XFAR)
        dma("y", [(T.X[32 * s:32 * s + 32, :], T.XL[s])], ["XL%d" % s], ["X%d" % s])
    XK = ["X%d" % s for s in range(4)]

    zero(T.SQ[:, 0:128], "SQp")
    zero(T.HW[:, 0:16], "HWp")
    ts(T.KB[:, 0:1], T.KI[:], 4, 1, A.arith_shift_right, A.bitwise_and, ["KI"], ["KB0"])
    ts(T.KB[:, 1:2], T.KI[:], 5, None, A.arith_shift_right, None, ["KI"], ["KB1"])
    cp(T.KF[:, 0:2], T.KB[:], ["KB0", "KB1"], ["KF"])
    ts(T.KF[:, 2:3], T.KF[:, 1:2], 8.0, None, mu, None, ["KF"], ["KF2"])
    ts(T.KF[:, 3:4], T.KF[:, 0:1], 64.0, T.KF[:, 2:3], mu, ad, ["KF", "KF2"], ["KF3"])
    ts(T.KF[:, 4:5], T.KF[:, 1:2], 256.0, None, mu, None, ["KF"], ["KF4"])
    act(T.IV[:], T.JV[:], F.Identity, ["JV", "KF4"], ["IV"], bias=T.KF[:, 4:5])
    for j in range(16):
        ts(T.BC[:, 128 * j:128 * j + 128], T.J16[:], float(j), None, eq, None, ["J16"], ["BC%d" % j], 0.5)
    ts(T.GG[:], T.JG[:], T.KF[:, 0:1], None, eq, None, ["JG", "KF"], ["GG"])
    ts(T.NG[:], T.JG[:], T.KF[:, 0:1], -1.0, eq, mu, ["JG", "KF"], ["NG"])
    ts(T.G2[:], T.JG[:], T.KF[:, 0:1], 2.0, eq, mu, ["JG", "KF"], ["G2"])
    ts(T.WD[:], T.JX[:], T.KF[:, 3:4], None, eq, None, ["JX", "KF3"], ["WD"], 0.5)

    ts(T.A16[:], T.A32[:], -H, None, ad, None, ["A32"], ["A16"])
    for j in range(8):
        mm(reg(BANKS[j], 288), T.SA[:, 128 * (j // 2):128 * (j // 2) + 128], T.A16[:, 288 * (j % 2):288 * (j % 2) + 288], True, True,
           ["SA", "A16"], BANKS[j])
    for t in range(2):
        for h in range(2):
            cp(T.OL[:, 32 * t + 8 * h:32 * t + 8 * h + 8], T.TQ[:, 64 * t + 32 * h:64 * t + 32 * h + 8], ["TQ"], ["OV%d%d" % (t, h)])
    for j in range(8):
        if j % 2 == 0 or j == 1:
            act(T.AW[:, 288 * j:288 * j + 288], reg(BANKS[j], 288), F.Copy, [BANKS[j]], ["AW%d" % j])
        else:
            cp(T.AW[:, 288 * j:288 * j + 288], reg(BANKS[j], 288), [BANKS[j]], ["AW%d" % j])
    AWK = ["AW%d" % j for j in range(8)]
    for name, src, sc in (("IN", "I1", -1.0), ("I2", "I1", 2.0), ("PN", "PM", -1.0), ("P2", "PM", 2.0), ("P64", "PM", 64.0)):
        act(T[name][:], T[src][:], F.Copy, [src], [name], scale=sc)
    act(T.SQ[:, 384:640], T.SQ[:, 128:384], F.Copy, ["SQ0"], ["SQ1"])
    act(T.SQ[:, 640:1152], T.SQ[:, 128:640], F.Copy, ["SQ0", "SQ1"], ["SQ2"])
    for j in range(5):
        n = min(512, V - 512 * j)
        act(T.IM[:, 512 * j:512 * j + n], T.ZR[:, 0:n], F.Copy, ["ZR"], ["IM%d" % j])
    for t in range(2):
        cp(T.CV[:, 256 * t:256 * t + 256], T.AW[:].indirect(T.OL[:, 32 * t:32 * t + 16]), AWK + ["OV%d0" % t, "OV%d1" % t], ["CV%d" % t], GATHER)
        bk = "M%d" % t
        for p in range(16):
            mm(T[bk][:, 0:16], T.SY[:, 144 * t + 15 - p:144 * t + 143 - p], T.CV[:, 256 * t + p:256 * t + 256:16], p == 0, p == 15,
               ["SY", "CV%d" % t], bk)
    for t in range(2):
        ts(T.OL[:, 32 * t + 16:32 * t + 32], T["M%d" % t][:, 0:16], H, None, ad, None, ["M%d" % t], ["OY%d" % t])
        cp(T.CY[:, 256 * t:256 * t + 256], T.AW[:].indirect(T.OL[:, 32 * t + 16:32 * t + 32]), AWK + ["OY%d" % t], ["CY%d" % t], GATHER)
        cp(T.YO[:, 16 * t:16 * t + 16], T["M%d" % t][:, 0:16], ["M%d" % t], ["YO%d" % t])
    CK = ["CY0", "CY1"]
    for c in range(4):
        for k in range(4):
            mm(T.WB[:, 32 * c + 8 * k:32 * c + 8 * k + 8], T.RK[:, 128 * k:128 * k + 128], T.YO[:, 8 * c:8 * c + 8], True, True,
               ["RK", "YO%d" % (c // 2)], "WB")
    ts(T.YL[:], T.WB[:, 0:128], H, None, ad, None, ["WB"], ["YL"])
    for t in range(2):
        for h in range(2):
            for k in range(4):
                mm(T.AT[:, 256 * t + 4 * h + k:256 * t + 256:8], T.CY[:, 256 * t + 128 * h:256 * t + 128 * h + 128], T.I1[:, 32 * k:32 * k + 32],
                   True, True, ["CY%d" % t, "I1"], "AT")
        cp(T.T1[:, 256 * t:256 * t + 256], T.AT[:, 256 * t:256 * t + 256], ["AT"], ["T1%d" % t])
    mm(T.AT[:], T.ZR[:, 0:128], T.ZR[:], True, True, ["ZR"], "AT")
    ops[-1]["wr"].append("A0")
    SQK = ["SQp"] + ["SQ%d" % k for k in range(3)]
    for j in range(4):
        b, o = bank(j)
        for q in range(8):
            for gr in range(2):
                c, c1 = 128 * (1 - gr) + q, 256 * (j // 2) + 128 * gr + 64 * (j % 2)
                mm(b[:, o + q:o + 512:8], T.SQ[:, c:c + 1017:8], T.T1[:, c1:c1 + 64], gr == 0, gr == 1, SQK + ["T1%d" % (j // 2)], BANKS[j])
    for j in range(2):
        ts(T.ZL[:, 1024 * j:1024 * j + 1024], T["PB%d" % j][:], H, float(V - 1), ad, A.min, ["PB%da" % j, "PB%db" % j], ["ZL%d" % j])

    ts(T.EN[:], T.CY[:], H, 64.0, eq, mu, CK, ["EN"], 0.5)
    mm(T.WB[:], T.PN[:], T.EN[:], True, False, ["PN", "EN"], "WB")

    def match(n):
        bk = "M%d" % (n % 2)
        if n >= 2:
            mm(T[bk][:], T.BC[:, 128 * n:128 * n + 128], T.CV[:], True, True, ["BC%d" % n, "CV0", "CV1"], bk)
        else:
            for t in range(2):
                j, src = (t, T.CY) if n == 0 else (1 - t, T.CV)
                mm(T[bk][:, 256 * t:256 * t + 256], T.BC[:, 128 * j:128 * j + 128], src[:, 256 * t:256 * t + 256], True, True,
                   ["BC0", "BC1", "CV0", "CV1"] + CK, bk)
        out, key = (T.EV[:], "EV") if n == 0 else (T.EQ[:, 512 * (n % 2):512 * (n % 2) + 512], "EQ%d" % (n % 2))
        tt(out, T[bk][:], T.CY[:], eq, [bk] + CK, [key])
        if n > 0:
            wn = "PM" if n == 1 else "P2"
            mm(T.WB[:], T[wn][:], out, False, False, [wn, key], "WB")

    for n in range(PRE):
        match(n)

    def ends(t):
        xv, xy = T.X[:].indirect(T.ZL[:, 1088 * t:1088 * t + 64]), T.X[:].indirect(T.YL[:, 64 * t:64 * t + 64])
        low, dist, y = T.LO[:, 2048 * t:2048 * t + 1024], T.DL[:, 2048 * t:2048 * t + 1024], T.XY[:, 1024 * t:1024 * t + 1024]
        if t == 0:
            act(T.XV[:], xv, F.Copy, XK + ["ZL0"], ["XV"], cyc=GATHER)
            tt(low, xy, T.XV[:], A.min, XK + ["YL", "XV"], ["LO0"], GATHER)
            ops[-1]["lead"] = FIRST
            act(y, xy, F.Copy, XK + ["YL"], ["XY0"], cyc=GATHER)
            for h, bk in enumerate(BANKS[0:2]):
                for m, (wn, src, key) in enumerate([("IN", T.XV, "XV"), ("IN", T.XY, "XY0"), ("I2", T.LO, "LO0")]):
                    mm(reg(bk, 512), T[wn][:], src[:, 512 * h:512 * h + 512], m == 0, m == 2, [wn, key], bk)
            ts(dist, T.PB0[:], -0.5, None, A.min, None, BANKS[0:2], ["DL0"])
        else:
            act(low, xv, F.Copy, XK + ["ZL1"], ["LO1"], cyc=GATHER)
            if LEAN:
                tt(y, xy, low, A.subtract, XK + ["YL", "LO1"], ["XY1"], GATHER)
                ts(T.NP[:], y, 0.0, None, A.min, None, ["XY1"], ["NP"], 0.5)
                add(low, T.NP[:], ["LO1", "NP"], ["LO1"])
                act(dist, y, F.Abs, ["XY1"], ["DL1"])
                ts(dist, dist, -1.0, -0.5, mu, A.min, ["DL1"], ["DL1"], 0.5)
            else:
                act(y, xy, F.Copy, XK + ["YL"], ["XY1"], scale=-1.0, cyc=GATHER)
                add(y, low, ["XY1", "LO1"], ["XY1"])
                ts(T.NP[:], y, 0.0, -1.0, A.max, mu, ["XY1"], ["NP"], 0.5)
                add(low, T.NP[:], ["LO1", "NP"], ["LO1"])
                add(y, T.NP[:], ["XY1", "NP"], ["XY1"])
                add(y, T.NP[:], ["XY1", "NP"], ["XY1"])
                ts(dist, y, -0.5, None, A.min, None, ["XY1"], ["DL1"], 0.5)
        for name, src in (("LO", low), ("DL", dist)):
            dma("y", [(T[name][:, 2048 * t + 1024:2048 * t + 2048], src)], ["%s%d" % (name, t)], ["%s%d+" % (name, t)])

    def merge(name):
        dma("y", [(T[name][16 * gr + k:128:32, :], T[name][32 * k + 16 * gr + 8:32 * k + 16 * gr + 12, :]) for k in range(4) for gr in range(2)],
            [name], [name], 5.0)

    def index():
        for c in range(2):
            op("s", lambda c=c: g.scalar.activation(T.IM[:].indirect(T.OL[:, 32 + 16 * c:48 + 16 * c]), T.IV[:], F.Silu),
               ["IV", "IM", "OV10", "OV11", "OY1"][:4 + c] + ["IM%d" % j for j in range(5)], ["IM"],
               0.065 + 256 * CYC * SCATTER + 1.3 * (1 - c))
            ops[-1]["ahead"] = SOON
        merge("IM")
        cp(T.IG[:], T.IM[:].indirect(T.OL[:, 0:32]), ["IM", "OY0"], ["IG"], GATHER)
        for p in range(16):
            mm(T.M0[:, 0:32], T.SY4[:, 15 - p:143 - p], T.IG[:, p:512:16], p == 0, p == 15, ["SY4", "IG"], "M0")
        cp(T.ML[:], T.M0[:, 0:32], ["M0"], ["ML"])

    grp, turn, row = [[-16, 8], [0, 16]], [[-16, 2], [0, 16], [-32, 4]], [[-16, 2], [128, 16], [-32, 4]]
    band(T.OG[:], 128, grp, 0, 16, 1.0, "OG")
    band(T.TR[:], 128, grp, 0, 16, 4096.0, "TR")
    select(T.TR[:], T.TR[:], [[1, 128]], ge, 0.0, 0, -1, ["TR"], "TR")
    select(T.TR[:], T.TR[:], [[1, 128]], ne, -4096.0, 0, -1, ["TR"], "TR")
    band(T.SY4[:], 144, [[-16, 9], [128, 16]], -128 * 15, 4, 1.0, "SY4")
    for j in range(4):
        iota(T.RM[:, 576 * j:576 * j + 576], [[0, 576]], 0, 0, ["RM%d" % j])
    band(T.MY[:], 128, [[-16, 8], [128, 16]], 0, 4, 1.0, "MY")
    band(T.RV0[:], 128, turn, 0, 4, -1.0, "RV0")
    band(T.RY0[:], 128, row, 0, 4, -64.0, "RY0")
    mark(T.RV1[:], 128, turn, 0, -1.0, "RV1")
    mark(T.RY1[:], 128, row, -128, -64.0, "RY1")
    for k in range(4):
        band(T.GK[:, 128 * k:128 * k + 128], 128, [[0, 4], [-16, 2], [0, 16]], -32 * k, 16, 1.0, "GK%d" % k)

    def masked(t, bm):
        c = 256 * t
        mm(reg(bm, 256), T.I1[:], T.EV[:, c:c + 256], True, False, ["I1", "EV"], bm)
        mm(reg(bm, 256), T.I1[:], T.EN[:, c:c + 256], False, False, ["I1", "EN"], bm)
        if t == 1:
            mm(reg(bm, 256), T.MY[:], T.RG0[:, 256:512], False, False, ["MY", "RG0"], bm)

    def sums_in(t, bm):
        act(T.AB[:], T.AT[:, 256 * t:256 * t + 256], F.Abs, ["AT"] + ["A%d%d" % (n, h) for n in range(15 * t, 15 * t + 15) for h in range(2)],
            ["AB"], bias=0.5, scale=1.0 / 128)
        for h in range(2):
            mm(reg(bm, 128, 128 * h), T.AB[:, 128 * h:128 * h + 128], T.I1[:], False, h == 1, ["AB", "I1"], bm)
        ts(T.OK[:], reg(bm, 256), 6.5 / 128, None, A.is_le, None, [bm], ["OK"])

    def column(t, bk, wn):
        mm(reg(bk, 256), T[wn][:], T.CY[:, 256 * t:256 * t + 256], True, False, [wn] + CK, bk)

    def first(t, bp):
        mm(reg(bp, 256), T.TR[:], T.OK[:], False, True, ["TR", "OK"], bp)
        ts(T.PR[:], reg(bp, 256), 4096.0, H, ad, A.min, [bp], ["PR"])

    def hit(t, bh):
        mm(reg(bh, 256), T.OG[:], T.OK[:], True, True, ["OG", "OK"], bh)
        act(T["HT%d" % t][:], reg(bh, 256), F.Sign, [bh], ["HT%d" % t])

    def same(t, bb):
        mm(reg(bb, 256), T.OG[:], T.PR[:], False, True, ["OG", "PR"], bb)
        ts(T.ES[:, 256 * t:256 * t + 256], reg(bb, 256), 15 * H, -1.0, eq, mu, [bb], ["ES%d" % t])

    def seps(t, bs):
        for j in range(16):
            x0 = 39 - 32 * (j // 8) - j % 8
            mm(reg(bs, 16), T.WD[:, x0:x0 + 128], T.PR[:, 16 * j:16 * j + 16], j == 0, j == 15, ["WD", "PR"], bs)
        sp, sd = T["SP%d" % t], T["SD%d" % t]
        act(sp[:], reg(bs, 16), F.Identity, [bs], ["SP%d" % t], bias=-14 * H)
        send(others, {d: sp[:] for d in others}, sd[r], T.sem["sa%d" % t], ["SP%d" % t], "ss%d" % t)
        dma("y", [(sd[r], sp[:])], ["SP%d" % t], ["SO%d" % t])
        arrive("SR%d" % t, T.sem["sa%d" % t], sum(inc.values()), "ss%d" % t, 2.5 + 5 * (1 - t))
        dma("y", [(T.ysep[:, 1024 * t:1024 * t + 1024], sd[:])], ["SO%d" % t, "SR%d" % t], ["ys%d" % t])
        ops[-1]["ahead"] = EARLY if t == 0 else 1.0

    def score(terms, sp):
        for m, (t, wn, src, c, key) in enumerate(terms):
            mm(reg("WB", 256, 256 * t), T[wn][:], T[src][:, c:c + 256], False, sp and m == len(terms) - 1, [wn, key], "WB")

    chunks = [(t, i) for t in range(2) for i in range(16) if i != t]
    pos, neg, two = T.GG[:, 0:17:16], T.NG[:, 0:17:16], T.G2[:, 0:17:16]
    jobs = [0]

    def sums(n, h, sg, s0, key, wc, ws):
        t, i = chunks[n]

        def fn():
            for b in range(4 * h, 4 * h + 4):
                a = T.AT[:, 256 * t + 32 * b + i:256 * t + 32 * b + i + 17:16]
                g.tensor.matmul(a, T.C[:, 1024 * n + 128 * b:1024 * n + 128 * b + 128], wc, True, False)
                last = g.tensor.matmul(a, sg[:, s0 + 128 * b:s0 + 128 * b + 128], ws, False, True)
            return last
        op("p", fn, ["C%d" % n, key, "GG", "NG", "G2", "A0"], ["A%d%d" % (n, h)], 4 * 64 * CYC)
        ops[-1]["bank"] = "AT"

    def unit(n0, kind):
        (t, i), w, kind = chunks[n0], len(kind), kind[0]
        keys, more = ["U%d" % n for n in range(n0, n0 + w)], "+" * (w - 1)
        u, z = T.U[:, 1024 * n0:1024 * (n0 + w)], T.X[:].indirect(T.ZL[:, 1024 * t + 64 * i:1024 * t + 64 * (i + w)])
        low, lk = T.LO[:, 2048 * t:2048 * t + 1024 * w], ["LO%d" % t, "LO%d" % t + more]
        if kind == "s":
            act(u, z, F.Copy, XK + ["ZL%d" % t], keys, scale=-1.0, cyc=GATHER)
            add(u, low, keys + lk, keys)
        else:
            tt(u, z, low, A.subtract, XK + ["ZL%d" % t] + lk, keys, GATHER)
        if kind == "w":
            act(T.C[:, 1024 * n0:1024 * (n0 + w)], u, F.Sign, keys, ["C%d" % n for n in range(n0, n0 + w)])
        else:
            ts(T.C[:, 1024 * n0:1024 * (n0 + w)], u, -1.0, 1.0, A.max, A.min, keys, ["C%d" % n for n in range(n0, n0 + w)], 0.5)
        if kind == "d":
            add(u, T.DL[:, 2048 * t:2048 * t + 1024 * w], keys + ["DL%d" % t, "DL%d" % t + more], keys)
            ts(u, u, -0.5, 0.5, A.max, A.min, keys, keys, 0.5)
        for n in range(n0, n0 + w):
            if kind == "d":
                for h in range(2):
                    sums(n, h, T.U, 1024 * n, "U%d" % n, neg, two)
                continue
            pb, s0, sk = "PB%d" % (jobs[0] % 2), 1024 * (jobs[0] % NS), "SG%d" % (jobs[0] % NS)
            jobs[0] += 1
            wn, wc, ws = ("IN", pos, neg) if kind == "s" else ("I1", neg, pos)
            for h, bk in enumerate((pb + "a", pb + "b")):
                mm(reg(bk, 512), T.I1[:], T.U[:, 1024 * n + 512 * h:1024 * n + 512 * h + 512], True, False, ["I1", "U%d" % n], bk)
                mm(reg(bk, 512), T[wn][:], T.DL[:, 2048 * t + 512 * h:2048 * t + 512 * h + 512], False, True, [wn, "DL%d" % t], bk)
            if kind == "h":
                act(T.SG[:, s0:s0 + 512], T[pb][:, 0:512], F.Sign, [pb + "a"], [sk + "a"])
                ts(T.SG[:, s0 + 512:s0 + 1024], T[pb][:, 512:1024], -0.5, 0.5, A.max, A.min, [pb + "b"], [sk + "b"])
            else:
                act(T.SG[:, s0:s0 + 1024], T[pb][:], F.Sign, [pb + "a", pb + "b"], [sk + "a", sk + "b"])
            for h in range(2):
                sums(n, h, T.SG, s0, sk + "ab"[h], wc, two if kind == "h" and h else ws)

    starts = [sum(len(k) for k in PLAN[:j]) for j in range(len(PLAN))]
    ends(0)
    ends(1)
    index()
    for n0, kind in zip(starts, PLAN):
        if n0 < 15:
            unit(n0, kind)
    masked(0, "M0")
    column(0, "M1", "I1")
    sums_in(0, "M0")
    first(0, "M1")
    hit(0, "M0")
    column(0, "M0", "IN")
    same(0, "M0")
    seps(0, "M1")
    for c in range(2):
        scatter(T.RM[:], T.OL[:, 16 * c:16 * c + 16], T.HT0[:], ["HT0", "RM", "OY0"] + ["RM%d" % j for j in range(4)], ["RM"])
    merge("RM")
    act(T.RG0[:], T.RM[:].indirect(T.OL[:, 32:64]), F.Copy, ["RM", "OY1"], ["RG0"], cyc=GATHER)
    for n in range(PRE, 16):
        match(n)
    masked(1, "M0")
    ops[-1]["ahead"] = LATE
    score([(0, "P64", "HT0", 0, "HT0"), (0, "P64", "ES", 0, "ES0"), (1, "RV0", "RG0", 0, "RG0"), (1, "RY0", "RG0", 256, "RG0")], False)
    ops[-1]["ahead"] = LATE
    column(1, "M1", "I1")
    for n0, kind in zip(starts, PLAN):
        if n0 >= 15:
            unit(n0, kind)

    column(1, "PB0b", "IN")
    sums_in(1, "M0")
    for k in range(4):
        mm(T.PB1[:, 256 * k:256 * k + 256], T.GK[:, 128 * k:128 * k + 128], T.OK[:], True, True, ["GK%d" % k, "OK"], BANKS[2 + k // 2])
    first(1, "M1")
    act(T.HW[:, 16:528], T.PB1[:, 0:512], F.Sign, ["PB1a"], ["HWa"])
    ts(T.HW[:, 528:1040], T.PB1[:, 512:1024], 1.0, None, A.min, None, ["PB1b"], ["HWb"])
    hit(1, "AT")
    same(1, "PB0b")
    HK = ["HWp", "HWa", "HWb", "ML"]
    act(T.RG1[:, 256:512], T.HW[:].indirect(T.ML[:, 16:32]), F.Copy, HK, ["RG1y"], cyc=GATHER)
    cp(T.RG1[:, 0:256], T.HW[:].indirect(T.ML[:, 0:16]), HK, ["RG1v"], GATHER)
    seps(1, "M0")
    score([(1, "P64", "HT1", 0, "HT1"), (1, "P64", "ES", 256, "ES1"), (0, "RY1", "RG1", 256, "RG1y"), (0, "RV1", "RG1", 0, "RG1v")], True)
    ts(T.FL[:], T.WB[:], 64.5, None, ge, None, ["WB"], ["FL"])
    send(others, {d: T.FL[:, 128 * d:128 * d + 128] for d in others}, T.FD[r], T.sem["fa%d" % r], ["FL"], "sf")
    dma("s", [(T.yflag[lo:lo + 32, :], T.FL[:, 128 * r:128 * r + 128])], ["FL"], ["yf%d" % r])
    for j, s in enumerate(near + far):
        arrive("FR%d" % s, T.sem["fa%d" % s], inc[s], "sf", 2.5 + 0.2 * j)
        dma("sys"[j], [(T.yflag[32 * s:32 * s + 32, :], T.FD[s])], ["FR%d" % s], ["yf%d" % s])

    ops = arrange(ops, fixed)
    for o in ops:
        if "bank" in o:
            o["wr"].append(o["bank"])
    deps = []
    for o, (raw, rest) in zip(ops, conflicts(ops)):
        last = {}
        for m in raw | rest:
            if ops[m]["kind"] != "r" and o["kind"] != "x" and not ops[m]["q"] == o["q"] == "p":
                c = ops[m]["q"] if ops[m]["kind"] == "c" else ("own", m)
                last[c] = max(last.get(c, -1), m)
        deps.append(sorted(last.values()))
    marked = set(m for d in deps for m in d)
    queue = {"v": g.vector, "s": g.scalar, "p": g.tensor, "g": g, "y": g.sync}
    esem = {"v": "ev", "s": "es", "p": "ep", "g": "eg"}
    count, sig, seen, dsems = {}, {}, {}, []
    for n, o in enumerate(ops):
        if o["kind"] == "x":
            sig[n] = (o["sem"], o["n"], "x%d" % n)
            continue
        for m in deps[n]:
            sem, val, name = sig[m]
            if seen.get((o["q"], name), 0) < val:
                queue[o["q"]].wait_ge(sem, val)
                seen[(o["q"], name)] = val
        ins = o["fn"]()
        if o["kind"] == "d":
            name = "d%d" % len(dsems)
            for one in ins:
                one.then_inc(T.sem[name], 16)
            sig[n] = (T.sem[name], 16 * len(ins), name)
            dsems.append(sig[n])
        elif n in marked:
            name = esem[o["q"]]
            count[name] = count.get(name, 0) + 1
            ins.then_inc(T.sem[name], 1)
            sig[n] = (T.sem[name], count[name], name)
    g.wait_ge(T.sem.sent, sent[0])
    for sem, val, name in dsems:
        if not any(k[1] == name for k in seen):
            g.sync.wait_ge(sem, val)
